import numpy as np
import ml_dtypes


def mxq(x, axis, fmt="e4m3"):
    dtype, down = {"e4m3": (ml_dtypes.float8_e4m3fn, 7), "e5m2": (ml_dtypes.float8_e5m2, 14)}[fmt]
    v = np.moveaxis(np.asarray(x, np.float32).astype(ml_dtypes.bfloat16).astype(np.float64), axis, -1)
    blocks = v.reshape(v.shape[:-1] + (-1, 32))
    amax = np.abs(blocks).max(-1, keepdims=True)
    byte = np.maximum(np.where(amax > 0, np.frexp(amax)[1] - 1 + 127, 0) - down, 1)
    scale = np.exp2(byte - 127.0)
    codes = (blocks / scale).astype(np.float32).astype(dtype).astype(np.float64)
    return np.moveaxis((codes * scale).reshape(v.shape), -1, axis)


WIDE = False


def mx_kscale(k):
    if not WIDE:
        return np.ones(k)
    levels = np.array([24, -24, 12, -12, 0])
    if k % 512:
        return np.exp2(np.random.permutation(np.resize(levels, k // 32))).repeat(32)
    a = np.empty((k // 512, 16))
    for p in range(k // 512):
        a[p, :8] = np.random.permutation(np.resize(levels, 8))
        for g in range(8):
            far = levels[np.abs(levels - a[p, g]) >= 10]
            a[p, g + 8] = far[np.random.randint(len(far))]
    return np.exp2(a.ravel()).repeat(32)


def f64(x):
    return np.asarray(x).astype(np.float64)


def striped(idx):
    return np.tile(idx.reshape(-1, 16).T, (8, 1)).astype(np.uint16)


def unstriped(offs):
    return offs[:16].T.reshape(-1).astype(np.int64)


def striped8(idx):
    return np.concatenate([v.reshape(-1, 16).T for v in idx]).astype(np.uint16)


def unstriped8(offs):
    return np.stack([offs[16 * g:16 * g + 16].T.reshape(-1) for g in range(8)]).astype(np.int64)


E2M1 = np.array([0.0, 0.5, 1.0, 1.5, 2.0, 3.0, 4.0, 6.0, -0.0, -0.5, -1.0, -1.5, -2.0, -3.0, -4.0, -6.0])


def pack_weight(w, fmt):
    k, n = w.shape
    w = f64(np.asarray(w, np.float32).astype(ml_dtypes.bfloat16)).reshape(k // 32, 32, n)
    amax = np.abs(w).max(1)
    if fmt == "e4m3":
        byte = np.frexp(amax)[1] - 1 + 127 - 7
    else:
        mant, ex = np.frexp(amax / 6.0)
        byte = np.where(mant > 0.5, ex, ex - 1) + 127
    byte = np.clip(np.where(amax > 0, byte, 1), 1, 254)
    scaled = (w * np.exp2(127.0 - byte)[:, None, :]).reshape(k, n).astype(np.float32)
    by_word = np.ascontiguousarray(scaled.reshape(k // 512, 128, 4, n).transpose(0, 1, 3, 2))
    if fmt == "e4m3":
        words = by_word.astype(ml_dtypes.float8_e4m3fn).view(np.uint8)
    else:
        c = by_word.astype(ml_dtypes.float4_e2m1fn).view(np.uint8) & 0xF
        words = (c[..., 0::2] | (c[..., 1::2] << 4)).reshape(k // 512, 128, 2 * n)
    return np.ascontiguousarray(words), np.ascontiguousarray(byte.astype(np.uint8).reshape(k // 512, 16, n))


def unpack_weight(words, scales, fmt):
    g, _, n = scales.shape
    words = np.ascontiguousarray(words).reshape(g, 128, n, -1)
    if fmt == "e4m3":
        vals = words.view(ml_dtypes.float8_e4m3fn).astype(np.float64)
    else:
        nib = np.empty((g, 128, n, 4), np.uint8)
        nib[..., 0::2] = words & 0xF
        nib[..., 1::2] = words >> 4
        vals = E2M1[nib]
    vals = vals * np.repeat(np.exp2(scales.astype(np.float64) - 127.0), 8, axis=1)[..., None]
    return vals.transpose(0, 1, 3, 2).reshape(g * 512, n)


def pack_table4(v):
    words, scales = pack_weight(v, "e2m1")
    g, t = words.shape[0] // 2, v.shape[1]
    return np.ascontiguousarray(words.reshape(g, 2, 128, t, 2).transpose(0, 2, 3, 1, 4).reshape(g, 128, t, 4)), scales


def unpack_table4(words, scales):
    g, _, t, _ = words.shape
    return unpack_weight(words.reshape(g, 128, t, 2, 2).transpose(0, 3, 1, 2, 4).reshape(2 * g, 128, 2 * t), scales, "e2m1")


def planes(y):
    n, m = y.shape
    v = y.astype(np.float32).astype(ml_dtypes.bfloat16).astype(np.float64).reshape(n // 32, 32, m)
    top = np.abs(v).max(1)
    byte = np.clip(np.where(top > 0, np.frexp(top)[1] - 1 + 127 - 7, 1), 1, 254)
    codes = (v * np.exp2(127.0 - byte)[:, None, :]).reshape(n, m).astype(np.float32).astype(ml_dtypes.float8_e4m3fn).view(np.uint8)
    words = codes.reshape(n // 512, 128, 4, m).transpose(0, 1, 3, 2)
    return np.ascontiguousarray(words), np.ascontiguousarray(byte.astype(np.uint8).reshape(n // 512, 16, m))


K, L, R, N, T, J = 512, 1024, 512, 512, 2048, 1024


def setup_inputs():
    n = np.random.standard_normal
    s = mx_kscale(K)[:, None]
    s2 = mx_kscale(L)[:, None]
    u = mx_kscale(R)[:, None]
    p_tab = pack_table4(n((L, T)) * s2)
    p_wa = pack_weight(n((K, R)) / np.sqrt(K) / s * u.T, "e4m3")
    p_wd = pack_weight(n((R, N)) / np.sqrt(R) / u, "e4m3")
    return {
        "tab_words": p_tab[0],
        "tab_scales": p_tab[1],
        "xT": (n((K, T)) * s).astype(np.float32),
        "wgt2": np.repeat(np.random.uniform(0.5, 2.0, (8, J)), 16, axis=0).astype(np.float32),
        "wa_words": p_wa[0],
        "wa_scales": p_wa[1],
        "wb": (n((L, R)) / np.sqrt(L) / s2).astype(np.float32),
        "wd_words": p_wd[0],
        "wd_scales": p_wd[1],
        "offs": striped(np.random.permutation(T)[:J]),
        "offs2": striped8(np.stack([np.random.permutation(T)[:J] for _ in range(8)])),
    }


def reference(tab_words, tab_scales, xT, wgt2, wa_words, wa_scales, wb, wd_words, wd_scales, offs, offs2):
    idx = unstriped(offs)
    idx2 = unstriped8(offs2)
    tab_ = unpack_table4(tab_words, tab_scales)[:, idx]
    rows = np.arange(K)
    xg = f64(wgt2)[rows // 4 % 128] * f64(xT)[rows[:, None], idx2[rows % 512 // 64]]
    xT_ = mxq(xg, 0, "e4m3")
    wa_ = unpack_weight(wa_words, wa_scales, "e4m3")
    wb_ = mxq(f64(wb), 0, "e4m3")
    ya = wa_.T @ xT_
    yb = wb_.T @ tab_
    h = ya * yb
    h_ = mxq(h, 0, "e4m3")
    wd_ = unpack_weight(wd_words, wd_scales, "e4m3")
    y = wd_.T @ h_
    return (y,) + planes(y)

@@ -1,0 +1,182 @@
+from contextlib import ExitStack
+
+import concourse.mybir as mybir
+
+K, L, R, N, T, J = 512, 1024, 512, 512, 2048, 1024
+FLOPS = 2 * J * (K * R + L * R + R * N)
+
+F32 = mybir.dt.float32
+BF16 = mybir.dt.bfloat16
+I32 = mybir.dt.int32
+U32 = mybir.dt.uint32
+U16 = mybir.dt.uint16
+U8 = mybir.dt.uint8
+FP8X4 = mybir.dt.float8_e4m3fn_x4
+FP4X4 = mybir.dt.float4_e2m1fn_x4
+MULT = mybir.AluOpType.mult
+
+P = 128
+BLK = 128
+CHUNKS = (256, 256, 256, 256)
+
+
+def tile_list_htabg_mul_noneP_kernel(
+    tc, tab_words, tab_scales, xT, wgt2, wa_words, wa_scales, wb, wd_words, wd_scales, offs, offs2, out_0, out_1, out_2
+):
+    nc = tc.nc
+    starts = [sum(CHUNKS[:c]) for c in range(len(CHUNKS))]
+    with ExitStack() as ctx:
+        keep = ctx.enter_context(tc.tile_pool(name="keep", bufs=1))
+        psum = ctx.enter_context(tc.psum_pool(name="psum", bufs=1))
+
+        def sb(name, shape, dtype):
+            return keep.tile(shape, dtype, name=name, align_bytes=64)
+
+        idx = keep.tile([P, J // 16], U16, name="idx")
+        idx2 = keep.tile([P, J // 16], U16, name="idx2")
+        tabw = sb("tabw", [P, T], I32)
+        tabs = sb("tabs", [P, T], U8)
+        wsc_raw = sb("wsc_raw", [P, R], U8)
+        sc1 = sb("sc1", [P, J], U8)
+
+        nc.vector.memset(tabs[:].bitcast(I32), 0)
+        nc.vector.memset(wsc_raw[:].bitcast(I32), 0)
+        nc.vector.memset(sc1[:].bitcast(I32), 0)
+
+        nc.sync.dma_start(tabw[:], tab_words[0].rearrange("p n i -> p (n i)").bitcast(I32))
+        nc.sync.dma_start(idx2[:], offs2)
+        for q in range(4):
+            nc.sync.dma_start(tabs[32 * q : 32 * q + 8, :].bitcast(I32), tab_scales[:, 4 * q : 4 * q + 4, :].bitcast(I32))
+        nc.sync.dma_start(idx[:], offs)
+        wb_raw = [sb(f"wb_raw{a}", [P, 4, R], F32) for a in range(2)]
+        for a in range(2):
+            nc.sync.dma_start(wb_raw[a][:], wb[512 * a : 512 * (a + 1), :].rearrange("(p i) r -> p i r", i=4))
+        wgt = sb("wgt", [P, J], F32)
+        nc.sync.dma_start(wgt[:], wgt2)
+        xplanes = xT.rearrange("(p i) t -> i p t", i=4)
+        xw = [sb(f"xw{i}", [P, T], F32) for i in range(4)]
+        for i in range(4):
+            nc.sync.dma_start(wsc_raw[32 * i : 32 * i + 4, :].bitcast(I32), wa_scales[0, 4 * i : 4 * i + 4, :].bitcast(I32))
+            nc.sync.dma_start(wsc_raw[32 * i + 4 : 32 * i + 8, :].bitcast(I32), wd_scales[0, 4 * i : 4 * i + 4, :].bitcast(I32))
+            nc.sync.dma_start(xw[i][:], xplanes[i])
+        wa_raw = sb("wa_raw", [P, R], I32)
+        wd_raw = sb("wd_raw", [P, N], I32)
+        nc.sync.dma_start(wa_raw[:], wa_words[0].rearrange("p n i -> p (n i)").bitcast(I32))
+        nc.sync.dma_start(wd_raw[:], wd_words[0].rearrange("p n i -> p (n i)").bitcast(I32))
+
+        gs = sb("gs", [P, J], U8)
+        gw = sb("gw", [P, J], U32)
+        nc.vector.tensor_copy(gs[:], tabs[:].indirect(idx[:]))
+        nc.vector.tensor_copy(gw[:], tabw[:].bitcast(U32).indirect(idx[:]))
+        for q in range(4):
+            nc.scalar.dma_start(sc1[32 * q : 32 * q + 4, :].bitcast(I32), gs[32 * q + 4 : 32 * q + 8, :].bitcast(I32))
+        parted = sb("parted", [P, 4 * J], U8)
+        nc.vector.tensor_copy(
+            parted[:].bitcast(U16).rearrange("p (d j) -> p d j", d=2),
+            gw[:].bitcast(U16).rearrange("p (j d) -> p d j", d=2),
+        )
+        tab_sc = [gs, sc1]
+
+        wb_codes, wb_sc = [], []
+        for a in range(2):
+            wb_bf = sb(f"wb_bf{a}", [P, 4 * R], BF16)
+            nc.scalar.copy(
+                wb_bf[:].rearrange("p (t m i) -> p m i t", t=4, i=4),
+                wb_raw[a][:].rearrange("p i (m t) -> p m i t", t=4),
+            )
+            wb_codes.append(sb(f"wb_codes{a}", [P, R], U32))
+            wb_sc.append(sb(f"wb_sc{a}", [P, R], U8))
+            nc.vector.quantize_mx(out=wb_codes[a][:].bitcast(FP8X4), scales=wb_sc[a][:], in_=wb_bf[:])
+
+        yb = []
+        for b in range(J // BLK):
+            bank = psum.tile([P, 4, BLK], F32, name="bank_b", tag="bank_b", bufs=2)
+            for t in range(4):
+                for a in range(2):
+                    nc.tensor.matmul_mx(
+                        out=bank[:, t, :],
+                        lhsT=wb_codes[a][:, BLK * t : BLK * (t + 1)].bitcast(FP8X4),
+                        lhsT_scale=wb_sc[a][:, BLK * t : BLK * (t + 1)],
+                        rhs=parted[:, 2 * (J * a + BLK * b) : 2 * (J * a + BLK * (b + 1))].bitcast(FP4X4),
+                        rhs_scale=tab_sc[a][:, BLK * b : BLK * (b + 1)],
+                        start=(a == 0),
+                        stop=(a == 1),
+                    )
+            yb.append(sb(f"yb{b}", [P, BLK, 4], F32))
+            nc.scalar.copy(yb[b][:], bank[:].rearrange("p t n -> p n t"))
+
+        xg = [sb(f"xg{c}", [P, 4, w], F32) for c, w in enumerate(CHUNKS)]
+        for i in range(4):
+            for c, w in enumerate(CHUNKS):
+                j0 = starts[c]
+                nc.vector.tensor_tensor(
+                    xg[c][:, i, :], xw[i][:].indirect(idx2[:, j0 // 16 : (j0 + w) // 16]), wgt[:, j0 : j0 + w], MULT
+                )
+
+        wsc = sb("wsc", [P, R], U8)
+        nc.vector.tensor_copy(wsc[:].rearrange("p (t m) -> p t m", t=4), wsc_raw[:].rearrange("p (m t) -> p t m", t=4))
+
+        wa = sb("wa", [P, R], I32)
+        wd = sb("wd", [P, N], I32)
+        for dst, raw in ((wa, wa_raw), (wd, wd_raw)):
+            nc.vector.tensor_copy(
+                dst[:].rearrange("p (t c e) -> p c t e", t=4, e=4),
+                raw[:].rearrange("p (c e t) -> p c t e", t=4, e=4),
+            )
+
+        y_sc = sb("y_sc", [P, J], U8)
+        out_rows = out_0.rearrange("(p t) j -> p t j", t=4)
+        out_words = out_1[0].rearrange("p j i -> p (j i)").bitcast(I32)
+
+        def project(name, w_codes, w_sc, codes, sc, n0):
+            bank = psum.tile([P, 4, BLK], F32, name=name, tag=name, bufs=3)
+            for t in range(4):
+                nc.tensor.matmul_mx(
+                    out=bank[:, t, :],
+                    lhsT=w_codes[:, BLK * t : BLK * (t + 1)].bitcast(FP8X4),
+                    lhsT_scale=w_sc[:, BLK * t : BLK * (t + 1)],
+                    rhs=codes[:, n0 : n0 + BLK].bitcast(FP8X4),
+                    rhs_scale=sc[:, n0 : n0 + BLK],
+                    start=True,
+                    stop=True,
+                )
+            return bank
+
+        def interleave(engine_copy, dst, src):
+            engine_copy(
+                dst[:].rearrange("p (c e t) -> p c t e", t=4, e=4),
+                src[:].rearrange("p t (c e) -> p c t e", e=4),
+            )
+
+        for c, w in enumerate(CHUNKS):
+            j0 = starts[c]
+            x_bf = sb(f"x_bf{c}", [P, 4 * w], BF16)
+            interleave(nc.scalar.copy, x_bf, xg[c])
+            x_codes = sb(f"x_codes{c}", [P, w], U32)
+            x_sc = sb(f"x_sc{c}", [P, w], U8)
+            nc.vector.quantize_mx(out=x_codes[:].bitcast(FP8X4), scales=x_sc[:], in_=x_bf[:])
+            h_bf = sb(f"h_bf{c}", [P, 4 * w], BF16)
+            for n0 in range(0, w, BLK):
+                bank = project("bank_a", wa, wsc[:, :], x_codes, x_sc, n0)
+                nc.vector.tensor_tensor(
+                    h_bf[:, 4 * n0 : 4 * (n0 + BLK)].rearrange("p (n t) -> p n t", t=4),
+                    bank[:].rearrange("p t n -> p n t"),
+                    yb[(j0 + n0) // BLK][:],
+                    MULT,
+                )
+            h_codes = sb(f"h_codes{c}", [P, w], U32)
+            h_sc = sb(f"h_sc{c}", [P, w], U8)
+            nc.vector.quantize_mx(out=h_codes[:].bitcast(FP8X4), scales=h_sc[:], in_=h_bf[:])
+            y = sb(f"y{c}", [P, 4, w], F32)
+            for n0 in range(0, w, BLK):
+                bank = project("bank_y", wd, wsc[4:P, :], h_codes, h_sc, n0)
+                nc.scalar.copy(y[:, :, n0 : n0 + BLK], bank[:])
+            nc.sync.dma_start(out_rows[:, :, j0 : j0 + w], y[:])
+            y_bf = sb(f"y_bf{c}", [P, 4 * w], BF16)
+            interleave(nc.vector.tensor_copy, y_bf, y)
+            y_codes = sb(f"y_codes{c}", [P, w], U32)
+            nc.vector.quantize_mx(out=y_codes[:].bitcast(FP8X4), scales=y_sc[:, j0 : j0 + w], in_=y_bf[:])
+            nc.sync.dma_start(out_words[:, j0 : j0 + w], y_codes[:].bitcast(I32))
+        for q in range(4):
+            queue = nc.sync if q % 2 == 0 else nc.scalar
+            queue.dma_start(out_2[0, 4 * q : 4 * q + 4, :].bitcast(I32), y_sc[32 * q : 32 * q + 4, :].bitcast(I32))

@@ -17,7 +17,8 @@ MULT = mybir.AluOpType.mult
 
 P = 128
 BLK = 128
-CHUNKS = (256, 256, 256, 256)
+CHUNKS = (256, 256, 256, 128, 128)
+SCALAR_ROUNDS = (0, 1)
 
 
 def tile_list_htabg_mul_noneP_kernel(
@@ -29,68 +30,87 @@ def tile_list_htabg_mul_noneP_kernel(
         keep = ctx.enter_context(tc.tile_pool(name="keep", bufs=1))
         psum = ctx.enter_context(tc.psum_pool(name="psum", bufs=1))
 
-        def sb(name, shape, dtype):
-            return keep.tile(shape, dtype, name=name, align_bytes=64)
+        def sb(name, shape, dtype, tag=None):
+            return keep.tile(shape, dtype, name=name, tag=tag or name, align_bytes=64)
 
         idx = keep.tile([P, J // 16], U16, name="idx")
         idx2 = keep.tile([P, J // 16], U16, name="idx2")
         tabw = sb("tabw", [P, T], I32)
         tabs = sb("tabs", [P, T], U8)
         wsc_raw = sb("wsc_raw", [P, R], U8)
-        sc1 = sb("sc1", [P, J], U8)
+        tab_sc = sb("tab_sc", [P, 2 * J], U8)
 
-        nc.vector.memset(tabs[:].bitcast(I32), 0)
-        nc.vector.memset(wsc_raw[:].bitcast(I32), 0)
-        nc.vector.memset(sc1[:].bitcast(I32), 0)
+        nc.vector.memset(tabs[32:64, :].bitcast(I32), 0)
+        nc.vector.memset(tabs[64:P, :].bitcast(I32), 0)
+        nc.vector.memset(tab_sc[:].bitcast(I32), 0)
+        nc.vector.memset(wsc_raw[32:64, :].bitcast(I32), 0)
+        nc.vector.memset(wsc_raw[64:P, :].bitcast(I32), 0)
+        wsc = sb("wsc", [P, 2 * R], U8)
+        nc.vector.memset(wsc[:].bitcast(I32), 0)
 
-        nc.sync.dma_start(tabw[:], tab_words[0].rearrange("p n i -> p (n i)").bitcast(I32))
-        nc.sync.dma_start(idx2[:], offs2)
-        for q in range(4):
-            nc.sync.dma_start(tabs[32 * q : 32 * q + 8, :].bitcast(I32), tab_scales[:, 4 * q : 4 * q + 4, :].bitcast(I32))
         nc.sync.dma_start(idx[:], offs)
+        nc.sync.dma_start(tabs[0:32, :].bitcast(I32), tab_scales.rearrange("a s t -> s a t").bitcast(I32))
+        nc.sync.dma_start(idx2[:], offs2)
+        nc.sync.dma_start(wsc_raw[0:32:2, :].bitcast(I32), wa_scales[0].bitcast(I32))
+        nc.sync.dma_start(wsc_raw[1:32:2, :].bitcast(I32), wd_scales[0].bitcast(I32))
+        nc.sync.dma_start(tabw[:], tab_words[0].rearrange("p n i -> p (n i)").bitcast(I32))
         wb_raw = [sb(f"wb_raw{a}", [P, 4, R], F32) for a in range(2)]
-        for a in range(2):
-            nc.sync.dma_start(wb_raw[a][:], wb[512 * a : 512 * (a + 1), :].rearrange("(p i) r -> p i r", i=4))
         wgt = sb("wgt", [P, J], F32)
-        nc.sync.dma_start(wgt[:], wgt2)
         xplanes = xT.rearrange("(p i) t -> i p t", i=4)
-        xw = [sb(f"xw{i}", [P, T], F32) for i in range(4)]
-        for i in range(4):
-            nc.sync.dma_start(wsc_raw[32 * i : 32 * i + 4, :].bitcast(I32), wa_scales[0, 4 * i : 4 * i + 4, :].bitcast(I32))
-            nc.sync.dma_start(wsc_raw[32 * i + 4 : 32 * i + 8, :].bitcast(I32), wd_scales[0, 4 * i : 4 * i + 4, :].bitcast(I32))
+        xw = [sb("xw0", [P, T], F32)]
+
+        def load_wb(a):
+            nc.sync.dma_start(wb_raw[a][:], wb[512 * a : 512 * (a + 1), :].rearrange("(p i) r -> p i r", i=4))
+
+        load_wb(0)
+        nc.sync.dma_start(wgt[:], wgt2)
+        nc.sync.dma_start(xw[0][:], xplanes[0])
+        load_wb(1)
+        for i in range(1, 4):
+            xw.append(sb(f"xw{i}", [P, T], F32))
             nc.sync.dma_start(xw[i][:], xplanes[i])
-        wa_raw = sb("wa_raw", [P, R], I32)
-        wd_raw = sb("wd_raw", [P, N], I32)
-        nc.sync.dma_start(wa_raw[:], wa_words[0].rearrange("p n i -> p (n i)").bitcast(I32))
-        nc.sync.dma_start(wd_raw[:], wd_words[0].rearrange("p n i -> p (n i)").bitcast(I32))
 
         gs = sb("gs", [P, J], U8)
         gw = sb("gw", [P, J], U32)
         nc.vector.tensor_copy(gs[:], tabs[:].indirect(idx[:]))
-        nc.vector.tensor_copy(gw[:], tabw[:].bitcast(U32).indirect(idx[:]))
         for q in range(4):
-            nc.scalar.dma_start(sc1[32 * q : 32 * q + 4, :].bitcast(I32), gs[32 * q + 4 : 32 * q + 8, :].bitcast(I32))
+            nc.gpsimd.dma_start(
+                tab_sc[32 * q : 32 * q + 4, :].bitcast(I32).rearrange("r (a j) -> r a j", a=2),
+                gs[8 * q : 8 * q + 8, :].bitcast(I32),
+            )
+        wsc_dealt = sb("wsc_dealt", [P, R], U8)
+        nc.vector.tensor_copy(wsc_dealt[:].rearrange("p (t m) -> p t m", t=4), wsc_raw[:].rearrange("p (m t) -> p t m", t=4))
+        for q in range(4):
+            nc.gpsimd.dma_start(
+                wsc[32 * q : 32 * q + 4, :].bitcast(I32).rearrange("r (a j) -> r a j", a=2),
+                wsc_dealt[8 * q : 8 * q + 8, :].bitcast(I32),
+            )
+        nc.vector.tensor_copy(gw[:], tabw[:].bitcast(U32).indirect(idx[:]))
         parted = sb("parted", [P, 4 * J], U8)
         nc.vector.tensor_copy(
             parted[:].bitcast(U16).rearrange("p (d j) -> p d j", d=2),
             gw[:].bitcast(U16).rearrange("p (j d) -> p d j", d=2),
         )
-        tab_sc = [gs, sc1]
 
         wb_codes, wb_sc = [], []
         for a in range(2):
             wb_bf = sb(f"wb_bf{a}", [P, 4 * R], BF16)
             nc.scalar.copy(
-                wb_bf[:].rearrange("p (t m i) -> p m i t", t=4, i=4),
-                wb_raw[a][:].rearrange("p i (m t) -> p m i t", t=4),
+                wb_bf[:].rearrange("p (t m i) -> p m t i", t=4, i=4),
+                wb_raw[a][:].rearrange("p i (m t) -> p m t i", t=4),
             )
             wb_codes.append(sb(f"wb_codes{a}", [P, R], U32))
             wb_sc.append(sb(f"wb_sc{a}", [P, R], U8))
             nc.vector.quantize_mx(out=wb_codes[a][:].bitcast(FP8X4), scales=wb_sc[a][:], in_=wb_bf[:])
 
+        wa_raw = sb("wa_raw", [P, R], I32)
+        wd_raw = sb("wd_raw", [P, N], I32)
+        nc.sync.dma_start(wa_raw[:], wa_words[0].rearrange("p n i -> p (n i)").bitcast(I32))
+        nc.sync.dma_start(wd_raw[:], wd_words[0].rearrange("p n i -> p (n i)").bitcast(I32))
+
         yb = []
         for b in range(J // BLK):
-            bank = psum.tile([P, 4, BLK], F32, name="bank_b", tag="bank_b", bufs=2)
+            bank = psum.tile([P, 4, BLK], F32, name="bank_b", bufs=2)
             for t in range(4):
                 for a in range(2):
                     nc.tensor.matmul_mx(
@@ -98,7 +118,7 @@ def tile_list_htabg_mul_noneP_kernel(
                         lhsT=wb_codes[a][:, BLK * t : BLK * (t + 1)].bitcast(FP8X4),
                         lhsT_scale=wb_sc[a][:, BLK * t : BLK * (t + 1)],
                         rhs=parted[:, 2 * (J * a + BLK * b) : 2 * (J * a + BLK * (b + 1))].bitcast(FP4X4),
-                        rhs_scale=tab_sc[a][:, BLK * b : BLK * (b + 1)],
+                        rhs_scale=tab_sc[:, J * a + BLK * b : J * a + BLK * (b + 1)],
                         start=(a == 0),
                         stop=(a == 1),
                     )
@@ -106,6 +126,8 @@ def tile_list_htabg_mul_noneP_kernel(
             nc.scalar.copy(yb[b][:], bank[:].rearrange("p t n -> p n t"))
 
         xg = [sb(f"xg{c}", [P, 4, w], F32) for c, w in enumerate(CHUNKS)]
+        wa = sb("wa", [P, R], I32)
+        wd = sb("wd", [P, N], I32)
         for i in range(4):
             for c, w in enumerate(CHUNKS):
                 j0 = starts[c]
@@ -113,11 +135,6 @@ def tile_list_htabg_mul_noneP_kernel(
                     xg[c][:, i, :], xw[i][:].indirect(idx2[:, j0 // 16 : (j0 + w) // 16]), wgt[:, j0 : j0 + w], MULT
                 )
 
-        wsc = sb("wsc", [P, R], U8)
-        nc.vector.tensor_copy(wsc[:].rearrange("p (t m) -> p t m", t=4), wsc_raw[:].rearrange("p (m t) -> p t m", t=4))
-
-        wa = sb("wa", [P, R], I32)
-        wd = sb("wd", [P, N], I32)
         for dst, raw in ((wa, wa_raw), (wd, wd_raw)):
             nc.vector.tensor_copy(
                 dst[:].rearrange("p (t c e) -> p c t e", t=4, e=4),
@@ -128,8 +145,8 @@ def tile_list_htabg_mul_noneP_kernel(
         out_rows = out_0.rearrange("(p t) j -> p t j", t=4)
         out_words = out_1[0].rearrange("p j i -> p (j i)").bitcast(I32)
 
-        def project(name, w_codes, w_sc, codes, sc, n0):
-            bank = psum.tile([P, 4, BLK], F32, name=name, tag=name, bufs=3)
+        def project(name, bufs, w_codes, w_sc, codes, sc, n0):
+            bank = psum.tile([P, 4, BLK], F32, name=name, bufs=bufs)
             for t in range(4):
                 nc.tensor.matmul_mx(
                     out=bank[:, t, :],
@@ -144,8 +161,8 @@ def tile_list_htabg_mul_noneP_kernel(
 
         def interleave(engine_copy, dst, src):
             engine_copy(
-                dst[:].rearrange("p (c e t) -> p c t e", t=4, e=4),
-                src[:].rearrange("p t (c e) -> p c t e", e=4),
+                dst[:].rearrange("p (n t) -> p n t", t=4),
+                src[:].rearrange("p t n -> p n t"),
             )
 
         for c, w in enumerate(CHUNKS):
@@ -157,7 +174,7 @@ def tile_list_htabg_mul_noneP_kernel(
             nc.vector.quantize_mx(out=x_codes[:].bitcast(FP8X4), scales=x_sc[:], in_=x_bf[:])
             h_bf = sb(f"h_bf{c}", [P, 4 * w], BF16)
             for n0 in range(0, w, BLK):
-                bank = project("bank_a", wa, wsc[:, :], x_codes, x_sc, n0)
+                bank = project("bank_a", 3, wa, wsc[:, 0:R], x_codes, x_sc, n0)
                 nc.vector.tensor_tensor(
                     h_bf[:, 4 * n0 : 4 * (n0 + BLK)].rearrange("p (n t) -> p n t", t=4),
                     bank[:].rearrange("p t n -> p n t"),
@@ -168,12 +185,18 @@ def tile_list_htabg_mul_noneP_kernel(
             h_sc = sb(f"h_sc{c}", [P, w], U8)
             nc.vector.quantize_mx(out=h_codes[:].bitcast(FP8X4), scales=h_sc[:], in_=h_bf[:])
             y = sb(f"y{c}", [P, 4, w], F32)
-            for n0 in range(0, w, BLK):
-                bank = project("bank_y", wd, wsc[4:P, :], h_codes, h_sc, n0)
-                nc.scalar.copy(y[:, :, n0 : n0 + BLK], bank[:])
-            nc.sync.dma_start(out_rows[:, :, j0 : j0 + w], y[:])
             y_bf = sb(f"y_bf{c}", [P, 4 * w], BF16)
-            interleave(nc.vector.tensor_copy, y_bf, y)
+            for n0 in range(0, w, BLK):
+                bank = project("bank_y", 3, wd, wsc[:, R : 2 * R], h_codes, h_sc, n0)
+                nc.scalar.copy(y[:, :, n0 : n0 + BLK], bank[:])
+                if c in SCALAR_ROUNDS:
+                    nc.scalar.copy(
+                        y_bf[:, 4 * n0 : 4 * (n0 + BLK)].rearrange("p (n t) -> p n t", t=4),
+                        bank[:].rearrange("p t n -> p n t"),
+                    )
+            nc.sync.dma_start(out_rows[:, :, j0 : j0 + w], y[:])
+            if c not in SCALAR_ROUNDS:
+                interleave(nc.vector.tensor_copy, y_bf, y)
             y_codes = sb(f"y_codes{c}", [P, w], U32)
             nc.vector.quantize_mx(out=y_codes[:].bitcast(FP8X4), scales=y_sc[:, j0 : j0 + w], in_=y_bf[:])
             nc.sync.dma_start(out_words[:, j0 : j0 + w], y_codes[:].bitcast(I32))

@@ -17,6 +17,7 @@ MULT = mybir.AluOpType.mult
 
 P = 128
 BLK = 128
+ROW = J + R
 CHUNKS = (256, 256, 256, 128, 128)
 SCALAR_ROUNDS = (0, 1)
 
@@ -35,55 +36,49 @@ def tile_list_htabg_mul_noneP_kernel(
 
         idx = keep.tile([P, J // 16], U16, name="idx")
         idx2 = keep.tile([P, J // 16], U16, name="idx2")
-        tabw = sb("tabw", [P, T], I32)
-        tabs = sb("tabs", [P, T], U8)
-        wsc_raw = sb("wsc_raw", [P, R], U8)
-        tab_sc = sb("tab_sc", [P, 2 * J], U8)
+        tabw = sb("tabw", [P, T], I32, tag="x2")
+        tabs = sb("tabs", [P, T], U8, tag="wb_raw1")
+        wsc_raw = sb("wsc_raw", [P, R], U8, tag="x1")
+        planes = sb("planes", [P, 2 * ROW], U8)
 
-        nc.vector.memset(tabs[32:64, :].bitcast(I32), 0)
-        nc.vector.memset(tabs[64:P, :].bitcast(I32), 0)
-        nc.vector.memset(tab_sc[:].bitcast(I32), 0)
-        nc.vector.memset(wsc_raw[32:64, :].bitcast(I32), 0)
-        nc.vector.memset(wsc_raw[64:P, :].bitcast(I32), 0)
-        wsc = sb("wsc", [P, 2 * R], U8)
-        nc.vector.memset(wsc[:].bitcast(I32), 0)
+        for rows in (slice(32, 64), slice(64, P)):
+            nc.vector.memset(tabs[rows, :].bitcast(I32), 0)
+            nc.vector.memset(wsc_raw[rows, :].bitcast(I32), 0)
+        nc.vector.memset(planes[:].bitcast(I32), 0)
 
         nc.sync.dma_start(idx[:], offs)
         nc.sync.dma_start(tabs[0:32, :].bitcast(I32), tab_scales.rearrange("a s t -> s a t").bitcast(I32))
-        nc.sync.dma_start(idx2[:], offs2)
         nc.sync.dma_start(wsc_raw[0:32:2, :].bitcast(I32), wa_scales[0].bitcast(I32))
         nc.sync.dma_start(wsc_raw[1:32:2, :].bitcast(I32), wd_scales[0].bitcast(I32))
+        nc.sync.dma_start(idx2[:], offs2)
         nc.sync.dma_start(tabw[:], tab_words[0].rearrange("p n i -> p (n i)").bitcast(I32))
-        wb_raw = [sb(f"wb_raw{a}", [P, 4, R], F32) for a in range(2)]
         wgt = sb("wgt", [P, J], F32)
         xplanes = xT.rearrange("(p i) t -> i p t", i=4)
-        xw = [sb("xw0", [P, T], F32)]
+        wb_raw, xw = [], []
 
         def load_wb(a):
+            wb_raw.append(sb(f"wb_raw{a}", [P, 4, R], F32))
             nc.sync.dma_start(wb_raw[a][:], wb[512 * a : 512 * (a + 1), :].rearrange("(p i) r -> p i r", i=4))
+
+        def load_x(i):
+            xw.append(sb(f"xw{i}", [P, T], F32, tag=f"x{i}"))
+            nc.sync.dma_start(xw[i][:], xplanes[i])
 
         load_wb(0)
         nc.sync.dma_start(wgt[:], wgt2)
-        nc.sync.dma_start(xw[0][:], xplanes[0])
-        load_wb(1)
-        for i in range(1, 4):
-            xw.append(sb(f"xw{i}", [P, T], F32))
-            nc.sync.dma_start(xw[i][:], xplanes[i])
 
         gs = sb("gs", [P, J], U8)
-        gw = sb("gw", [P, J], U32)
+        gw = sb("gw", [P, J], U32, tag="x3")
+        rows = sb("rows", [P, ROW], U8)
         nc.vector.tensor_copy(gs[:], tabs[:].indirect(idx[:]))
+        nc.vector.tensor_copy(
+            rows[:, J:ROW].rearrange("p (t m) -> p t m", t=4), wsc_raw[:].rearrange("p (m t) -> p t m", t=4)
+        )
+        nc.vector.tensor_copy(rows[:, 0:J].bitcast(I32), gs[:].bitcast(I32))
         for q in range(4):
-            nc.gpsimd.dma_start(
-                tab_sc[32 * q : 32 * q + 4, :].bitcast(I32).rearrange("r (a j) -> r a j", a=2),
-                gs[8 * q : 8 * q + 8, :].bitcast(I32),
-            )
-        wsc_dealt = sb("wsc_dealt", [P, R], U8)
-        nc.vector.tensor_copy(wsc_dealt[:].rearrange("p (t m) -> p t m", t=4), wsc_raw[:].rearrange("p (m t) -> p t m", t=4))
-        for q in range(4):
-            nc.gpsimd.dma_start(
-                wsc[32 * q : 32 * q + 4, :].bitcast(I32).rearrange("r (a j) -> r a j", a=2),
-                wsc_dealt[8 * q : 8 * q + 8, :].bitcast(I32),
+            nc.scalar.dma_start(
+                planes[32 * q : 32 * q + 4, :].bitcast(I32).rearrange("r (a j) -> r a j", a=2),
+                rows[8 * q : 8 * q + 8, :].bitcast(I32),
             )
         nc.vector.tensor_copy(gw[:], tabw[:].bitcast(U32).indirect(idx[:]))
         parted = sb("parted", [P, 4 * J], U8)
@@ -91,6 +86,10 @@ def tile_list_htabg_mul_noneP_kernel(
             parted[:].bitcast(U16).rearrange("p (d j) -> p d j", d=2),
             gw[:].bitcast(U16).rearrange("p (j d) -> p d j", d=2),
         )
+        load_x(0)
+        load_wb(1)
+        for i in range(1, 4):
+            load_x(i)
 
         wb_codes, wb_sc = [], []
         for a in range(2):
@@ -103,8 +102,8 @@ def tile_list_htabg_mul_noneP_kernel(
             wb_sc.append(sb(f"wb_sc{a}", [P, R], U8))
             nc.vector.quantize_mx(out=wb_codes[a][:].bitcast(FP8X4), scales=wb_sc[a][:], in_=wb_bf[:])
 
-        wa_raw = sb("wa_raw", [P, R], I32)
-        wd_raw = sb("wd_raw", [P, N], I32)
+        wa_raw = sb("wa_raw", [P, R], I32, tag="wb_raw0")
+        wd_raw = sb("wd_raw", [P, N], I32, tag="wb_bf0")
         nc.sync.dma_start(wa_raw[:], wa_words[0].rearrange("p n i -> p (n i)").bitcast(I32))
         nc.sync.dma_start(wd_raw[:], wd_words[0].rearrange("p n i -> p (n i)").bitcast(I32))
 
@@ -118,7 +117,7 @@ def tile_list_htabg_mul_noneP_kernel(
                         lhsT=wb_codes[a][:, BLK * t : BLK * (t + 1)].bitcast(FP8X4),
                         lhsT_scale=wb_sc[a][:, BLK * t : BLK * (t + 1)],
                         rhs=parted[:, 2 * (J * a + BLK * b) : 2 * (J * a + BLK * (b + 1))].bitcast(FP4X4),
-                        rhs_scale=tab_sc[:, J * a + BLK * b : J * a + BLK * (b + 1)],
+                        rhs_scale=planes[:, ROW * a + BLK * b : ROW * a + BLK * (b + 1)],
                         start=(a == 0),
                         stop=(a == 1),
                     )
@@ -174,7 +173,7 @@ def tile_list_htabg_mul_noneP_kernel(
             nc.vector.quantize_mx(out=x_codes[:].bitcast(FP8X4), scales=x_sc[:], in_=x_bf[:])
             h_bf = sb(f"h_bf{c}", [P, 4 * w], BF16)
             for n0 in range(0, w, BLK):
-                bank = project("bank_a", 3, wa, wsc[:, 0:R], x_codes, x_sc, n0)
+                bank = project("bank_a", 3, wa, planes[:, J:ROW], x_codes, x_sc, n0)
                 nc.vector.tensor_tensor(
                     h_bf[:, 4 * n0 : 4 * (n0 + BLK)].rearrange("p (n t) -> p n t", t=4),
                     bank[:].rearrange("p t n -> p n t"),
@@ -187,7 +186,7 @@ def tile_list_htabg_mul_noneP_kernel(
             y = sb(f"y{c}", [P, 4, w], F32)
             y_bf = sb(f"y_bf{c}", [P, 4 * w], BF16)
             for n0 in range(0, w, BLK):
-                bank = project("bank_y", 3, wd, wsc[:, R : 2 * R], h_codes, h_sc, n0)
+                bank = project("bank_y", 3, wd, planes[:, ROW + J : 2 * ROW], h_codes, h_sc, n0)
                 nc.scalar.copy(y[:, :, n0 : n0 + BLK], bank[:])
                 if c in SCALAR_ROUNDS:
                     nc.scalar.copy(

@@ -18,6 +18,7 @@ MULT = mybir.AluOpType.mult
 P = 128
 BLK = 128
 ROW = J + R
+HALF = 512
 CHUNKS = (256, 256, 256, 128, 128)
 SCALAR_ROUNDS = (0, 1)
 
@@ -36,9 +37,9 @@ def tile_list_htabg_mul_noneP_kernel(
 
         idx = keep.tile([P, J // 16], U16, name="idx")
         idx2 = keep.tile([P, J // 16], U16, name="idx2")
-        tabw = sb("tabw", [P, T], I32, tag="x2")
-        tabs = sb("tabs", [P, T], U8, tag="wb_raw1")
-        wsc_raw = sb("wsc_raw", [P, R], U8, tag="x1")
+        tabw = sb("tabw", [P, T], I32, tag="x1")
+        tabs = sb("tabs", [P, T], U8, tag="x0")
+        wsc_raw = sb("wsc_raw", [P, R], U8, tag="wgt1")
         planes = sb("planes", [P, 2 * ROW], U8)
 
         for rows in (slice(32, 64), slice(64, P)):
@@ -52,23 +53,27 @@ def tile_list_htabg_mul_noneP_kernel(
         nc.sync.dma_start(wsc_raw[1:32:2, :].bitcast(I32), wd_scales[0].bitcast(I32))
         nc.sync.dma_start(idx2[:], offs2)
         nc.sync.dma_start(tabw[:], tab_words[0].rearrange("p n i -> p (n i)").bitcast(I32))
-        wgt = sb("wgt", [P, J], F32)
         xplanes = xT.rearrange("(p i) t -> i p t", i=4)
-        wb_raw, xw = [], []
+        wb_raw, xw, wgt = [], [], []
 
         def load_wb(a):
-            wb_raw.append(sb(f"wb_raw{a}", [P, 4, R], F32))
+            wb_raw.append(sb(f"wb_raw{a}", [P, 4, R], F32, tag=("x3", "wd_raw")[a]))
             nc.sync.dma_start(wb_raw[a][:], wb[512 * a : 512 * (a + 1), :].rearrange("(p i) r -> p i r", i=4))
 
         def load_x(i):
             xw.append(sb(f"xw{i}", [P, T], F32, tag=f"x{i}"))
             nc.sync.dma_start(xw[i][:], xplanes[i])
 
+        def load_wgt(h):
+            wgt.append(sb(f"wgt{h}", [P, HALF], F32))
+            nc.sync.dma_start(wgt[h][:], wgt2[:, HALF * h : HALF * (h + 1)])
+
         load_wb(0)
-        nc.sync.dma_start(wgt[:], wgt2)
+        load_wb(1)
+        load_wgt(0)
 
         gs = sb("gs", [P, J], U8)
-        gw = sb("gw", [P, J], U32, tag="x3")
+        gw = sb("gw", [P, J], U32, tag="x2")
         rows = sb("rows", [P, ROW], U8)
         nc.vector.tensor_copy(gs[:], tabs[:].indirect(idx[:]))
         nc.vector.tensor_copy(
@@ -87,13 +92,13 @@ def tile_list_htabg_mul_noneP_kernel(
             gw[:].bitcast(U16).rearrange("p (j d) -> p d j", d=2),
         )
         load_x(0)
-        load_wb(1)
-        for i in range(1, 4):
-            load_x(i)
+        load_wgt(1)
+        load_x(1)
+        load_x(2)
 
         wb_codes, wb_sc = [], []
         for a in range(2):
-            wb_bf = sb(f"wb_bf{a}", [P, 4 * R], BF16)
+            wb_bf = sb(f"wb_bf{a}", [P, 4 * R], BF16, tag=("wa_raw", "wb_bf1")[a])
             nc.scalar.copy(
                 wb_bf[:].rearrange("p (t m i) -> p m t i", t=4, i=4),
                 wb_raw[a][:].rearrange("p i (m t) -> p m t i", t=4),
@@ -102,36 +107,38 @@ def tile_list_htabg_mul_noneP_kernel(
             wb_sc.append(sb(f"wb_sc{a}", [P, R], U8))
             nc.vector.quantize_mx(out=wb_codes[a][:].bitcast(FP8X4), scales=wb_sc[a][:], in_=wb_bf[:])
 
-        wa_raw = sb("wa_raw", [P, R], I32, tag="wb_raw0")
-        wd_raw = sb("wd_raw", [P, N], I32, tag="wb_bf0")
+        load_x(3)
+        wa_raw = sb("wa_raw", [P, R], I32)
+        wd_raw = sb("wd_raw", [P, N], I32)
         nc.sync.dma_start(wa_raw[:], wa_words[0].rearrange("p n i -> p (n i)").bitcast(I32))
         nc.sync.dma_start(wd_raw[:], wd_words[0].rearrange("p n i -> p (n i)").bitcast(I32))
 
+        banks = [psum.tile([P, 4, BLK], F32, name=("bank_a", "bank_y")[b // 4], bufs=4) for b in range(J // BLK)]
         yb = []
-        for b in range(J // BLK):
-            bank = psum.tile([P, 4, BLK], F32, name="bank_b", bufs=2)
-            for t in range(4):
-                for a in range(2):
+        for a in range(2):
+            for b, bank in enumerate(banks):
+                for t in range(4):
                     nc.tensor.matmul_mx(
                         out=bank[:, t, :],
                         lhsT=wb_codes[a][:, BLK * t : BLK * (t + 1)].bitcast(FP8X4),
                         lhsT_scale=wb_sc[a][:, BLK * t : BLK * (t + 1)],
                         rhs=parted[:, 2 * (J * a + BLK * b) : 2 * (J * a + BLK * (b + 1))].bitcast(FP4X4),
                         rhs_scale=planes[:, ROW * a + BLK * b : ROW * a + BLK * (b + 1)],
-                        start=(a == 0),
-                        stop=(a == 1),
+                        start=(a == 0 and t == 0),
+                        stop=(a == 1 and t == 3),
                     )
-            yb.append(sb(f"yb{b}", [P, BLK, 4], F32))
-            nc.scalar.copy(yb[b][:], bank[:].rearrange("p t n -> p n t"))
+                if a == 1:
+                    yb.append(sb(f"yb{b}", [P, BLK, 4], F32))
+                    nc.scalar.copy(yb[b][:], bank[:].rearrange("p t n -> p n t"))
 
-        xg = [sb(f"xg{c}", [P, 4, w], F32) for c, w in enumerate(CHUNKS)]
+        xg = [sb(f"xg{h}", [P, 4, HALF], F32) for h in range(J // HALF)]
         wa = sb("wa", [P, R], I32)
         wd = sb("wd", [P, N], I32)
         for i in range(4):
-            for c, w in enumerate(CHUNKS):
-                j0 = starts[c]
+            for j0, w in zip(starts, CHUNKS) if i == 3 else ((0, HALF), (HALF, HALF)):
+                h, n0 = divmod(j0, HALF)
                 nc.vector.tensor_tensor(
-                    xg[c][:, i, :], xw[i][:].indirect(idx2[:, j0 // 16 : (j0 + w) // 16]), wgt[:, j0 : j0 + w], MULT
+                    xg[h][:, i, n0 : n0 + w], xw[i][:].indirect(idx2[:, j0 // 16 : (j0 + w) // 16]), wgt[h][:, n0 : n0 + w], MULT
                 )
 
         for dst, raw in ((wa, wa_raw), (wd, wd_raw)):
@@ -161,19 +168,19 @@ def tile_list_htabg_mul_noneP_kernel(
         def interleave(engine_copy, dst, src):
             engine_copy(
                 dst[:].rearrange("p (n t) -> p n t", t=4),
-                src[:].rearrange("p t n -> p n t"),
+                src.rearrange("p t n -> p n t"),
             )
 
         for c, w in enumerate(CHUNKS):
             j0 = starts[c]
             x_bf = sb(f"x_bf{c}", [P, 4 * w], BF16)
-            interleave(nc.scalar.copy, x_bf, xg[c])
+            interleave(nc.scalar.copy, x_bf, xg[j0 // HALF][:, :, j0 % HALF : j0 % HALF + w])
             x_codes = sb(f"x_codes{c}", [P, w], U32)
             x_sc = sb(f"x_sc{c}", [P, w], U8)
             nc.vector.quantize_mx(out=x_codes[:].bitcast(FP8X4), scales=x_sc[:], in_=x_bf[:])
             h_bf = sb(f"h_bf{c}", [P, 4 * w], BF16)
             for n0 in range(0, w, BLK):
-                bank = project("bank_a", 3, wa, planes[:, J:ROW], x_codes, x_sc, n0)
+                bank = project("bank_a", 4, wa, planes[:, J:ROW], x_codes, x_sc, n0)
                 nc.vector.tensor_tensor(
                     h_bf[:, 4 * n0 : 4 * (n0 + BLK)].rearrange("p (n t) -> p n t", t=4),
                     bank[:].rearrange("p t n -> p n t"),
@@ -186,7 +193,7 @@ def tile_list_htabg_mul_noneP_kernel(
             y = sb(f"y{c}", [P, 4, w], F32)
             y_bf = sb(f"y_bf{c}", [P, 4 * w], BF16)
             for n0 in range(0, w, BLK):
-                bank = project("bank_y", 3, wd, planes[:, ROW + J : 2 * ROW], h_codes, h_sc, n0)
+                bank = project("bank_y", 4, wd, planes[:, ROW + J : 2 * ROW], h_codes, h_sc, n0)
                 nc.scalar.copy(y[:, :, n0 : n0 + BLK], bank[:])
                 if c in SCALAR_ROUNDS:
                     nc.scalar.copy(
@@ -195,7 +202,7 @@ def tile_list_htabg_mul_noneP_kernel(
                     )
             nc.sync.dma_start(out_rows[:, :, j0 : j0 + w], y[:])
             if c not in SCALAR_ROUNDS:
-                interleave(nc.vector.tensor_copy, y_bf, y)
+                interleave(nc.vector.tensor_copy, y_bf, y[:])
             y_codes = sb(f"y_codes{c}", [P, w], U32)
             nc.vector.quantize_mx(out=y_codes[:].bitcast(FP8X4), scales=y_sc[:, j0 : j0 + w], in_=y_bf[:])
             nc.sync.dma_start(out_words[:, j0 : j0 + w], y_codes[:].bitcast(I32))

@@ -19,8 +19,9 @@ P = 128
 BLK = 128
 ROW = J + R
 HALF = 512
-CHUNKS = (256, 256, 256, 128, 128)
-SCALAR_ROUNDS = (0, 1)
+CHUNKS = (128, 128, 256, 256, 128, 128)
+SCALAR_ROUNDS = (0, 1, 2)
+CODE_STORES = (3, 5)
 
 
 def tile_list_htabg_mul_noneP_kernel(
@@ -37,15 +38,19 @@ def tile_list_htabg_mul_noneP_kernel(
 
         idx = keep.tile([P, J // 16], U16, name="idx")
         idx2 = keep.tile([P, J // 16], U16, name="idx2")
-        tabw = sb("tabw", [P, T], I32, tag="x1")
-        tabs = sb("tabs", [P, T], U8, tag="x0")
-        wsc_raw = sb("wsc_raw", [P, R], U8, tag="wgt1")
+        tabw = sb("tabw", [P, T], I32, tag="wgt1")
+        tabs = sb("tabs", [P, T], U8)
+        wsc_raw = sb("wsc_raw", [P, R], U8)
         planes = sb("planes", [P, 2 * ROW], U8)
 
         for rows in (slice(32, 64), slice(64, P)):
             nc.vector.memset(tabs[rows, :].bitcast(I32), 0)
             nc.vector.memset(wsc_raw[rows, :].bitcast(I32), 0)
         nc.vector.memset(planes[:].bitcast(I32), 0)
+
+        warm = sb("warm", [P, 2], F32)
+        nc.vector.memset(warm[:, 0:1], 0.0)
+        nc.scalar.copy(warm[:, 1:2], warm[:, 0:1])
 
         nc.sync.dma_start(idx[:], offs)
         nc.sync.dma_start(tabs[0:32, :].bitcast(I32), tab_scales.rearrange("a s t -> s a t").bitcast(I32))
@@ -57,7 +62,7 @@ def tile_list_htabg_mul_noneP_kernel(
         wb_raw, xw, wgt = [], [], []
 
         def load_wb(a):
-            wb_raw.append(sb(f"wb_raw{a}", [P, 4, R], F32, tag=("x3", "wd_raw")[a]))
+            wb_raw.append(sb(f"wb_raw{a}", [P, 4, R], F32, tag=("x2", "x3")[a]))
             nc.sync.dma_start(wb_raw[a][:], wb[512 * a : 512 * (a + 1), :].rearrange("(p i) r -> p i r", i=4))
 
         def load_x(i):
@@ -72,8 +77,8 @@ def tile_list_htabg_mul_noneP_kernel(
         load_wb(1)
         load_wgt(0)
 
-        gs = sb("gs", [P, J], U8)
-        gw = sb("gw", [P, J], U32, tag="x2")
+        gs = sb("gs", [P, J], U8, tag="x0")
+        gw = sb("gw", [P, J], U32, tag="x1")
         rows = sb("rows", [P, ROW], U8)
         nc.vector.tensor_copy(gs[:], tabs[:].indirect(idx[:]))
         nc.vector.tensor_copy(
@@ -94,29 +99,43 @@ def tile_list_htabg_mul_noneP_kernel(
         load_x(0)
         load_wgt(1)
         load_x(1)
-        load_x(2)
 
-        wb_codes, wb_sc = [], []
+        wb_codes, wb_sc, wb_bf = [], [], []
         for a in range(2):
-            wb_bf = sb(f"wb_bf{a}", [P, 4 * R], BF16, tag=("wa_raw", "wb_bf1")[a])
-            nc.scalar.copy(
-                wb_bf[:].rearrange("p (t m i) -> p m t i", t=4, i=4),
-                wb_raw[a][:].rearrange("p i (m t) -> p m t i", t=4),
-            )
+            wb_bf.append(sb(f"wb_bf{a}", [P, 4, BLK, 4], BF16, tag=("wa_raw", "wd_raw")[a]))
             wb_codes.append(sb(f"wb_codes{a}", [P, R], U32))
             wb_sc.append(sb(f"wb_sc{a}", [P, R], U8))
-            nc.vector.quantize_mx(out=wb_codes[a][:].bitcast(FP8X4), scales=wb_sc[a][:], in_=wb_bf[:])
 
+        def round_wb(copy, a, m0, m1):
+            copy(
+                wb_bf[a][:, :, m0:m1, :].rearrange("p t m i -> p m i t"),
+                wb_raw[a][:, :, 4 * m0 : 4 * m1].rearrange("p i (m t) -> p m i t", t=4),
+            )
+
+        def quant_wb(a, t0, t1):
+            cols = slice(BLK * t0, BLK * t1)
+            nc.vector.quantize_mx(
+                out=wb_codes[a][:, cols].bitcast(FP8X4), scales=wb_sc[a][:, cols],
+                in_=wb_bf[a][:, t0:t1].rearrange("p t m i -> p (t m i)"),
+            )
+
+        round_wb(nc.scalar.copy, 0, 0, BLK)
+        round_wb(nc.vector.tensor_copy, 1, 0, BLK // 2)
+        quant_wb(0, 0, 4)
+        round_wb(nc.scalar.copy, 1, BLK // 2, BLK)
+        quant_wb(1, 0, 4)
+
+        load_x(2)
         load_x(3)
         wa_raw = sb("wa_raw", [P, R], I32)
         wd_raw = sb("wd_raw", [P, N], I32)
         nc.sync.dma_start(wa_raw[:], wa_words[0].rearrange("p n i -> p (n i)").bitcast(I32))
         nc.sync.dma_start(wd_raw[:], wd_words[0].rearrange("p n i -> p (n i)").bitcast(I32))
 
-        banks = [psum.tile([P, 4, BLK], F32, name=("bank_a", "bank_y")[b // 4], bufs=4) for b in range(J // BLK)]
         yb = []
-        for a in range(2):
-            for b, bank in enumerate(banks):
+        for b in range(J // BLK):
+            bank = psum.tile([P, 4, BLK], F32, name=("bank_a", "bank_y")[b // 4], bufs=4)
+            for a in range(2):
                 for t in range(4):
                     nc.tensor.matmul_mx(
                         out=bank[:, t, :],
@@ -127,32 +146,39 @@ def tile_list_htabg_mul_noneP_kernel(
                         start=(a == 0 and t == 0),
                         stop=(a == 1 and t == 3),
                     )
-                if a == 1:
-                    yb.append(sb(f"yb{b}", [P, BLK, 4], F32))
-                    nc.scalar.copy(yb[b][:], bank[:].rearrange("p t n -> p n t"))
+            yb.append(sb(f"yb{b}", [P, BLK, 4], F32))
+            nc.scalar.copy(yb[b][:], bank[:].rearrange("p t n -> p n t"))
 
-        xg = [sb(f"xg{h}", [P, 4, HALF], F32) for h in range(J // HALF)]
-        wa = sb("wa", [P, R], I32)
-        wd = sb("wd", [P, N], I32)
+        def gather(dst, i, j0, w):
+            h, n0 = divmod(j0, HALF)
+            nc.vector.tensor_tensor(dst, xw[i][:].indirect(idx2[:, j0 // 16 : (j0 + w) // 16]), wgt[h][:, n0 : n0 + w], MULT)
+
+        def weave(copy, dst, src):
+            copy(dst, src.rearrange("p t n -> p n t"))
+
+        def weave_lines(copy, dst, src):
+            copy(dst.rearrange("p (c e) t -> p c t e", e=4), src.rearrange("p t (c e) -> p c t e", e=4))
+
+        xg = [sb(f"xg{h}", [P, 4, HALF], F32) for h in range(2)]
         for i in range(4):
             for j0, w in zip(starts, CHUNKS) if i == 3 else ((0, HALF), (HALF, HALF)):
-                h, n0 = divmod(j0, HALF)
-                nc.vector.tensor_tensor(
-                    xg[h][:, i, n0 : n0 + w], xw[i][:].indirect(idx2[:, j0 // 16 : (j0 + w) // 16]), wgt[h][:, n0 : n0 + w], MULT
-                )
+                gather(xg[j0 // HALF][:, i, j0 % HALF : j0 % HALF + w], i, j0, w)
+        wa = sb("wa", [P, R], I32)
+        wd = sb("wd", [P, N], I32)
 
-        for dst, raw in ((wa, wa_raw), (wd, wd_raw)):
+        def deal(dst, raw):
             nc.vector.tensor_copy(
                 dst[:].rearrange("p (t c e) -> p c t e", t=4, e=4),
                 raw[:].rearrange("p (c e t) -> p c t e", t=4, e=4),
             )
 
         y_sc = sb("y_sc", [P, J], U8)
+        y_codes = sb("y_codes", [P, J], U32)
         out_rows = out_0.rearrange("(p t) j -> p t j", t=4)
         out_words = out_1[0].rearrange("p j i -> p (j i)").bitcast(I32)
 
-        def project(name, bufs, w_codes, w_sc, codes, sc, n0):
-            bank = psum.tile([P, 4, BLK], F32, name=name, bufs=bufs)
+        def project(name, w_codes, w_sc, codes, sc, n0):
+            bank = psum.tile([P, 4, BLK], F32, name=name, bufs=4)
             for t in range(4):
                 nc.tensor.matmul_mx(
                     out=bank[:, t, :],
@@ -165,47 +191,43 @@ def tile_list_htabg_mul_noneP_kernel(
                 )
             return bank
 
-        def interleave(engine_copy, dst, src):
-            engine_copy(
-                dst[:].rearrange("p (n t) -> p n t", t=4),
-                src.rearrange("p t n -> p n t"),
-            )
-
+        stored = 0
         for c, w in enumerate(CHUNKS):
             j0 = starts[c]
-            x_bf = sb(f"x_bf{c}", [P, 4 * w], BF16)
-            interleave(nc.scalar.copy, x_bf, xg[j0 // HALF][:, :, j0 % HALF : j0 % HALF + w])
+            x_bf = sb(f"x_bf{c}", [P, w, 4], BF16)
+            weave_lines(nc.scalar.copy, x_bf[:], xg[j0 // HALF][:, :, j0 % HALF : j0 % HALF + w])
+            if c == 0:
+                deal(wa, wa_raw)
             x_codes = sb(f"x_codes{c}", [P, w], U32)
             x_sc = sb(f"x_sc{c}", [P, w], U8)
-            nc.vector.quantize_mx(out=x_codes[:].bitcast(FP8X4), scales=x_sc[:], in_=x_bf[:])
-            h_bf = sb(f"h_bf{c}", [P, 4 * w], BF16)
+            nc.vector.quantize_mx(out=x_codes[:].bitcast(FP8X4), scales=x_sc[:], in_=x_bf[:].rearrange("p n t -> p (n t)"))
+            if c == 0:
+                deal(wd, wd_raw)
+            h_bf = sb(f"h_bf{c}", [P, w, 4], BF16)
             for n0 in range(0, w, BLK):
-                bank = project("bank_a", 4, wa, planes[:, J:ROW], x_codes, x_sc, n0)
+                bank = project("bank_a", wa, planes[:, J:ROW], x_codes, x_sc, n0)
                 nc.vector.tensor_tensor(
-                    h_bf[:, 4 * n0 : 4 * (n0 + BLK)].rearrange("p (n t) -> p n t", t=4),
-                    bank[:].rearrange("p t n -> p n t"),
-                    yb[(j0 + n0) // BLK][:],
-                    MULT,
+                    h_bf[:, n0 : n0 + BLK, :], bank[:].rearrange("p t n -> p n t"), yb[(j0 + n0) // BLK][:], MULT
                 )
             h_codes = sb(f"h_codes{c}", [P, w], U32)
             h_sc = sb(f"h_sc{c}", [P, w], U8)
-            nc.vector.quantize_mx(out=h_codes[:].bitcast(FP8X4), scales=h_sc[:], in_=h_bf[:])
+            nc.vector.quantize_mx(out=h_codes[:].bitcast(FP8X4), scales=h_sc[:], in_=h_bf[:].rearrange("p n t -> p (n t)"))
             y = sb(f"y{c}", [P, 4, w], F32)
-            y_bf = sb(f"y_bf{c}", [P, 4 * w], BF16)
+            y_bf = sb(f"y_bf{c}", [P, w, 4], BF16)
             for n0 in range(0, w, BLK):
-                bank = project("bank_y", 4, wd, planes[:, ROW + J : 2 * ROW], h_codes, h_sc, n0)
+                bank = project("bank_y", wd, planes[:, ROW + J : 2 * ROW], h_codes, h_sc, n0)
                 nc.scalar.copy(y[:, :, n0 : n0 + BLK], bank[:])
                 if c in SCALAR_ROUNDS:
-                    nc.scalar.copy(
-                        y_bf[:, 4 * n0 : 4 * (n0 + BLK)].rearrange("p (n t) -> p n t", t=4),
-                        bank[:].rearrange("p t n -> p n t"),
-                    )
+                    weave(nc.scalar.copy, y_bf[:, n0 : n0 + BLK, :], bank[:])
             nc.sync.dma_start(out_rows[:, :, j0 : j0 + w], y[:])
             if c not in SCALAR_ROUNDS:
-                interleave(nc.vector.tensor_copy, y_bf, y[:])
-            y_codes = sb(f"y_codes{c}", [P, w], U32)
-            nc.vector.quantize_mx(out=y_codes[:].bitcast(FP8X4), scales=y_sc[:, j0 : j0 + w], in_=y_bf[:])
-            nc.sync.dma_start(out_words[:, j0 : j0 + w], y_codes[:].bitcast(I32))
+                weave_lines(nc.vector.tensor_copy, y_bf[:], y[:])
+            nc.vector.quantize_mx(
+                out=y_codes[:, j0 : j0 + w].bitcast(FP8X4), scales=y_sc[:, j0 : j0 + w], in_=y_bf[:].rearrange("p n t -> p (n t)")
+            )
+            if c in CODE_STORES:
+                nc.sync.dma_start(out_words[:, stored : j0 + w], y_codes[:, stored : j0 + w].bitcast(I32))
+                stored = j0 + w
         for q in range(4):
             queue = nc.sync if q % 2 == 0 else nc.scalar
             queue.dma_start(out_2[0, 4 * q : 4 * q + 4, :].bitcast(I32), y_sc[32 * q : 32 * q + 4, :].bitcast(I32))

@@ -1,6 +1,7 @@
 from contextlib import ExitStack
 
 import concourse.mybir as mybir
+from concourse.masks import make_identity
 
 K, L, R, N, T, J = 512, 1024, 512, 512, 2048, 1024
 FLOPS = 2 * J * (K * R + L * R + R * N)
@@ -38,7 +39,7 @@ def tile_list_htabg_mul_noneP_kernel(
 
         idx = keep.tile([P, J // 16], U16, name="idx")
         idx2 = keep.tile([P, J // 16], U16, name="idx2")
-        tabw = sb("tabw", [P, T], I32, tag="wgt1")
+        tabw = sb("tabw", [P, T], I32)
         tabs = sb("tabs", [P, T], U8)
         wsc_raw = sb("wsc_raw", [P, R], U8)
         planes = sb("planes", [P, 2 * ROW], U8)
@@ -47,6 +48,10 @@ def tile_list_htabg_mul_noneP_kernel(
             nc.vector.memset(tabs[rows, :].bitcast(I32), 0)
             nc.vector.memset(wsc_raw[rows, :].bitcast(I32), 0)
         nc.vector.memset(planes[:].bitcast(I32), 0)
+        wrows = sb("wrows", [P, BLK], F32)
+        nc.vector.memset(wrows[64:P, :], 0.0)
+        ident = sb("ident", [P, P], F32)
+        make_identity(nc, ident[:])
 
         warm = sb("warm", [P, 2], F32)
         nc.vector.memset(warm[:, 0:1], 0.0)
@@ -57,6 +62,7 @@ def tile_list_htabg_mul_noneP_kernel(
         nc.sync.dma_start(wsc_raw[0:32:2, :].bitcast(I32), wa_scales[0].bitcast(I32))
         nc.sync.dma_start(wsc_raw[1:32:2, :].bitcast(I32), wd_scales[0].bitcast(I32))
         nc.sync.dma_start(idx2[:], offs2)
+        nc.sync.dma_start(wrows[0:64, :], wgt2[0:P:16, :].rearrange("g (c e) -> g c e", e=BLK))
         nc.sync.dma_start(tabw[:], tab_words[0].rearrange("p n i -> p (n i)").bitcast(I32))
         xplanes = xT.rearrange("(p i) t -> i p t", i=4)
         wb_raw, xw, wgt = [], [], []
@@ -69,13 +75,21 @@ def tile_list_htabg_mul_noneP_kernel(
             xw.append(sb(f"xw{i}", [P, T], F32, tag=f"x{i}"))
             nc.sync.dma_start(xw[i][:], xplanes[i])
 
-        def load_wgt(h):
-            wgt.append(sb(f"wgt{h}", [P, HALF], F32))
-            nc.sync.dma_start(wgt[h][:], wgt2[:, HALF * h : HALF * (h + 1)])
-
         load_wb(0)
         load_wb(1)
-        load_wgt(0)
+
+        turned = psum.tile([P, 4, BLK], F32, name="bank_a", bufs=4)
+        nc.tensor.transpose(turned[:, 0, :], wrows[:], ident[:])
+        spread = sb("spread", [P, 8, 8, 16], F32)
+        nc.scalar.copy(
+            spread[:], turned[:, 0, 0:64].rearrange("e (g c) -> e c g", c=8).unsqueeze(3).to_broadcast([P, 8, 8, 16])
+        )
+        for h in range(2):
+            back = psum.tile([P, 4, BLK], F32, name="bank_a", bufs=4)
+            for c in range(4):
+                nc.tensor.transpose(back[:, c, :], spread[:, 4 * h + c].rearrange("e g s -> e (g s)"), ident[:])
+            wgt.append(sb(f"wgt{h}", [P, HALF], F32))
+            nc.scalar.copy(wgt[h][:], back[:].rearrange("p c e -> p (c e)"))
 
         gs = sb("gs", [P, J], U8, tag="x0")
         gw = sb("gw", [P, J], U32, tag="x1")
@@ -97,7 +111,6 @@ def tile_list_htabg_mul_noneP_kernel(
             gw[:].bitcast(U16).rearrange("p (j d) -> p d j", d=2),
         )
         load_x(0)
-        load_wgt(1)
         load_x(1)
 
         wb_codes, wb_sc, wb_bf = [], [], []
@@ -191,7 +204,7 @@ def tile_list_htabg_mul_noneP_kernel(
                 )
             return bank
 
-        stored = 0
+        xq = []
         for c, w in enumerate(CHUNKS):
             j0 = starts[c]
             x_bf = sb(f"x_bf{c}", [P, w, 4], BF16)
@@ -201,27 +214,43 @@ def tile_list_htabg_mul_noneP_kernel(
             x_codes = sb(f"x_codes{c}", [P, w], U32)
             x_sc = sb(f"x_sc{c}", [P, w], U8)
             nc.vector.quantize_mx(out=x_codes[:].bitcast(FP8X4), scales=x_sc[:], in_=x_bf[:].rearrange("p n t -> p (n t)"))
-            if c == 0:
+            xq.append((x_codes, x_sc))
+            if c == 1:
                 deal(wd, wd_raw)
+
+        ys = []
+        for c, w in enumerate(CHUNKS):
+            j0 = starts[c]
             h_bf = sb(f"h_bf{c}", [P, w, 4], BF16)
             for n0 in range(0, w, BLK):
-                bank = project("bank_a", wa, planes[:, J:ROW], x_codes, x_sc, n0)
+                bank = project("bank_a", wa, planes[:, J:ROW], *xq[c], n0)
                 nc.vector.tensor_tensor(
                     h_bf[:, n0 : n0 + BLK, :], bank[:].rearrange("p t n -> p n t"), yb[(j0 + n0) // BLK][:], MULT
                 )
             h_codes = sb(f"h_codes{c}", [P, w], U32)
             h_sc = sb(f"h_sc{c}", [P, w], U8)
             nc.vector.quantize_mx(out=h_codes[:].bitcast(FP8X4), scales=h_sc[:], in_=h_bf[:].rearrange("p n t -> p (n t)"))
-            y = sb(f"y{c}", [P, 4, w], F32)
+            if c != 1:
+                y_wide = sb(f"y{c}", [P, 4, 2 * w if c == 0 else w], F32)
+            y = y_wide[:, :, w : 2 * w] if c == 1 else y_wide[:, :, 0:w]
             y_bf = sb(f"y_bf{c}", [P, w, 4], BF16)
             for n0 in range(0, w, BLK):
                 bank = project("bank_y", wd, planes[:, ROW + J : 2 * ROW], h_codes, h_sc, n0)
                 nc.scalar.copy(y[:, :, n0 : n0 + BLK], bank[:])
                 if c in SCALAR_ROUNDS:
                     weave(nc.scalar.copy, y_bf[:, n0 : n0 + BLK, :], bank[:])
-            nc.sync.dma_start(out_rows[:, :, j0 : j0 + w], y[:])
+            if c == 1:
+                nc.sync.dma_start(out_rows[:, :, 0 : 2 * w], y_wide[:])
+            elif c > 1:
+                nc.sync.dma_start(out_rows[:, :, j0 : j0 + w], y)
+            ys.append((y, y_bf))
+
+        stored = 0
+        for c, w in enumerate(CHUNKS):
+            j0 = starts[c]
+            y, y_bf = ys[c]
             if c not in SCALAR_ROUNDS:
-                weave_lines(nc.vector.tensor_copy, y_bf[:], y[:])
+                weave_lines(nc.vector.tensor_copy, y_bf[:], y)
             nc.vector.quantize_mx(
                 out=y_codes[:, j0 : j0 + w].bitcast(FP8X4), scales=y_sc[:, j0 : j0 + w], in_=y_bf[:].rearrange("p n t -> p (n t)")
             )

@@ -20,9 +20,10 @@ P = 128
 BLK = 128
 ROW = J + R
 HALF = 512
-CHUNKS = (128, 128, 256, 256, 128, 128)
-SCALAR_ROUNDS = (0, 1, 2)
-CODE_STORES = (3, 5)
+CHUNKS = (256, 256, 256, 128, 128)
+SCALAR_ROUNDS = (0, 1)
+CODE_STORES = {0: 0, 1: 256, 2: 512, 4: 768}
+LAG = 1
 
 
 def tile_list_htabg_mul_noneP_kernel(
@@ -65,7 +66,7 @@ def tile_list_htabg_mul_noneP_kernel(
         nc.sync.dma_start(wrows[0:64, :], wgt2[0:P:16, :].rearrange("g (c e) -> g c e", e=BLK))
         nc.sync.dma_start(tabw[:], tab_words[0].rearrange("p n i -> p (n i)").bitcast(I32))
         xplanes = xT.rearrange("(p i) t -> i p t", i=4)
-        wb_raw, xw, wgt = [], [], []
+        wb_raw, xw = [], []
 
         def load_wb(a):
             wb_raw.append(sb(f"wb_raw{a}", [P, 4, R], F32, tag=("x2", "x3")[a]))
@@ -84,12 +85,12 @@ def tile_list_htabg_mul_noneP_kernel(
         nc.scalar.copy(
             spread[:], turned[:, 0, 0:64].rearrange("e (g c) -> e c g", c=8).unsqueeze(3).to_broadcast([P, 8, 8, 16])
         )
+        wgt = sb("wgt", [P, J], F32)
         for h in range(2):
             back = psum.tile([P, 4, BLK], F32, name="bank_a", bufs=4)
             for c in range(4):
                 nc.tensor.transpose(back[:, c, :], spread[:, 4 * h + c].rearrange("e g s -> e (g s)"), ident[:])
-            wgt.append(sb(f"wgt{h}", [P, HALF], F32))
-            nc.scalar.copy(wgt[h][:], back[:].rearrange("p c e -> p (c e)"))
+            nc.scalar.copy(wgt[:, HALF * h : HALF * (h + 1)], back[:].rearrange("p c e -> p (c e)"))
 
         gs = sb("gs", [P, J], U8, tag="x0")
         gw = sb("gw", [P, J], U32, tag="x1")
@@ -163,8 +164,7 @@ def tile_list_htabg_mul_noneP_kernel(
             nc.scalar.copy(yb[b][:], bank[:].rearrange("p t n -> p n t"))
 
         def gather(dst, i, j0, w):
-            h, n0 = divmod(j0, HALF)
-            nc.vector.tensor_tensor(dst, xw[i][:].indirect(idx2[:, j0 // 16 : (j0 + w) // 16]), wgt[h][:, n0 : n0 + w], MULT)
+            nc.vector.tensor_tensor(dst, xw[i][:].indirect(idx2[:, j0 // 16 : (j0 + w) // 16]), wgt[:, j0 : j0 + w], MULT)
 
         def weave(copy, dst, src):
             copy(dst, src.rearrange("p t n -> p n t"))
@@ -172,10 +172,10 @@ def tile_list_htabg_mul_noneP_kernel(
         def weave_lines(copy, dst, src):
             copy(dst.rearrange("p (c e) t -> p c t e", e=4), src.rearrange("p t (c e) -> p c t e", e=4))
 
-        xg = [sb(f"xg{h}", [P, 4, HALF], F32) for h in range(2)]
+        xg = sb("xg", [P, 4, J], F32)
         for i in range(4):
-            for j0, w in zip(starts, CHUNKS) if i == 3 else ((0, HALF), (HALF, HALF)):
-                gather(xg[j0 // HALF][:, i, j0 % HALF : j0 % HALF + w], i, j0, w)
+            for j0, w in zip(starts, CHUNKS) if i == 3 else ((0, J),):
+                gather(xg[:, i, j0 : j0 + w], i, j0, w)
         wa = sb("wa", [P, R], I32)
         wd = sb("wd", [P, N], I32)
 
@@ -208,20 +208,33 @@ def tile_list_htabg_mul_noneP_kernel(
         for c, w in enumerate(CHUNKS):
             j0 = starts[c]
             x_bf = sb(f"x_bf{c}", [P, w, 4], BF16)
-            weave_lines(nc.scalar.copy, x_bf[:], xg[j0 // HALF][:, :, j0 % HALF : j0 % HALF + w])
+            weave_lines(nc.scalar.copy, x_bf[:], xg[:, :, j0 : j0 + w])
             if c == 0:
                 deal(wa, wa_raw)
             x_codes = sb(f"x_codes{c}", [P, w], U32)
             x_sc = sb(f"x_sc{c}", [P, w], U8)
             nc.vector.quantize_mx(out=x_codes[:].bitcast(FP8X4), scales=x_sc[:], in_=x_bf[:].rearrange("p n t -> p (n t)"))
             xq.append((x_codes, x_sc))
-            if c == 1:
+            if c == 0:
                 deal(wd, wd_raw)
 
         ys = []
+
+        def finish(c):
+            j0, w = starts[c], CHUNKS[c]
+            y, y_bf = ys[c]
+            if c not in SCALAR_ROUNDS:
+                weave_lines(nc.vector.tensor_copy, y_bf[:], y[:])
+            nc.vector.quantize_mx(
+                out=y_codes[:, j0 : j0 + w].bitcast(FP8X4), scales=y_sc[:, j0 : j0 + w], in_=y_bf[:].rearrange("p n t -> p (n t)")
+            )
+            if c in CODE_STORES:
+                first = CODE_STORES[c]
+                nc.sync.dma_start(out_words[:, first : j0 + w], y_codes[:, first : j0 + w].bitcast(I32))
+
         for c, w in enumerate(CHUNKS):
             j0 = starts[c]
-            h_bf = sb(f"h_bf{c}", [P, w, 4], BF16)
+            h_bf = sb(f"h_bf{c}", [P, w, 4], BF16, tag=f"x_bf{c + 1}")
             for n0 in range(0, w, BLK):
                 bank = project("bank_a", wa, planes[:, J:ROW], *xq[c], n0)
                 nc.vector.tensor_tensor(
@@ -230,33 +243,20 @@ def tile_list_htabg_mul_noneP_kernel(
             h_codes = sb(f"h_codes{c}", [P, w], U32)
             h_sc = sb(f"h_sc{c}", [P, w], U8)
             nc.vector.quantize_mx(out=h_codes[:].bitcast(FP8X4), scales=h_sc[:], in_=h_bf[:].rearrange("p n t -> p (n t)"))
-            if c != 1:
-                y_wide = sb(f"y{c}", [P, 4, 2 * w if c == 0 else w], F32)
-            y = y_wide[:, :, w : 2 * w] if c == 1 else y_wide[:, :, 0:w]
+            y = sb(f"y{c}", [P, 4, w], F32)
             y_bf = sb(f"y_bf{c}", [P, w, 4], BF16)
             for n0 in range(0, w, BLK):
                 bank = project("bank_y", wd, planes[:, ROW + J : 2 * ROW], h_codes, h_sc, n0)
                 nc.scalar.copy(y[:, :, n0 : n0 + BLK], bank[:])
                 if c in SCALAR_ROUNDS:
                     weave(nc.scalar.copy, y_bf[:, n0 : n0 + BLK, :], bank[:])
-            if c == 1:
-                nc.sync.dma_start(out_rows[:, :, 0 : 2 * w], y_wide[:])
-            elif c > 1:
-                nc.sync.dma_start(out_rows[:, :, j0 : j0 + w], y)
+            nc.sync.dma_start(out_rows[:, :, j0 : j0 + w], y[:])
             ys.append((y, y_bf))
+            if c >= LAG:
+                finish(c - LAG)
 
-        stored = 0
-        for c, w in enumerate(CHUNKS):
-            j0 = starts[c]
-            y, y_bf = ys[c]
-            if c not in SCALAR_ROUNDS:
-                weave_lines(nc.vector.tensor_copy, y_bf[:], y)
-            nc.vector.quantize_mx(
-                out=y_codes[:, j0 : j0 + w].bitcast(FP8X4), scales=y_sc[:, j0 : j0 + w], in_=y_bf[:].rearrange("p n t -> p (n t)")
-            )
-            if c in CODE_STORES:
-                nc.sync.dma_start(out_words[:, stored : j0 + w], y_codes[:, stored : j0 + w].bitcast(I32))
-                stored = j0 + w
+        for c in range(len(CHUNKS) - LAG, len(CHUNKS)):
+            finish(c)
         for q in range(4):
             queue = nc.sync if q % 2 == 0 else nc.scalar
             queue.dma_start(out_2[0, 4 * q : 4 * q + 4, :].bitcast(I32), y_sc[32 * q : 32 * q + 4, :].bitcast(I32))

@@ -21,8 +21,8 @@ BLK = 128
 ROW = J + R
 HALF = 512
 CHUNKS = (256, 256, 256, 128, 128)
-SCALAR_ROUNDS = (0, 1)
-CODE_STORES = {0: 0, 1: 256, 2: 512, 4: 768}
+SCALAR_ROUNDS = (0,)
+CODE_STORES = {1: 0, 2: 512, 4: 768}
 LAG = 1
 
 
@@ -58,10 +58,10 @@ def tile_list_htabg_mul_noneP_kernel(
         nc.vector.memset(warm[:, 0:1], 0.0)
         nc.scalar.copy(warm[:, 1:2], warm[:, 0:1])
 
-        nc.sync.dma_start(idx[:], offs)
-        nc.sync.dma_start(tabs[0:32, :].bitcast(I32), tab_scales.rearrange("a s t -> s a t").bitcast(I32))
         nc.sync.dma_start(wsc_raw[0:32:2, :].bitcast(I32), wa_scales[0].bitcast(I32))
         nc.sync.dma_start(wsc_raw[1:32:2, :].bitcast(I32), wd_scales[0].bitcast(I32))
+        nc.sync.dma_start(idx[:], offs)
+        nc.sync.dma_start(tabs[0:32, :].bitcast(I32), tab_scales.rearrange("a s t -> s a t").bitcast(I32))
         nc.sync.dma_start(idx2[:], offs2)
         nc.sync.dma_start(wrows[0:64, :], wgt2[0:P:16, :].rearrange("g (c e) -> g c e", e=BLK))
         nc.sync.dma_start(tabw[:], tab_words[0].rearrange("p n i -> p (n i)").bitcast(I32))
@@ -95,10 +95,10 @@ def tile_list_htabg_mul_noneP_kernel(
         gs = sb("gs", [P, J], U8, tag="x0")
         gw = sb("gw", [P, J], U32, tag="x1")
         rows = sb("rows", [P, ROW], U8)
-        nc.vector.tensor_copy(gs[:], tabs[:].indirect(idx[:]))
         nc.vector.tensor_copy(
             rows[:, J:ROW].rearrange("p (t m) -> p t m", t=4), wsc_raw[:].rearrange("p (m t) -> p t m", t=4)
         )
+        nc.vector.tensor_copy(gs[:], tabs[:].indirect(idx[:]))
         nc.vector.tensor_copy(rows[:, 0:J].bitcast(I32), gs[:].bitcast(I32))
         for q in range(4):
             nc.scalar.dma_start(

@@ -22,8 +22,6 @@ ROW = J + R
 HALF = 512
 CHUNKS = (256, 256, 256, 128, 128)
 SCALAR_ROUNDS = (0,)
-CODE_STORES = {1: 0, 2: 512, 4: 768}
-LAG = 1
 
 
 def tile_list_htabg_mul_noneP_kernel(
@@ -204,59 +202,79 @@ def tile_list_htabg_mul_noneP_kernel(
                 )
             return bank
 
-        xq = []
-        for c, w in enumerate(CHUNKS):
-            j0 = starts[c]
+        xq, hq, ys = {}, {}, {}
+        y_bf = sb("y_bf", [P, J, 4], BF16)
+
+        def round_x(c):
+            j0, w = starts[c], CHUNKS[c]
             x_bf = sb(f"x_bf{c}", [P, w, 4], BF16)
             weave_lines(nc.scalar.copy, x_bf[:], xg[:, :, j0 : j0 + w])
-            if c == 0:
-                deal(wa, wa_raw)
-            x_codes = sb(f"x_codes{c}", [P, w], U32)
-            x_sc = sb(f"x_sc{c}", [P, w], U8)
-            nc.vector.quantize_mx(out=x_codes[:].bitcast(FP8X4), scales=x_sc[:], in_=x_bf[:].rearrange("p n t -> p (n t)"))
-            xq.append((x_codes, x_sc))
-            if c == 0:
-                deal(wd, wd_raw)
+            xq[c] = (x_bf, sb(f"x_codes{c}", [P, w], U32), sb(f"x_sc{c}", [P, w], U8))
 
-        ys = []
+        def quant(bf, codes, sc):
+            nc.vector.quantize_mx(out=codes.bitcast(FP8X4), scales=sc, in_=bf.rearrange("p n t -> p (n t)"))
 
-        def finish(c):
+        def quant_x(c):
+            round_x(c)
+            quant(xq[c][0][:], xq[c][1][:], xq[c][2][:])
+
+        def make_h(c, n0):
             j0, w = starts[c], CHUNKS[c]
-            y, y_bf = ys[c]
-            if c not in SCALAR_ROUNDS:
-                weave_lines(nc.vector.tensor_copy, y_bf[:], y[:])
-            nc.vector.quantize_mx(
-                out=y_codes[:, j0 : j0 + w].bitcast(FP8X4), scales=y_sc[:, j0 : j0 + w], in_=y_bf[:].rearrange("p n t -> p (n t)")
+            if n0 == 0:
+                h_bf = sb(f"h_bf{c}", [P, w, 4], BF16, tag=f"x_bf{c + 1}")
+                hq[c] = (h_bf, sb(f"h_codes{c}", [P, w], U32), sb(f"h_sc{c}", [P, w], U8))
+            bank = project("bank_a", wa, planes[:, J:ROW], xq[c][1], xq[c][2], n0)
+            nc.vector.tensor_tensor(
+                hq[c][0][:, n0 : n0 + BLK, :], bank[:].rearrange("p t n -> p n t"), yb[(j0 + n0) // BLK][:], MULT
             )
-            if c in CODE_STORES:
-                first = CODE_STORES[c]
-                nc.sync.dma_start(out_words[:, first : j0 + w], y_codes[:, first : j0 + w].bitcast(I32))
 
-        for c, w in enumerate(CHUNKS):
-            j0 = starts[c]
-            h_bf = sb(f"h_bf{c}", [P, w, 4], BF16, tag=f"x_bf{c + 1}")
-            for n0 in range(0, w, BLK):
-                bank = project("bank_a", wa, planes[:, J:ROW], *xq[c], n0)
-                nc.vector.tensor_tensor(
-                    h_bf[:, n0 : n0 + BLK, :], bank[:].rearrange("p t n -> p n t"), yb[(j0 + n0) // BLK][:], MULT
-                )
-            h_codes = sb(f"h_codes{c}", [P, w], U32)
-            h_sc = sb(f"h_sc{c}", [P, w], U8)
-            nc.vector.quantize_mx(out=h_codes[:].bitcast(FP8X4), scales=h_sc[:], in_=h_bf[:].rearrange("p n t -> p (n t)"))
-            y = sb(f"y{c}", [P, 4, w], F32)
-            y_bf = sb(f"y_bf{c}", [P, w, 4], BF16)
-            for n0 in range(0, w, BLK):
-                bank = project("bank_y", wd, planes[:, ROW + J : 2 * ROW], h_codes, h_sc, n0)
-                nc.scalar.copy(y[:, :, n0 : n0 + BLK], bank[:])
-                if c in SCALAR_ROUNDS:
-                    weave(nc.scalar.copy, y_bf[:, n0 : n0 + BLK, :], bank[:])
-            nc.sync.dma_start(out_rows[:, :, j0 : j0 + w], y[:])
-            ys.append((y, y_bf))
-            if c >= LAG:
-                finish(c - LAG)
+        def quant_h(c):
+            j0, w = starts[c], CHUNKS[c]
+            quant(hq[c][0][:], hq[c][1][:], hq[c][2][:])
+            ys[c] = sb(f"y{c}", [P, 4, w], F32)
+            banks = [project("bank_y", wd, planes[:, ROW + J : 2 * ROW], hq[c][1], hq[c][2], n0) for n0 in range(0, w, BLK)]
+            for b, bank in enumerate(banks):
+                nc.scalar.copy(ys[c][:, :, BLK * b : BLK * (b + 1)], bank[:])
+            nc.sync.dma_start(out_rows[:, :, j0 : j0 + w], ys[c][:])
+            if c in SCALAR_ROUNDS:
+                for b, bank in enumerate(banks):
+                    weave(nc.scalar.copy, y_bf[:, j0 + BLK * b : j0 + BLK * (b + 1), :], bank[:])
 
-        for c in range(len(CHUNKS) - LAG, len(CHUNKS)):
-            finish(c)
+        def round_y(c):
+            j0, w = starts[c], CHUNKS[c]
+            weave_lines(nc.vector.tensor_copy, y_bf[:, j0 : j0 + w, :], ys[c][:])
+
+        def quant_y(j0, j1):
+            quant(y_bf[:, j0:j1, :], y_codes[:, j0:j1], y_sc[:, j0:j1])
+            nc.sync.dma_start(out_words[:, j0:j1], y_codes[:, j0:j1].bitcast(I32))
+
+        deal(wa, wa_raw)
+        quant_x(0)
+        deal(wd, wd_raw)
+        quant_x(1)
+        make_h(0, 0)
+        make_h(0, BLK)
+        quant_x(2)
+        quant_h(0)
+        make_h(1, 0)
+        make_h(1, BLK)
+        quant_x(3)
+        quant_h(1)
+        quant_x(4)
+        make_h(2, 0)
+        make_h(2, BLK)
+        make_h(3, 0)
+        quant_h(2)
+        make_h(4, 0)
+        quant_h(3)
+        quant_y(0, 256)
+        quant_h(4)
+        round_y(1)
+        round_y(2)
+        round_y(3)
+        quant_y(256, 768)
+        round_y(4)
+        quant_y(768, J)
         for q in range(4):
             queue = nc.sync if q % 2 == 0 else nc.scalar
             queue.dma_start(out_2[0, 4 * q : 4 * q + 4, :].bitcast(I32), y_sc[32 * q : 32 * q + 4, :].bitcast(I32))

@@ -18,10 +18,10 @@ MULT = mybir.AluOpType.mult
 
 P = 128
 BLK = 128
-ROW = J + R
 HALF = 512
 CHUNKS = (256, 256, 256, 128, 128)
 SCALAR_ROUNDS = (0,)
+WB_SPLIT = 80
 
 
 def tile_list_htabg_mul_noneP_kernel(
@@ -39,9 +39,9 @@ def tile_list_htabg_mul_noneP_kernel(
         idx = keep.tile([P, J // 16], U16, name="idx")
         idx2 = keep.tile([P, J // 16], U16, name="idx2")
         tabw = sb("tabw", [P, T], I32)
-        tabs = sb("tabs", [P, T], U8)
+        tabs = sb("tabs", [P, T], U8, tag="x3")
         wsc_raw = sb("wsc_raw", [P, R], U8)
-        planes = sb("planes", [P, 2 * ROW], U8)
+        planes = sb("planes", [P, 2 * J], U8)
 
         for rows in (slice(32, 64), slice(64, P)):
             nc.vector.memset(tabs[rows, :].bitcast(I32), 0)
@@ -74,8 +74,8 @@ def tile_list_htabg_mul_noneP_kernel(
             xw.append(sb(f"xw{i}", [P, T], F32, tag=f"x{i}"))
             nc.sync.dma_start(xw[i][:], xplanes[i])
 
+        load_x(0)
         load_wb(0)
-        load_wb(1)
 
         turned = psum.tile([P, 4, BLK], F32, name="bank_a", bufs=4)
         nc.tensor.transpose(turned[:, 0, :], wrows[:], ident[:])
@@ -90,31 +90,32 @@ def tile_list_htabg_mul_noneP_kernel(
                 nc.tensor.transpose(back[:, c, :], spread[:, 4 * h + c].rearrange("e g s -> e (g s)"), ident[:])
             nc.scalar.copy(wgt[:, HALF * h : HALF * (h + 1)], back[:].rearrange("p c e -> p (c e)"))
 
-        gs = sb("gs", [P, J], U8, tag="x0")
+        gs = sb("gs", [P, J], U8)
         gw = sb("gw", [P, J], U32, tag="x1")
-        rows = sb("rows", [P, ROW], U8)
-        nc.vector.tensor_copy(
-            rows[:, J:ROW].rearrange("p (t m) -> p t m", t=4), wsc_raw[:].rearrange("p (m t) -> p t m", t=4)
-        )
+        wsc = sb("wsc", [P, R], U8)
+        nc.vector.tensor_copy(wsc[:].rearrange("p (t m) -> p t m", t=4), wsc_raw[:].rearrange("p (m t) -> p t m", t=4))
+
+        def move_rows(queue, dst, src):
+            for q in (0, 2, 1, 3):
+                queue.dma_start(
+                    dst[32 * q : 32 * q + 4, :].bitcast(I32).rearrange("r (a j) -> r a j", a=2),
+                    src[8 * q : 8 * q + 8, :].bitcast(I32),
+                )
+
         nc.vector.tensor_copy(gs[:], tabs[:].indirect(idx[:]))
-        nc.vector.tensor_copy(rows[:, 0:J].bitcast(I32), gs[:].bitcast(I32))
-        for q in range(4):
-            nc.scalar.dma_start(
-                planes[32 * q : 32 * q + 4, :].bitcast(I32).rearrange("r (a j) -> r a j", a=2),
-                rows[8 * q : 8 * q + 8, :].bitcast(I32),
-            )
+        move_rows(nc.sync, planes, gs)
+        load_wb(1)
         nc.vector.tensor_copy(gw[:], tabw[:].bitcast(U32).indirect(idx[:]))
         parted = sb("parted", [P, 4 * J], U8)
         nc.vector.tensor_copy(
             parted[:].bitcast(U16).rearrange("p (d j) -> p d j", d=2),
             gw[:].bitcast(U16).rearrange("p (j d) -> p d j", d=2),
         )
-        load_x(0)
         load_x(1)
 
         wb_codes, wb_sc, wb_bf = [], [], []
         for a in range(2):
-            wb_bf.append(sb(f"wb_bf{a}", [P, 4, BLK, 4], BF16, tag=("wa_raw", "wd_raw")[a]))
+            wb_bf.append(sb(f"wb_bf{a}", [P, 4, BLK, 4], BF16))
             wb_codes.append(sb(f"wb_codes{a}", [P, R], U32))
             wb_sc.append(sb(f"wb_sc{a}", [P, R], U8))
 
@@ -131,38 +132,38 @@ def tile_list_htabg_mul_noneP_kernel(
                 in_=wb_bf[a][:, t0:t1].rearrange("p t m i -> p (t m i)"),
             )
 
+        def gather(dst, i, j0, w):
+            nc.vector.tensor_tensor(dst, xw[i][:].indirect(idx2[:, j0 // 16 : (j0 + w) // 16]), wgt[:, j0 : j0 + w], MULT)
+
+        xg = sb("xg", [P, 4, J], F32)
+        gather(xg[:, 0, :], 0, 0, J)
         round_wb(nc.scalar.copy, 0, 0, BLK)
-        round_wb(nc.vector.tensor_copy, 1, 0, BLK // 2)
         quant_wb(0, 0, 4)
-        round_wb(nc.scalar.copy, 1, BLK // 2, BLK)
+        round_wb(nc.vector.tensor_copy, 1, 0, WB_SPLIT)
+        round_wb(nc.scalar.copy, 1, WB_SPLIT, BLK)
         quant_wb(1, 0, 4)
 
         load_x(2)
         load_x(3)
-        wa_raw = sb("wa_raw", [P, R], I32)
-        wd_raw = sb("wd_raw", [P, N], I32)
-        nc.sync.dma_start(wa_raw[:], wa_words[0].rearrange("p n i -> p (n i)").bitcast(I32))
-        nc.sync.dma_start(wd_raw[:], wd_words[0].rearrange("p n i -> p (n i)").bitcast(I32))
 
+        banks_b = [psum.tile([P, 4, BLK], F32, name=("bank_a", "bank_y")[b // 4], bufs=4) for b in range(J // BLK)]
         yb = []
-        for b in range(J // BLK):
-            bank = psum.tile([P, 4, BLK], F32, name=("bank_a", "bank_y")[b // 4], bufs=4)
-            for a in range(2):
+        for b, bank in enumerate(banks_b):
+            order = (0, 1) if b < 4 else (1, 0)
+            for a in order:
                 for t in range(4):
                     nc.tensor.matmul_mx(
                         out=bank[:, t, :],
                         lhsT=wb_codes[a][:, BLK * t : BLK * (t + 1)].bitcast(FP8X4),
                         lhsT_scale=wb_sc[a][:, BLK * t : BLK * (t + 1)],
                         rhs=parted[:, 2 * (J * a + BLK * b) : 2 * (J * a + BLK * (b + 1))].bitcast(FP4X4),
-                        rhs_scale=planes[:, ROW * a + BLK * b : ROW * a + BLK * (b + 1)],
-                        start=(a == 0 and t == 0),
-                        stop=(a == 1 and t == 3),
+                        rhs_scale=planes[:, J * a + BLK * b : J * a + BLK * (b + 1)],
+                        start=(a == order[0] and t == 0),
+                        stop=(a == order[1] and t == 3),
                     )
-            yb.append(sb(f"yb{b}", [P, BLK, 4], F32))
-            nc.scalar.copy(yb[b][:], bank[:].rearrange("p t n -> p n t"))
-
-        def gather(dst, i, j0, w):
-            nc.vector.tensor_tensor(dst, xw[i][:].indirect(idx2[:, j0 // 16 : (j0 + w) // 16]), wgt[:, j0 : j0 + w], MULT)
+                if a == order[1]:
+                    yb.append(sb(f"yb{b}", [P, BLK, 4], F32))
+                    nc.scalar.copy(yb[b][:], bank[:].rearrange("p t n -> p n t"))
 
         def weave(copy, dst, src):
             copy(dst, src.rearrange("p t n -> p n t"))
@@ -170,12 +171,17 @@ def tile_list_htabg_mul_noneP_kernel(
         def weave_lines(copy, dst, src):
             copy(dst.rearrange("p (c e) t -> p c t e", e=4), src.rearrange("p t (c e) -> p c t e", e=4))
 
-        xg = sb("xg", [P, 4, J], F32)
-        for i in range(4):
-            for j0, w in zip(starts, CHUNKS) if i == 3 else ((0, J),):
-                gather(xg[:, i, j0 : j0 + w], i, j0, w)
+        for i in (1, 2):
+            gather(xg[:, i, :], i, 0, J)
+        for c in (0, 1):
+            gather(xg[:, 3, starts[c] : starts[c] + CHUNKS[c]], 3, starts[c], CHUNKS[c])
+        wa_raw = sb("wa_raw", [P, R], I32, tag="x0")
+        wd_raw = sb("wd_raw", [P, N], I32, tag="x1")
+        nc.sync.dma_start(wa_raw[:], wa_words[0].rearrange("p n i -> p (n i)").bitcast(I32))
+        nc.sync.dma_start(wd_raw[:], wd_words[0].rearrange("p n i -> p (n i)").bitcast(I32))
+        wplanes = planes[:, 0 : 2 * R]
+        move_rows(nc.sync, wplanes, wsc)
         wa = sb("wa", [P, R], I32)
-        wd = sb("wd", [P, N], I32)
 
         def deal(dst, raw):
             nc.vector.tensor_copy(
@@ -207,8 +213,11 @@ def tile_list_htabg_mul_noneP_kernel(
 
         def round_x(c):
             j0, w = starts[c], CHUNKS[c]
-            x_bf = sb(f"x_bf{c}", [P, w, 4], BF16)
-            weave_lines(nc.scalar.copy, x_bf[:], xg[:, :, j0 : j0 + w])
+            if c == 0:
+                x_bf = xg[:, 3, HALF:J].bitcast(BF16).rearrange("p (n t) -> p n t", t=4)
+            else:
+                x_bf = sb(f"x_bf{c}", [P, w, 4], BF16)[:]
+            weave_lines(nc.scalar.copy, x_bf, xg[:, :, j0 : j0 + w])
             xq[c] = (x_bf, sb(f"x_codes{c}", [P, w], U32), sb(f"x_sc{c}", [P, w], U8))
 
         def quant(bf, codes, sc):
@@ -216,14 +225,14 @@ def tile_list_htabg_mul_noneP_kernel(
 
         def quant_x(c):
             round_x(c)
-            quant(xq[c][0][:], xq[c][1][:], xq[c][2][:])
+            quant(xq[c][0], xq[c][1][:], xq[c][2][:])
 
         def make_h(c, n0):
             j0, w = starts[c], CHUNKS[c]
             if n0 == 0:
-                h_bf = sb(f"h_bf{c}", [P, w, 4], BF16, tag=f"x_bf{c + 1}")
+                h_bf = sb(f"h_bf{c}", [P, w, 4], BF16, tag=f"x_bf{c + 1}" if c else None)
                 hq[c] = (h_bf, sb(f"h_codes{c}", [P, w], U32), sb(f"h_sc{c}", [P, w], U8))
-            bank = project("bank_a", wa, planes[:, J:ROW], xq[c][1], xq[c][2], n0)
+            bank = project("bank_a", wa, wplanes[:, 0:R], xq[c][1], xq[c][2], n0)
             nc.vector.tensor_tensor(
                 hq[c][0][:, n0 : n0 + BLK, :], bank[:].rearrange("p t n -> p n t"), yb[(j0 + n0) // BLK][:], MULT
             )
@@ -232,7 +241,7 @@ def tile_list_htabg_mul_noneP_kernel(
             j0, w = starts[c], CHUNKS[c]
             quant(hq[c][0][:], hq[c][1][:], hq[c][2][:])
             ys[c] = sb(f"y{c}", [P, 4, w], F32)
-            banks = [project("bank_y", wd, planes[:, ROW + J : 2 * ROW], hq[c][1], hq[c][2], n0) for n0 in range(0, w, BLK)]
+            banks = [project("bank_y", wd, wplanes[:, R : 2 * R], hq[c][1], hq[c][2], n0) for n0 in range(0, w, BLK)]
             for b, bank in enumerate(banks):
                 nc.scalar.copy(ys[c][:, :, BLK * b : BLK * (b + 1)], bank[:])
             nc.sync.dma_start(out_rows[:, :, j0 : j0 + w], ys[c][:])
@@ -250,12 +259,14 @@ def tile_list_htabg_mul_noneP_kernel(
 
         deal(wa, wa_raw)
         quant_x(0)
-        deal(wd, wd_raw)
-        quant_x(1)
+        gather(xg[:, 3, HALF:J], 3, HALF, HALF)
         make_h(0, 0)
         make_h(0, BLK)
-        quant_x(2)
+        quant_x(1)
+        wd = sb("wd", [P, N], I32, tag="x_bf1")
+        deal(wd, wd_raw)
         quant_h(0)
+        quant_x(2)
         make_h(1, 0)
         make_h(1, BLK)
         quant_x(3)

@@ -20,8 +20,8 @@ P = 128
 BLK = 128
 HALF = 512
 CHUNKS = (256, 256, 256, 128, 128)
-SCALAR_ROUNDS = (0,)
-WB_SPLIT = 80
+SCALAR_ROUNDS = (0, 4)
+WB_SPLIT = 64
 
 
 def tile_list_htabg_mul_noneP_kernel(
@@ -103,7 +103,7 @@ def tile_list_htabg_mul_noneP_kernel(
                 )
 
         nc.vector.tensor_copy(gs[:], tabs[:].indirect(idx[:]))
-        move_rows(nc.sync, planes, gs)
+        move_rows(nc.scalar, planes, gs)
         load_wb(1)
         nc.vector.tensor_copy(gw[:], tabw[:].bitcast(U32).indirect(idx[:]))
         parted = sb("parted", [P, 4 * J], U8)
@@ -175,10 +175,10 @@ def tile_list_htabg_mul_noneP_kernel(
             gather(xg[:, i, :], i, 0, J)
         for c in (0, 1):
             gather(xg[:, 3, starts[c] : starts[c] + CHUNKS[c]], 3, starts[c], CHUNKS[c])
-        wa_raw = sb("wa_raw", [P, R], I32, tag="x0")
-        wd_raw = sb("wd_raw", [P, N], I32, tag="x1")
-        nc.sync.dma_start(wa_raw[:], wa_words[0].rearrange("p n i -> p (n i)").bitcast(I32))
-        nc.sync.dma_start(wd_raw[:], wd_words[0].rearrange("p n i -> p (n i)").bitcast(I32))
+        w_raw = sb("w_raw", [P, R + N], I32, tag="x1")
+        wa_raw, wd_raw = w_raw[:, 0:R], w_raw[:, R : R + N]
+        nc.sync.dma_start(wa_raw, wa_words[0].rearrange("p n i -> p (n i)").bitcast(I32))
+        nc.sync.dma_start(wd_raw, wd_words[0].rearrange("p n i -> p (n i)").bitcast(I32))
         wplanes = planes[:, 0 : 2 * R]
         move_rows(nc.sync, wplanes, wsc)
         wa = sb("wa", [P, R], I32)
@@ -186,7 +186,7 @@ def tile_list_htabg_mul_noneP_kernel(
         def deal(dst, raw):
             nc.vector.tensor_copy(
                 dst[:].rearrange("p (t c e) -> p c t e", t=4, e=4),
-                raw[:].rearrange("p (c e t) -> p c t e", t=4, e=4),
+                raw.rearrange("p (c e t) -> p c t e", t=4, e=4),
             )
 
         y_sc = sb("y_sc", [P, J], U8)
@@ -240,21 +240,26 @@ def tile_list_htabg_mul_noneP_kernel(
         def quant_h(c):
             j0, w = starts[c], CHUNKS[c]
             quant(hq[c][0][:], hq[c][1][:], hq[c][2][:])
-            ys[c] = sb(f"y{c}", [P, 4, w], F32)
+            if c < 4:
+                ys[c] = sb(f"y{c}", [P, 4, 2 * BLK], F32)
+            y = ys[min(c, 3)][:, :, j0 % 256 : j0 % 256 + w]
             banks = [project("bank_y", wd, wplanes[:, R : 2 * R], hq[c][1], hq[c][2], n0) for n0 in range(0, w, BLK)]
             for b, bank in enumerate(banks):
-                nc.scalar.copy(ys[c][:, :, BLK * b : BLK * (b + 1)], bank[:])
-            nc.sync.dma_start(out_rows[:, :, j0 : j0 + w], ys[c][:])
+                nc.scalar.copy(y[:, :, BLK * b : BLK * (b + 1)], bank[:])
+            if c != 3:
+                nc.sync.dma_start(out_rows[:, :, j0 + w - 256 : j0 + w], ys[min(c, 3)][:])
             if c in SCALAR_ROUNDS:
                 for b, bank in enumerate(banks):
                     weave(nc.scalar.copy, y_bf[:, j0 + BLK * b : j0 + BLK * (b + 1), :], bank[:])
 
         def round_y(c):
             j0, w = starts[c], CHUNKS[c]
-            weave_lines(nc.vector.tensor_copy, y_bf[:, j0 : j0 + w, :], ys[c][:])
+            weave_lines(nc.vector.tensor_copy, y_bf[:, j0 : j0 + w, :], ys[c][:, :, 0:w])
 
         def quant_y(j0, j1):
             quant(y_bf[:, j0:j1, :], y_codes[:, j0:j1], y_sc[:, j0:j1])
+
+        def store_codes(j0, j1):
             nc.sync.dma_start(out_words[:, j0:j1], y_codes[:, j0:j1].bitcast(I32))
 
         deal(wa, wa_raw)
@@ -271,21 +276,22 @@ def tile_list_htabg_mul_noneP_kernel(
         make_h(1, BLK)
         quant_x(3)
         quant_h(1)
-        quant_x(4)
         make_h(2, 0)
         make_h(2, BLK)
-        make_h(3, 0)
+        quant_x(4)
         quant_h(2)
+        make_h(3, 0)
         make_h(4, 0)
         quant_h(3)
         quant_y(0, 256)
+        store_codes(0, 256)
         quant_h(4)
         round_y(1)
         round_y(2)
         round_y(3)
         quant_y(256, 768)
-        round_y(4)
+        store_codes(256, 768)
         quant_y(768, J)
-        for q in range(4):
-            queue = nc.sync if q % 2 == 0 else nc.scalar
-            queue.dma_start(out_2[0, 4 * q : 4 * q + 4, :].bitcast(I32), y_sc[32 * q : 32 * q + 4, :].bitcast(I32))
+        store_codes(768, J)
+        for q in (0, 2, 1, 3):
+            nc.scalar.dma_start(out_2[0, 4 * q : 4 * q + 4, :].bitcast(I32), y_sc[32 * q : 32 * q + 4, :].bitcast(I32))

@@ -39,7 +39,7 @@ def tile_list_htabg_mul_noneP_kernel(
         idx = keep.tile([P, J // 16], U16, name="idx")
         idx2 = keep.tile([P, J // 16], U16, name="idx2")
         tabw = sb("tabw", [P, T], I32)
-        tabs = sb("tabs", [P, T], U8, tag="x3")
+        tabs = sb("tabs", [P, T], U8, tag="x0")
         wsc_raw = sb("wsc_raw", [P, R], U8)
         planes = sb("planes", [P, 2 * J], U8)
 
@@ -74,8 +74,8 @@ def tile_list_htabg_mul_noneP_kernel(
             xw.append(sb(f"xw{i}", [P, T], F32, tag=f"x{i}"))
             nc.sync.dma_start(xw[i][:], xplanes[i])
 
-        load_x(0)
         load_wb(0)
+        load_wb(1)
 
         turned = psum.tile([P, 4, BLK], F32, name="bank_a", bufs=4)
         nc.tensor.transpose(turned[:, 0, :], wrows[:], ident[:])
@@ -104,7 +104,7 @@ def tile_list_htabg_mul_noneP_kernel(
 
         nc.vector.tensor_copy(gs[:], tabs[:].indirect(idx[:]))
         move_rows(nc.scalar, planes, gs)
-        load_wb(1)
+        load_x(0)
         nc.vector.tensor_copy(gw[:], tabw[:].bitcast(U32).indirect(idx[:]))
         parted = sb("parted", [P, 4 * J], U8)
         nc.vector.tensor_copy(
@@ -136,10 +136,9 @@ def tile_list_htabg_mul_noneP_kernel(
             nc.vector.tensor_tensor(dst, xw[i][:].indirect(idx2[:, j0 // 16 : (j0 + w) // 16]), wgt[:, j0 : j0 + w], MULT)
 
         xg = sb("xg", [P, 4, J], F32)
-        gather(xg[:, 0, :], 0, 0, J)
         round_wb(nc.scalar.copy, 0, 0, BLK)
-        quant_wb(0, 0, 4)
         round_wb(nc.vector.tensor_copy, 1, 0, WB_SPLIT)
+        quant_wb(0, 0, 4)
         round_wb(nc.scalar.copy, 1, WB_SPLIT, BLK)
         quant_wb(1, 0, 4)
 
@@ -149,7 +148,7 @@ def tile_list_htabg_mul_noneP_kernel(
         banks_b = [psum.tile([P, 4, BLK], F32, name=("bank_a", "bank_y")[b // 4], bufs=4) for b in range(J // BLK)]
         yb = []
         for b, bank in enumerate(banks_b):
-            order = (0, 1) if b < 4 else (1, 0)
+            order = (0, 1)
             for a in order:
                 for t in range(4):
                     nc.tensor.matmul_mx(
@@ -171,7 +170,7 @@ def tile_list_htabg_mul_noneP_kernel(
         def weave_lines(copy, dst, src):
             copy(dst.rearrange("p (c e) t -> p c t e", e=4), src.rearrange("p t (c e) -> p c t e", e=4))
 
-        for i in (1, 2):
+        for i in range(3):
             gather(xg[:, i, :], i, 0, J)
         for c in (0, 1):
             gather(xg[:, 3, starts[c] : starts[c] + CHUNKS[c]], 3, starts[c], CHUNKS[c])

@@ -18,10 +18,14 @@ MULT = mybir.AluOpType.mult
 
 P = 128
 BLK = 128
-HALF = 512
-CHUNKS = (256, 256, 256, 128, 128)
-SCALAR_ROUNDS = (0, 4)
-WB_SPLIT = 64
+WIDE = 2 * BLK
+HALF = J // 2
+RING = 4
+CHUNKS = (WIDE, WIDE, WIDE, BLK, BLK)
+LAST = len(CHUNKS) - 1
+SCALAR_ROUNDS = (0, LAST)
+WB_SPLIT = BLK // 2
+QUADRANTS = (0, 2, 1, 3)
 
 
 def tile_list_htabg_mul_noneP_kernel(
@@ -36,6 +40,18 @@ def tile_list_htabg_mul_noneP_kernel(
         def sb(name, shape, dtype, tag=None):
             return keep.tile(shape, dtype, name=name, tag=tag or name, align_bytes=64)
 
+        def words(dram):
+            return dram[0].rearrange("p n i -> p (n i)").bitcast(I32)
+
+        def weave(copy, dst, src):
+            copy(dst, src.rearrange("p t n -> p n t"))
+
+        def weave_lines(copy, dst, src):
+            copy(dst.rearrange("p (c e) t -> p c t e", e=4), src.rearrange("p t (c e) -> p c t e", e=4))
+
+        def quant(bf, codes, sc):
+            nc.vector.quantize_mx(out=codes.bitcast(FP8X4), scales=sc, in_=bf.rearrange("p n t -> p (n t)"))
+
         idx = keep.tile([P, J // 16], U16, name="idx")
         idx2 = keep.tile([P, J // 16], U16, name="idx2")
         tabw = sb("tabw", [P, T], I32)
@@ -48,21 +64,19 @@ def tile_list_htabg_mul_noneP_kernel(
             nc.vector.memset(wsc_raw[rows, :].bitcast(I32), 0)
         nc.vector.memset(planes[:].bitcast(I32), 0)
         wrows = sb("wrows", [P, BLK], F32)
-        nc.vector.memset(wrows[64:P, :], 0.0)
+        zero = sb("zero", [P, 1], F32)
+        nc.vector.memset(zero[:], 0.0)
+        nc.scalar.copy(wrows[64:P, :], zero[64:P, :].to_broadcast([64, BLK]))
         ident = sb("ident", [P, P], F32)
         make_identity(nc, ident[:])
 
-        warm = sb("warm", [P, 2], F32)
-        nc.vector.memset(warm[:, 0:1], 0.0)
-        nc.scalar.copy(warm[:, 1:2], warm[:, 0:1])
-
-        nc.sync.dma_start(wsc_raw[0:32:2, :].bitcast(I32), wa_scales[0].bitcast(I32))
-        nc.sync.dma_start(wsc_raw[1:32:2, :].bitcast(I32), wd_scales[0].bitcast(I32))
         nc.sync.dma_start(idx[:], offs)
         nc.sync.dma_start(tabs[0:32, :].bitcast(I32), tab_scales.rearrange("a s t -> s a t").bitcast(I32))
-        nc.sync.dma_start(idx2[:], offs2)
         nc.sync.dma_start(wrows[0:64, :], wgt2[0:P:16, :].rearrange("g (c e) -> g c e", e=BLK))
-        nc.sync.dma_start(tabw[:], tab_words[0].rearrange("p n i -> p (n i)").bitcast(I32))
+        nc.sync.dma_start(tabw[:], words(tab_words))
+        nc.sync.dma_start(idx2[:], offs2)
+        nc.sync.dma_start(wsc_raw[0:32:2, :].bitcast(I32), wa_scales[0].bitcast(I32))
+        nc.sync.dma_start(wsc_raw[1:32:2, :].bitcast(I32), wd_scales[0].bitcast(I32))
         xplanes = xT.rearrange("(p i) t -> i p t", i=4)
         wb_raw, xw = [], []
 
@@ -77,33 +91,30 @@ def tile_list_htabg_mul_noneP_kernel(
         load_wb(0)
         load_wb(1)
 
-        turned = psum.tile([P, 4, BLK], F32, name="bank_a", bufs=4)
+        turned = psum.tile([P, 4, BLK], F32, name="bank_a", bufs=RING)
         nc.tensor.transpose(turned[:, 0, :], wrows[:], ident[:])
         spread = sb("spread", [P, 8, 8, 16], F32)
         nc.scalar.copy(
             spread[:], turned[:, 0, 0:64].rearrange("e (g c) -> e c g", c=8).unsqueeze(3).to_broadcast([P, 8, 8, 16])
         )
         wgt = sb("wgt", [P, J], F32)
-        for h in range(2):
-            back = psum.tile([P, 4, BLK], F32, name="bank_a", bufs=4)
+        for half in range(2):
+            back = psum.tile([P, 4, BLK], F32, name="bank_a", bufs=RING)
             for c in range(4):
-                nc.tensor.transpose(back[:, c, :], spread[:, 4 * h + c].rearrange("e g s -> e (g s)"), ident[:])
-            nc.scalar.copy(wgt[:, HALF * h : HALF * (h + 1)], back[:].rearrange("p c e -> p (c e)"))
-
-        gs = sb("gs", [P, J], U8)
-        gw = sb("gw", [P, J], U32, tag="x1")
-        wsc = sb("wsc", [P, R], U8)
-        nc.vector.tensor_copy(wsc[:].rearrange("p (t m) -> p t m", t=4), wsc_raw[:].rearrange("p (m t) -> p t m", t=4))
+                nc.tensor.transpose(back[:, c, :], spread[:, 4 * half + c].rearrange("e g s -> e (g s)"), ident[:])
+            nc.scalar.copy(wgt[:, HALF * half : HALF * (half + 1)], back[:].rearrange("p c e -> p (c e)"))
 
         def move_rows(queue, dst, src):
-            for q in (0, 2, 1, 3):
+            for q in QUADRANTS:
                 queue.dma_start(
                     dst[32 * q : 32 * q + 4, :].bitcast(I32).rearrange("r (a j) -> r a j", a=2),
                     src[8 * q : 8 * q + 8, :].bitcast(I32),
                 )
 
+        gs = sb("gs", [P, J], U8)
+        gw = sb("gw", [P, J], U32, tag="x1")
         nc.vector.tensor_copy(gs[:], tabs[:].indirect(idx[:]))
-        move_rows(nc.scalar, planes, gs)
+        move_rows(nc.sync, planes, gs)
         load_x(0)
         nc.vector.tensor_copy(gw[:], tabw[:].bitcast(U32).indirect(idx[:]))
         parted = sb("parted", [P, 4 * J], U8)
@@ -111,45 +122,32 @@ def tile_list_htabg_mul_noneP_kernel(
             parted[:].bitcast(U16).rearrange("p (d j) -> p d j", d=2),
             gw[:].bitcast(U16).rearrange("p (j d) -> p d j", d=2),
         )
+        wsc = sb("wsc", [P, R], U8, tag="tabw")
+        nc.vector.tensor_copy(wsc[:].rearrange("p (t m) -> p t m", t=4), wsc_raw[:].rearrange("p (m t) -> p t m", t=4))
         load_x(1)
 
-        wb_codes, wb_sc, wb_bf = [], [], []
-        for a in range(2):
-            wb_bf.append(sb(f"wb_bf{a}", [P, 4, BLK, 4], BF16))
-            wb_codes.append(sb(f"wb_codes{a}", [P, R], U32))
-            wb_sc.append(sb(f"wb_sc{a}", [P, R], U8))
+        wb_bf = [sb(f"wb_bf{a}", [P, R, 4], BF16) for a in range(2)]
+        wb_codes = [sb(f"wb_codes{a}", [P, R], U32) for a in range(2)]
+        wb_sc = [sb(f"wb_sc{a}", [P, R], U8) for a in range(2)]
 
         def round_wb(copy, a, m0, m1):
             copy(
-                wb_bf[a][:, :, m0:m1, :].rearrange("p t m i -> p m i t"),
+                wb_bf[a][:].rearrange("p (t m) i -> p m i t", t=4)[:, m0:m1],
                 wb_raw[a][:, :, 4 * m0 : 4 * m1].rearrange("p i (m t) -> p m i t", t=4),
             )
 
-        def quant_wb(a, t0, t1):
-            cols = slice(BLK * t0, BLK * t1)
-            nc.vector.quantize_mx(
-                out=wb_codes[a][:, cols].bitcast(FP8X4), scales=wb_sc[a][:, cols],
-                in_=wb_bf[a][:, t0:t1].rearrange("p t m i -> p (t m i)"),
-            )
-
-        def gather(dst, i, j0, w):
-            nc.vector.tensor_tensor(dst, xw[i][:].indirect(idx2[:, j0 // 16 : (j0 + w) // 16]), wgt[:, j0 : j0 + w], MULT)
-
-        xg = sb("xg", [P, 4, J], F32)
         round_wb(nc.scalar.copy, 0, 0, BLK)
         round_wb(nc.vector.tensor_copy, 1, 0, WB_SPLIT)
-        quant_wb(0, 0, 4)
+        quant(wb_bf[0][:], wb_codes[0][:], wb_sc[0][:])
         round_wb(nc.scalar.copy, 1, WB_SPLIT, BLK)
-        quant_wb(1, 0, 4)
-
+        quant(wb_bf[1][:], wb_codes[1][:], wb_sc[1][:])
         load_x(2)
         load_x(3)
 
-        banks_b = [psum.tile([P, 4, BLK], F32, name=("bank_a", "bank_y")[b // 4], bufs=4) for b in range(J // BLK)]
         yb = []
-        for b, bank in enumerate(banks_b):
-            order = (0, 1)
-            for a in order:
+        for b in range(J // BLK):
+            bank = psum.tile([P, 4, BLK], F32, name=("bank_a", "bank_y")[b // RING], bufs=RING)
+            for a in range(2):
                 for t in range(4):
                     nc.tensor.matmul_mx(
                         out=bank[:, t, :],
@@ -157,44 +155,40 @@ def tile_list_htabg_mul_noneP_kernel(
                         lhsT_scale=wb_sc[a][:, BLK * t : BLK * (t + 1)],
                         rhs=parted[:, 2 * (J * a + BLK * b) : 2 * (J * a + BLK * (b + 1))].bitcast(FP4X4),
                         rhs_scale=planes[:, J * a + BLK * b : J * a + BLK * (b + 1)],
-                        start=(a == order[0] and t == 0),
-                        stop=(a == order[1] and t == 3),
+                        start=(a == 0 and t == 0),
+                        stop=(a == 1 and t == 3),
                     )
-                if a == order[1]:
-                    yb.append(sb(f"yb{b}", [P, BLK, 4], F32))
-                    nc.scalar.copy(yb[b][:], bank[:].rearrange("p t n -> p n t"))
+            yb.append(sb(f"yb{b}", [P, BLK, 4], F32))
+            weave(nc.scalar.copy, yb[b][:], bank[:])
 
-        def weave(copy, dst, src):
-            copy(dst, src.rearrange("p t n -> p n t"))
+        xg = sb("xg", [P, 4, J], F32)
 
-        def weave_lines(copy, dst, src):
-            copy(dst.rearrange("p (c e) t -> p c t e", e=4), src.rearrange("p t (c e) -> p c t e", e=4))
-
-        for i in range(3):
-            gather(xg[:, i, :], i, 0, J)
-        for c in (0, 1):
-            gather(xg[:, 3, starts[c] : starts[c] + CHUNKS[c]], 3, starts[c], CHUNKS[c])
-        w_raw = sb("w_raw", [P, R + N], I32, tag="x1")
-        wa_raw, wd_raw = w_raw[:, 0:R], w_raw[:, R : R + N]
-        nc.sync.dma_start(wa_raw, wa_words[0].rearrange("p n i -> p (n i)").bitcast(I32))
-        nc.sync.dma_start(wd_raw, wd_words[0].rearrange("p n i -> p (n i)").bitcast(I32))
-        wplanes = planes[:, 0 : 2 * R]
-        move_rows(nc.sync, wplanes, wsc)
-        wa = sb("wa", [P, R], I32)
-
-        def deal(dst, raw):
-            nc.vector.tensor_copy(
-                dst[:].rearrange("p (t c e) -> p c t e", t=4, e=4),
-                raw.rearrange("p (c e t) -> p c t e", t=4, e=4),
+        def gather(i, j0, w):
+            nc.vector.tensor_tensor(
+                xg[:, i, j0 : j0 + w], xw[i][:].indirect(idx2[:, j0 // 16 : (j0 + w) // 16]), wgt[:, j0 : j0 + w], MULT
             )
 
-        y_sc = sb("y_sc", [P, J], U8)
-        y_codes = sb("y_codes", [P, J], U32)
-        out_rows = out_0.rearrange("(p t) j -> p t j", t=4)
-        out_words = out_1[0].rearrange("p j i -> p (j i)").bitcast(I32)
+        for i in range(3):
+            gather(i, 0, J)
+        for c in range(2):
+            gather(3, starts[c], CHUNKS[c])
+
+        w_raw = sb("w_raw", [P, R + N], I32, tag="x1")
+        wa_raw, wd_raw = w_raw[:, 0:R], w_raw[:, R : R + N]
+        nc.sync.dma_start(wa_raw, words(wa_words))
+        nc.sync.dma_start(wd_raw, words(wd_words))
+        move_rows(nc.sync, planes[:, 0 : R + N], wsc)
+        wa_sc, wd_sc = planes[:, 0:R], planes[:, R : R + N]
+
+        def deal(name, raw):
+            dealt = sb(name, [P, R], I32)
+            nc.vector.tensor_copy(
+                dealt[:].rearrange("p (t c e) -> p c t e", t=4, e=4), raw.rearrange("p (c e t) -> p c t e", t=4, e=4)
+            )
+            return dealt
 
         def project(name, w_codes, w_sc, codes, sc, n0):
-            bank = psum.tile([P, 4, BLK], F32, name=name, bufs=4)
+            bank = psum.tile([P, 4, BLK], F32, name=name, bufs=RING)
             for t in range(4):
                 nc.tensor.matmul_mx(
                     out=bank[:, t, :],
@@ -209,88 +203,70 @@ def tile_list_htabg_mul_noneP_kernel(
 
         xq, hq, ys = {}, {}, {}
         y_bf = sb("y_bf", [P, J, 4], BF16)
+        y_sc = sb("y_sc", [P, J], U8)
+        y_codes = sb("y_codes", [P, J], U32)
+        out_rows = out_0.rearrange("(p t) j -> p t j", t=4)
+        out_words = words(out_1)
 
-        def round_x(c):
+        def quant_x(c):
             j0, w = starts[c], CHUNKS[c]
             if c == 0:
                 x_bf = xg[:, 3, HALF:J].bitcast(BF16).rearrange("p (n t) -> p n t", t=4)
             else:
                 x_bf = sb(f"x_bf{c}", [P, w, 4], BF16)[:]
             weave_lines(nc.scalar.copy, x_bf, xg[:, :, j0 : j0 + w])
-            xq[c] = (x_bf, sb(f"x_codes{c}", [P, w], U32), sb(f"x_sc{c}", [P, w], U8))
+            xq[c] = (sb(f"x_codes{c}", [P, w], U32), sb(f"x_sc{c}", [P, w], U8))
+            quant(x_bf, xq[c][0][:], xq[c][1][:])
 
-        def quant(bf, codes, sc):
-            nc.vector.quantize_mx(out=codes.bitcast(FP8X4), scales=sc, in_=bf.rearrange("p n t -> p (n t)"))
-
-        def quant_x(c):
-            round_x(c)
-            quant(xq[c][0], xq[c][1][:], xq[c][2][:])
-
-        def make_h(c, n0):
+        def make_h(c):
             j0, w = starts[c], CHUNKS[c]
-            if n0 == 0:
-                h_bf = sb(f"h_bf{c}", [P, w, 4], BF16, tag=f"x_bf{c + 1}" if c else None)
-                hq[c] = (h_bf, sb(f"h_codes{c}", [P, w], U32), sb(f"h_sc{c}", [P, w], U8))
-            bank = project("bank_a", wa, wplanes[:, 0:R], xq[c][1], xq[c][2], n0)
-            nc.vector.tensor_tensor(
-                hq[c][0][:, n0 : n0 + BLK, :], bank[:].rearrange("p t n -> p n t"), yb[(j0 + n0) // BLK][:], MULT
-            )
+            hq[c] = sb(f"h_bf{c}", [P, w, 4], BF16, tag=f"x_bf{c + 1}" if c else None)
+            for n0 in range(0, w, BLK):
+                bank = project("bank_a", wa, wa_sc, *xq[c], n0)
+                nc.vector.tensor_tensor(
+                    hq[c][:, n0 : n0 + BLK, :], bank[:].rearrange("p t n -> p n t"), yb[(j0 + n0) // BLK][:], MULT
+                )
 
-        def quant_h(c):
+        def make_y(c):
             j0, w = starts[c], CHUNKS[c]
-            quant(hq[c][0][:], hq[c][1][:], hq[c][2][:])
-            if c < 4:
-                ys[c] = sb(f"y{c}", [P, 4, 2 * BLK], F32)
-            y = ys[min(c, 3)][:, :, j0 % 256 : j0 % 256 + w]
-            banks = [project("bank_y", wd, wplanes[:, R : 2 * R], hq[c][1], hq[c][2], n0) for n0 in range(0, w, BLK)]
+            h_codes, h_sc = sb(f"h_codes{c}", [P, w], U32), sb(f"h_sc{c}", [P, w], U8)
+            quant(hq[c][:], h_codes[:], h_sc[:])
+            s, s0 = divmod(j0, WIDE)
+            if s0 == 0:
+                ys[s] = sb(f"y{s}", [P, 4, WIDE], F32)
+            banks = [project("bank_y", wd, wd_sc, h_codes, h_sc, n0) for n0 in range(0, w, BLK)]
             for b, bank in enumerate(banks):
-                nc.scalar.copy(y[:, :, BLK * b : BLK * (b + 1)], bank[:])
-            if c != 3:
-                nc.sync.dma_start(out_rows[:, :, j0 + w - 256 : j0 + w], ys[min(c, 3)][:])
+                nc.scalar.copy(ys[s][:, :, s0 + BLK * b : s0 + BLK * (b + 1)], bank[:])
+            if s0 + w == WIDE:
+                nc.sync.dma_start(out_rows[:, :, WIDE * s : WIDE * (s + 1)], ys[s][:])
             if c in SCALAR_ROUNDS:
                 for b, bank in enumerate(banks):
                     weave(nc.scalar.copy, y_bf[:, j0 + BLK * b : j0 + BLK * (b + 1), :], bank[:])
 
-        def round_y(c):
-            j0, w = starts[c], CHUNKS[c]
-            weave_lines(nc.vector.tensor_copy, y_bf[:, j0 : j0 + w, :], ys[c][:, :, 0:w])
-
-        def quant_y(j0, j1):
+        def planes_y(j0, j1):
             quant(y_bf[:, j0:j1, :], y_codes[:, j0:j1], y_sc[:, j0:j1])
-
-        def store_codes(j0, j1):
             nc.sync.dma_start(out_words[:, j0:j1], y_codes[:, j0:j1].bitcast(I32))
 
-        deal(wa, wa_raw)
+        wa = deal("wa", wa_raw)
+        wd = deal("wd", wd_raw)
         quant_x(0)
-        gather(xg[:, 3, HALF:J], 3, HALF, HALF)
-        make_h(0, 0)
-        make_h(0, BLK)
+        gather(3, HALF, HALF)
+        make_h(0)
         quant_x(1)
-        wd = sb("wd", [P, N], I32, tag="x_bf1")
-        deal(wd, wd_raw)
-        quant_h(0)
+        make_y(0)
         quant_x(2)
-        make_h(1, 0)
-        make_h(1, BLK)
-        quant_x(3)
-        quant_h(1)
-        make_h(2, 0)
-        make_h(2, BLK)
-        quant_x(4)
-        quant_h(2)
-        make_h(3, 0)
-        make_h(4, 0)
-        quant_h(3)
-        quant_y(0, 256)
-        store_codes(0, 256)
-        quant_h(4)
-        round_y(1)
-        round_y(2)
-        round_y(3)
-        quant_y(256, 768)
-        store_codes(256, 768)
-        quant_y(768, J)
-        store_codes(768, J)
-        for q in (0, 2, 1, 3):
+        for c in (1, 2):
+            make_h(c)
+            quant_x(c + 2)
+            make_y(c)
+        make_h(LAST - 1)
+        make_h(LAST)
+        make_y(LAST - 1)
+        planes_y(0, WIDE)
+        make_y(LAST)
+        for c in range(1, LAST):
+            weave_lines(nc.vector.tensor_copy, y_bf[:, starts[c] : starts[c + 1], :], ys[c][:, :, 0 : CHUNKS[c]])
+        planes_y(WIDE, starts[LAST - 1])
+        planes_y(starts[LAST - 1], J)
+        for q in QUADRANTS:
             nc.scalar.dma_start(out_2[0, 4 * q : 4 * q + 4, :].bitcast(I32), y_sc[32 * q : 32 * q + 4, :].bitcast(I32))

@@ -23,8 +23,8 @@ HALF = J // 2
 RING = 4
 CHUNKS = (WIDE, WIDE, WIDE, BLK, BLK)
 LAST = len(CHUNKS) - 1
-SCALAR_ROUNDS = (0, LAST)
-WB_SPLIT = BLK // 2
+SCALAR_ROUNDS = {0: 0, 1: 1, LAST: 7}
+WB_SPLIT = 3 * BLK // 4
 QUADRANTS = (0, 2, 1, 3)
 
 
@@ -170,8 +170,8 @@ def tile_list_htabg_mul_noneP_kernel(
 
         for i in range(3):
             gather(i, 0, J)
-        for c in range(2):
-            gather(3, starts[c], CHUNKS[c])
+        for j0, w in ((0, BLK), (BLK, BLK), (WIDE, WIDE), (HALF, WIDE)):
+            gather(3, j0, w)
 
         w_raw = sb("w_raw", [P, R + N], I32, tag="x1")
         wa_raw, wd_raw = w_raw[:, 0:R], w_raw[:, R : R + N]
@@ -180,8 +180,8 @@ def tile_list_htabg_mul_noneP_kernel(
         move_rows(nc.sync, planes[:, 0 : R + N], wsc)
         wa_sc, wd_sc = planes[:, 0:R], planes[:, R : R + N]
 
-        def deal(name, raw):
-            dealt = sb(name, [P, R], I32)
+        def deal(name, raw, tag=None):
+            dealt = sb(name, [P, R], I32, tag=tag)
             nc.vector.tensor_copy(
                 dealt[:].rearrange("p (t c e) -> p c t e", t=4, e=4), raw.rearrange("p (c e t) -> p c t e", t=4, e=4)
             )
@@ -201,7 +201,7 @@ def tile_list_htabg_mul_noneP_kernel(
                 )
             return bank
 
-        xq, hq, ys = {}, {}, {}
+        xq, hq, ys, y_banks = {}, {}, {}, []
         y_bf = sb("y_bf", [P, J, 4], BF16)
         y_sc = sb("y_sc", [P, J], U8)
         y_codes = sb("y_codes", [P, J], U32)
@@ -210,13 +210,15 @@ def tile_list_htabg_mul_noneP_kernel(
 
         def quant_x(c):
             j0, w = starts[c], CHUNKS[c]
-            if c == 0:
-                x_bf = xg[:, 3, HALF:J].bitcast(BF16).rearrange("p (n t) -> p n t", t=4)
-            else:
-                x_bf = sb(f"x_bf{c}", [P, w, 4], BF16)[:]
-            weave_lines(nc.scalar.copy, x_bf, xg[:, :, j0 : j0 + w])
             xq[c] = (sb(f"x_codes{c}", [P, w], U32), sb(f"x_sc{c}", [P, w], U8))
-            quant(x_bf, xq[c][0][:], xq[c][1][:])
+            if c == 0:
+                borrowed = xg[:, 3, J - WIDE : J].bitcast(BF16).rearrange("p (n t) -> p n t", t=4)
+                parts = ((0, BLK, sb("x_bf0", [P, BLK, 4], BF16)[:]), (BLK, WIDE, borrowed))
+            else:
+                parts = ((0, w, sb(f"x_bf{c}", [P, w, 4], BF16)[:]),)
+            for n0, n1, x_bf in parts:
+                weave_lines(nc.scalar.copy, x_bf, xg[:, :, j0 + n0 : j0 + n1])
+                quant(x_bf, xq[c][0][:, n0:n1], xq[c][1][:, n0:n1])
 
         def make_h(c):
             j0, w = starts[c], CHUNKS[c]
@@ -239,20 +241,21 @@ def tile_list_htabg_mul_noneP_kernel(
                 nc.scalar.copy(ys[s][:, :, s0 + BLK * b : s0 + BLK * (b + 1)], bank[:])
             if s0 + w == WIDE:
                 nc.sync.dma_start(out_rows[:, :, WIDE * s : WIDE * (s + 1)], ys[s][:])
+            y_banks.extend(banks)
             if c in SCALAR_ROUNDS:
-                for b, bank in enumerate(banks):
-                    weave(nc.scalar.copy, y_bf[:, j0 + BLK * b : j0 + BLK * (b + 1), :], bank[:])
+                b = SCALAR_ROUNDS[c]
+                weave(nc.scalar.copy, y_bf[:, BLK * b : BLK * (b + 1), :], y_banks[b][:])
 
         def planes_y(j0, j1):
             quant(y_bf[:, j0:j1, :], y_codes[:, j0:j1], y_sc[:, j0:j1])
             nc.sync.dma_start(out_words[:, j0:j1], y_codes[:, j0:j1].bitcast(I32))
 
         wa = deal("wa", wa_raw)
-        wd = deal("wd", wd_raw)
         quant_x(0)
-        gather(3, HALF, HALF)
+        gather(3, J - WIDE, WIDE)
         make_h(0)
         quant_x(1)
+        wd = deal("wd", wd_raw, tag="x_bf1")
         make_y(0)
         quant_x(2)
         for c in (1, 2):

@@ -24,7 +24,7 @@ RING = 4
 CHUNKS = (WIDE, WIDE, WIDE, BLK, BLK)
 LAST = len(CHUNKS) - 1
 SCALAR_ROUNDS = {0: 0, 1: 1, LAST: 7}
-WB_SPLIT = 3 * BLK // 4
+WB_SPLIT = (BLK // 4, BLK // 2)
 QUADRANTS = (0, 2, 1, 3)
 
 
@@ -122,8 +122,6 @@ def tile_list_htabg_mul_noneP_kernel(
             parted[:].bitcast(U16).rearrange("p (d j) -> p d j", d=2),
             gw[:].bitcast(U16).rearrange("p (j d) -> p d j", d=2),
         )
-        wsc = sb("wsc", [P, R], U8, tag="tabw")
-        nc.vector.tensor_copy(wsc[:].rearrange("p (t m) -> p t m", t=4), wsc_raw[:].rearrange("p (m t) -> p t m", t=4))
         load_x(1)
 
         wb_bf = [sb(f"wb_bf{a}", [P, R, 4], BF16) for a in range(2)]
@@ -136,10 +134,13 @@ def tile_list_htabg_mul_noneP_kernel(
                 wb_raw[a][:, :, 4 * m0 : 4 * m1].rearrange("p i (m t) -> p m i t", t=4),
             )
 
-        round_wb(nc.scalar.copy, 0, 0, BLK)
-        round_wb(nc.vector.tensor_copy, 1, 0, WB_SPLIT)
+        round_wb(nc.scalar.copy, 0, WB_SPLIT[0], BLK)
+        round_wb(nc.vector.tensor_copy, 0, 0, WB_SPLIT[0])
         quant(wb_bf[0][:], wb_codes[0][:], wb_sc[0][:])
-        round_wb(nc.scalar.copy, 1, WB_SPLIT, BLK)
+        round_wb(nc.scalar.copy, 1, WB_SPLIT[1], BLK)
+        round_wb(nc.vector.tensor_copy, 1, 0, WB_SPLIT[1])
+        wsc = sb("wsc", [P, R], U8, tag="wb_bf0")
+        nc.vector.tensor_copy(wsc[:].rearrange("p (t m) -> p t m", t=4), wsc_raw[:].rearrange("p (m t) -> p t m", t=4))
         quant(wb_bf[1][:], wb_codes[1][:], wb_sc[1][:])
         load_x(2)
         load_x(3)

@@ -114,8 +114,8 @@ def tile_list_htabg_mul_noneP_kernel(
         gs = sb("gs", [P, J], U8)
         gw = sb("gw", [P, J], U32, tag="x1")
         nc.vector.tensor_copy(gs[:], tabs[:].indirect(idx[:]))
-        move_rows(nc.sync, planes, gs)
         load_x(0)
+        move_rows(nc.sync, planes, gs)
         nc.vector.tensor_copy(gw[:], tabw[:].bitcast(U32).indirect(idx[:]))
         parted = sb("parted", [P, 4 * J], U8)
         nc.vector.tensor_copy(
@@ -181,12 +181,12 @@ def tile_list_htabg_mul_noneP_kernel(
         move_rows(nc.sync, planes[:, 0 : R + N], wsc)
         wa_sc, wd_sc = planes[:, 0:R], planes[:, R : R + N]
 
-        def deal(name, raw, tag=None):
-            dealt = sb(name, [P, R], I32, tag=tag)
-            nc.vector.tensor_copy(
-                dealt[:].rearrange("p (t c e) -> p c t e", t=4, e=4), raw.rearrange("p (c e t) -> p c t e", t=4, e=4)
-            )
-            return dealt
+        dealt = sb("dealt", [P, R + N], I32)
+        nc.vector.tensor_copy(
+            dealt[:].rearrange("p (w t c e) -> p w c t e", w=2, t=4, e=4),
+            w_raw[:].rearrange("p (w c e t) -> p w c t e", w=2, t=4, e=4),
+        )
+        wa, wd = dealt[:, 0:R], dealt[:, R : R + N]
 
         def project(name, w_codes, w_sc, codes, sc, n0):
             bank = psum.tile([P, 4, BLK], F32, name=name, bufs=RING)
@@ -249,14 +249,14 @@ def tile_list_htabg_mul_noneP_kernel(
 
         def planes_y(j0, j1):
             quant(y_bf[:, j0:j1, :], y_codes[:, j0:j1], y_sc[:, j0:j1])
+
+        def store_words(j0, j1):
             nc.sync.dma_start(out_words[:, j0:j1], y_codes[:, j0:j1].bitcast(I32))
 
-        wa = deal("wa", wa_raw)
         quant_x(0)
         gather(3, J - WIDE, WIDE)
         make_h(0)
         quant_x(1)
-        wd = deal("wd", wd_raw, tag="x_bf1")
         make_y(0)
         quant_x(2)
         for c in (1, 2):
@@ -267,10 +267,12 @@ def tile_list_htabg_mul_noneP_kernel(
         make_h(LAST)
         make_y(LAST - 1)
         planes_y(0, WIDE)
+        store_words(0, WIDE)
         make_y(LAST)
         for c in range(1, LAST):
             weave_lines(nc.vector.tensor_copy, y_bf[:, starts[c] : starts[c + 1], :], ys[c][:, :, 0 : CHUNKS[c]])
         planes_y(WIDE, starts[LAST - 1])
         planes_y(starts[LAST - 1], J)
+        store_words(WIDE, J)
         for q in QUADRANTS:
             nc.scalar.dma_start(out_2[0, 4 * q : 4 * q + 4, :].bitcast(I32), y_sc[32 * q : 32 * q + 4, :].bitcast(I32))

@@ -275,4 +275,4 @@ def tile_list_htabg_mul_noneP_kernel(
         planes_y(starts[LAST - 1], J)
         store_words(WIDE, J)
         for q in QUADRANTS:
-            nc.scalar.dma_start(out_2[0, 4 * q : 4 * q + 4, :].bitcast(I32), y_sc[32 * q : 32 * q + 4, :].bitcast(I32))
+            nc.sync.dma_start(out_2[0, 4 * q : 4 * q + 4, :].bitcast(I32), y_sc[32 * q : 32 * q + 4, :].bitcast(I32))

@@ -267,12 +267,11 @@ def tile_list_htabg_mul_noneP_kernel(
         make_h(LAST)
         make_y(LAST - 1)
         planes_y(0, WIDE)
-        store_words(0, WIDE)
         make_y(LAST)
         for c in range(1, LAST):
             weave_lines(nc.vector.tensor_copy, y_bf[:, starts[c] : starts[c + 1], :], ys[c][:, :, 0 : CHUNKS[c]])
         planes_y(WIDE, starts[LAST - 1])
         planes_y(starts[LAST - 1], J)
-        store_words(WIDE, J)
+        store_words(0, J)
         for q in QUADRANTS:
-            nc.sync.dma_start(out_2[0, 4 * q : 4 * q + 4, :].bitcast(I32), y_sc[32 * q : 32 * q + 4, :].bitcast(I32))
+            (nc.scalar, nc.sync)[q % 2].dma_start(out_2[0, 4 * q : 4 * q + 4, :].bitcast(I32), y_sc[32 * q : 32 * q + 4, :].bitcast(I32))

@@ -93,15 +93,15 @@ def tile_list_htabg_mul_noneP_kernel(
 
         turned = psum.tile([P, 4, BLK], F32, name="bank_a", bufs=RING)
         nc.tensor.transpose(turned[:, 0, :], wrows[:], ident[:])
-        spread = sb("spread", [P, 8, 8, 16], F32)
-        nc.scalar.copy(
-            spread[:], turned[:, 0, 0:64].rearrange("e (g c) -> e c g", c=8).unsqueeze(3).to_broadcast([P, 8, 8, 16])
-        )
+        pieces = turned[:, 0, 0:64].rearrange("e (g c) -> e c g", c=8)
+        spread = [sb(f"spread{half}", [P, 4, 8, 16], F32, tag=("spread", "wb_bf0")[half]) for half in range(2)]
+        for half in range(2):
+            nc.scalar.copy(spread[half][:], pieces[:, 4 * half : 4 * half + 4].unsqueeze(3).to_broadcast([P, 4, 8, 16]))
         wgt = sb("wgt", [P, J], F32)
         for half in range(2):
             back = psum.tile([P, 4, BLK], F32, name="bank_a", bufs=RING)
             for c in range(4):
-                nc.tensor.transpose(back[:, c, :], spread[:, 4 * half + c].rearrange("e g s -> e (g s)"), ident[:])
+                nc.tensor.transpose(back[:, c, :], spread[half][:, c].rearrange("e g s -> e (g s)"), ident[:])
             nc.scalar.copy(wgt[:, HALF * half : HALF * (half + 1)], back[:].rearrange("p c e -> p (c e)"))
 
         def move_rows(queue, dst, src):

@@ -49,6 +49,9 @@ def tile_list_htabg_mul_noneP_kernel(
         def weave_lines(copy, dst, src):
             copy(dst.rearrange("p (c e) t -> p c t e", e=4), src.rearrange("p t (c e) -> p c t e", e=4))
 
+        def weave_pairs(copy, dst, src):
+            copy(dst.rearrange("p (c e) t -> p c t e", e=2), src.rearrange("p t (c e) -> p c t e", e=2))
+
         def quant(bf, codes, sc):
             nc.vector.quantize_mx(out=codes.bitcast(FP8X4), scales=sc, in_=bf.rearrange("p n t -> p (n t)"))
 
@@ -218,7 +221,7 @@ def tile_list_htabg_mul_noneP_kernel(
             else:
                 parts = ((0, w, sb(f"x_bf{c}", [P, w, 4], BF16)[:]),)
             for n0, n1, x_bf in parts:
-                weave_lines(nc.scalar.copy, x_bf, xg[:, :, j0 + n0 : j0 + n1])
+                weave_pairs(nc.scalar.copy, x_bf, xg[:, :, j0 + n0 : j0 + n1])
                 quant(x_bf, xq[c][0][:, n0:n1], xq[c][1][:, n0:n1])
 
         def make_h(c):

@@ -148,22 +148,21 @@ def tile_list_htabg_mul_noneP_kernel(
         load_x(2)
         load_x(3)
 
-        yb = []
-        for b in range(J // BLK):
-            bank = psum.tile([P, 4, BLK], F32, name=("bank_a", "bank_y")[b // RING], bufs=RING)
-            for a in range(2):
-                for t in range(4):
+        yb = sb("yb", [P, 4, J], F32)
+        for half in range(2):
+            for t in range(4):
+                bank = psum.tile([P, HALF], F32, name=("bank_a", "bank_y")[half], bufs=RING)
+                for a in range(2):
                     nc.tensor.matmul_mx(
-                        out=bank[:, t, :],
+                        out=bank[:],
                         lhsT=wb_codes[a][:, BLK * t : BLK * (t + 1)].bitcast(FP8X4),
                         lhsT_scale=wb_sc[a][:, BLK * t : BLK * (t + 1)],
-                        rhs=parted[:, 2 * (J * a + BLK * b) : 2 * (J * a + BLK * (b + 1))].bitcast(FP4X4),
-                        rhs_scale=planes[:, J * a + BLK * b : J * a + BLK * (b + 1)],
-                        start=(a == 0 and t == 0),
-                        stop=(a == 1 and t == 3),
+                        rhs=parted[:, 2 * (J * a + HALF * half) : 2 * (J * a + HALF * (half + 1))].bitcast(FP4X4),
+                        rhs_scale=planes[:, J * a + HALF * half : J * a + HALF * (half + 1)],
+                        start=(a == 0),
+                        stop=(a == 1),
                     )
-            yb.append(sb(f"yb{b}", [P, BLK, 4], F32))
-            weave(nc.scalar.copy, yb[b][:], bank[:])
+                nc.scalar.copy(yb[:, t, HALF * half : HALF * (half + 1)], bank[:])
 
         xg = sb("xg", [P, 4, J], F32)
 
@@ -230,7 +229,10 @@ def tile_list_htabg_mul_noneP_kernel(
             for n0 in range(0, w, BLK):
                 bank = project("bank_a", wa, wa_sc, *xq[c], n0)
                 nc.vector.tensor_tensor(
-                    hq[c][:, n0 : n0 + BLK, :], bank[:].rearrange("p t n -> p n t"), yb[(j0 + n0) // BLK][:], MULT
+                    hq[c][:, n0 : n0 + BLK, :].rearrange("p (c e) t -> p c t e", e=2),
+                    bank[:].rearrange("p t (c e) -> p c t e", e=2),
+                    yb[:, :, j0 + n0 : j0 + n0 + BLK].rearrange("p t (c e) -> p c t e", e=2),
+                    MULT,
                 )
 
         def make_y(c):

@@ -43,9 +43,6 @@ def tile_list_htabg_mul_noneP_kernel(
         def words(dram):
             return dram[0].rearrange("p n i -> p (n i)").bitcast(I32)
 
-        def weave(copy, dst, src):
-            copy(dst, src.rearrange("p t n -> p n t"))
-
         def weave_lines(copy, dst, src):
             copy(dst.rearrange("p (c e) t -> p c t e", e=4), src.rearrange("p t (c e) -> p c t e", e=4))
 
@@ -183,12 +180,11 @@ def tile_list_htabg_mul_noneP_kernel(
         move_rows(nc.sync, planes[:, 0 : R + N], wsc)
         wa_sc, wd_sc = planes[:, 0:R], planes[:, R : R + N]
 
-        dealt = sb("dealt", [P, R + N], I32)
-        nc.vector.tensor_copy(
-            dealt[:].rearrange("p (w t c e) -> p w c t e", w=2, t=4, e=4),
-            w_raw[:].rearrange("p (w c e t) -> p w c t e", w=2, t=4, e=4),
-        )
-        wa, wd = dealt[:, 0:R], dealt[:, R : R + N]
+        def deal(copy, dealt, raw):
+            copy(dealt.rearrange("p (t c e) -> p c t e", t=4, e=4), raw.rearrange("p (c e t) -> p c t e", t=4, e=4))
+
+        wa = sb("wa", [P, R], I32)
+        deal(nc.vector.tensor_copy, wa[:], wa_raw)
 
         def project(name, w_codes, w_sc, codes, sc, n0):
             bank = psum.tile([P, 4, BLK], F32, name=name, bufs=RING)
@@ -211,17 +207,23 @@ def tile_list_htabg_mul_noneP_kernel(
         out_rows = out_0.rearrange("(p t) j -> p t j", t=4)
         out_words = words(out_1)
 
+        x_bf = {}
+
+        def round_x(c):
+            x_bf[c] = sb(f"x_bf{c}", [P, CHUNKS[c], 4], BF16)
+            weave_pairs(nc.scalar.copy, x_bf[c][:], xg[:, :, starts[c] : starts[c] + CHUNKS[c]])
+
         def quant_x(c):
             j0, w = starts[c], CHUNKS[c]
             xq[c] = (sb(f"x_codes{c}", [P, w], U32), sb(f"x_sc{c}", [P, w], U8))
             if c == 0:
                 borrowed = xg[:, 3, J - WIDE : J].bitcast(BF16).rearrange("p (n t) -> p n t", t=4)
                 parts = ((0, BLK, sb("x_bf0", [P, BLK, 4], BF16)[:]), (BLK, WIDE, borrowed))
+                for n0, n1, part in parts:
+                    weave_pairs(nc.scalar.copy, part, xg[:, :, j0 + n0 : j0 + n1])
+                    quant(part, xq[c][0][:, n0:n1], xq[c][1][:, n0:n1])
             else:
-                parts = ((0, w, sb(f"x_bf{c}", [P, w, 4], BF16)[:]),)
-            for n0, n1, x_bf in parts:
-                weave_pairs(nc.scalar.copy, x_bf, xg[:, :, j0 + n0 : j0 + n1])
-                quant(x_bf, xq[c][0][:, n0:n1], xq[c][1][:, n0:n1])
+                quant(x_bf[c][:], xq[c][0][:], xq[c][1][:])
 
         def make_h(c):
             j0, w = starts[c], CHUNKS[c]
@@ -250,7 +252,7 @@ def tile_list_htabg_mul_noneP_kernel(
             y_banks.extend(banks)
             if c in SCALAR_ROUNDS:
                 b = SCALAR_ROUNDS[c]
-                weave(nc.scalar.copy, y_bf[:, BLK * b : BLK * (b + 1), :], y_banks[b][:])
+                weave_pairs(nc.scalar.copy, y_bf[:, BLK * b : BLK * (b + 1), :], y_banks[b][:])
 
         def planes_y(j0, j1):
             quant(y_bf[:, j0:j1, :], y_codes[:, j0:j1], y_sc[:, j0:j1])
@@ -260,6 +262,10 @@ def tile_list_htabg_mul_noneP_kernel(
 
         quant_x(0)
         gather(3, J - WIDE, WIDE)
+        for c in range(1, len(CHUNKS)):
+            round_x(c)
+        wd = sb("wd", [P, N], U32, tag="xg")
+        deal(nc.scalar.copy, wd[:], wd_raw.bitcast(U32))
         make_h(0)
         quant_x(1)
         make_y(0)

@@ -145,7 +145,7 @@ def tile_list_htabg_mul_noneP_kernel(
         load_x(2)
         load_x(3)
 
-        yb = sb("yb", [P, 4, J], F32)
+        yb_first, yb = sb("yb_first", [P, 4, BLK], F32), sb("yb", [P, 4, J], F32)
         for half in range(2):
             for t in range(4):
                 bank = psum.tile([P, HALF], F32, name=("bank_a", "bank_y")[half], bufs=RING)
@@ -159,7 +159,11 @@ def tile_list_htabg_mul_noneP_kernel(
                         start=(a == 0),
                         stop=(a == 1),
                     )
-                nc.scalar.copy(yb[:, t, HALF * half : HALF * (half + 1)], bank[:])
+                if half == 0:
+                    nc.scalar.copy(yb_first[:, t, :], bank[:, 0:BLK])
+                    nc.scalar.copy(yb[:, t, BLK:HALF], bank[:, BLK:HALF])
+                else:
+                    nc.scalar.copy(yb[:, t, HALF:J], bank[:])
 
         xg = sb("xg", [P, 4, J], F32)
 
@@ -215,7 +219,7 @@ def tile_list_htabg_mul_noneP_kernel(
 
         def quant_x(c):
             j0, w = starts[c], CHUNKS[c]
-            xq[c] = (sb(f"x_codes{c}", [P, w], U32), sb(f"x_sc{c}", [P, w], U8))
+            xq[c] = (sb(f"x_codes{c}", [P, w], U32, tag="yb_first" if c == 2 else None), sb(f"x_sc{c}", [P, w], U8))
             if c == 0:
                 borrowed = xg[:, 3, J - WIDE : J].bitcast(BF16).rearrange("p (n t) -> p n t", t=4)
                 parts = ((0, BLK, sb("x_bf0", [P, BLK, 4], BF16)[:]), (BLK, WIDE, borrowed))
@@ -233,7 +237,7 @@ def tile_list_htabg_mul_noneP_kernel(
                 nc.vector.tensor_tensor(
                     hq[c][:, n0 : n0 + BLK, :].rearrange("p (c e) t -> p c t e", e=2),
                     bank[:].rearrange("p t (c e) -> p c t e", e=2),
-                    yb[:, :, j0 + n0 : j0 + n0 + BLK].rearrange("p t (c e) -> p c t e", e=2),
+                    (yb[:, :, j0 + n0 : j0 + n0 + BLK] if j0 + n0 else yb_first[:]).rearrange("p t (c e) -> p c t e", e=2),
                     MULT,
                 )
 
@@ -262,14 +266,15 @@ def tile_list_htabg_mul_noneP_kernel(
 
         quant_x(0)
         gather(3, J - WIDE, WIDE)
-        for c in range(1, len(CHUNKS)):
-            round_x(c)
-        wd = sb("wd", [P, N], U32, tag="xg")
+        round_x(1)
+        wd = sb("wd", [P, N], U32, tag="x_bf0")
         deal(nc.scalar.copy, wd[:], wd_raw.bitcast(U32))
-        make_h(0)
+        for c in range(2, len(CHUNKS)):
+            round_x(c)
         quant_x(1)
-        make_y(0)
+        make_h(0)
         quant_x(2)
+        make_y(0)
         for c in (1, 2):
             make_h(c)
             quant_x(c + 2)

@@ -15,16 +15,13 @@ U8 = mybir.dt.uint8
 FP8X4 = mybir.dt.float8_e4m3fn_x4
 FP4X4 = mybir.dt.float4_e2m1fn_x4
 MULT = mybir.AluOpType.mult
+ADD = mybir.AluOpType.add
 
 P = 128
-BLK = 128
-WIDE = 2 * BLK
+G = 128
 HALF = J // 2
 RING = 4
-CHUNKS = (WIDE, WIDE, WIDE, BLK, BLK)
-LAST = len(CHUNKS) - 1
-SCALAR_ROUNDS = {0: 0, 1: 1, LAST: 7}
-WB_SPLIT = (BLK // 4, BLK // 2)
+WB_SPLIT = (G // 4, G // 2)
 QUADRANTS = (0, 2, 1, 3)
 
 
@@ -32,22 +29,21 @@ def tile_list_htabg_mul_noneP_kernel(
     tc, tab_words, tab_scales, xT, wgt2, wa_words, wa_scales, wb, wd_words, wd_scales, offs, offs2, out_0, out_1, out_2
 ):
     nc = tc.nc
-    starts = [sum(CHUNKS[:c]) for c in range(len(CHUNKS))]
     with ExitStack() as ctx:
         keep = ctx.enter_context(tc.tile_pool(name="keep", bufs=1))
         psum = ctx.enter_context(tc.psum_pool(name="psum", bufs=1))
 
         def sb(name, shape, dtype, tag=None):
-            return keep.tile(shape, dtype, name=name, tag=tag or name, align_bytes=64)
+            return keep.tile(shape, dtype, name=name, tag=tag or name, align_bytes=256)
 
         def words(dram):
             return dram[0].rearrange("p n i -> p (n i)").bitcast(I32)
 
-        def weave_lines(copy, dst, src):
-            copy(dst.rearrange("p (c e) t -> p c t e", e=4), src.rearrange("p t (c e) -> p c t e", e=4))
+        def by(e, dst, src):
+            return dst.rearrange("p (c e) t -> p c t e", e=e), src.rearrange("p t (c e) -> p c t e", e=e)
 
-        def weave_pairs(copy, dst, src):
-            copy(dst.rearrange("p (c e) t -> p c t e", e=2), src.rearrange("p t (c e) -> p c t e", e=2))
+        def tokens(g0, g1):
+            return slice(G * g0, G * g1)
 
         def quant(bf, codes, sc):
             nc.vector.quantize_mx(out=codes.bitcast(FP8X4), scales=sc, in_=bf.rearrange("p n t -> p (n t)"))
@@ -58,29 +54,27 @@ def tile_list_htabg_mul_noneP_kernel(
         tabs = sb("tabs", [P, T], U8, tag="x0")
         wsc_raw = sb("wsc_raw", [P, R], U8)
         planes = sb("planes", [P, 2 * J], U8)
-
         for rows in (slice(32, 64), slice(64, P)):
             nc.vector.memset(tabs[rows, :].bitcast(I32), 0)
             nc.vector.memset(wsc_raw[rows, :].bitcast(I32), 0)
         nc.vector.memset(planes[:].bitcast(I32), 0)
-        wrows = sb("wrows", [P, BLK], F32)
+        wrows = sb("wrows", [P, G], F32)
         zero = sb("zero", [P, 1], F32)
         nc.vector.memset(zero[:], 0.0)
-        nc.scalar.copy(wrows[64:P, :], zero[64:P, :].to_broadcast([64, BLK]))
+        nc.scalar.copy(wrows[0:64, :], zero[0:64, :].to_broadcast([64, G]))
         ident = sb("ident", [P, P], F32)
         make_identity(nc, ident[:])
 
         nc.sync.dma_start(idx[:], offs)
         nc.sync.dma_start(tabs[0:32, :].bitcast(I32), tab_scales.rearrange("a s t -> s a t").bitcast(I32))
-        nc.sync.dma_start(wrows[0:64, :], wgt2[0:P:16, :].rearrange("g (c e) -> g c e", e=BLK))
+        nc.sync.dma_start(wrows[64:P, :], wgt2[0:P:16, :].rearrange("g (c e) -> g c e", e=G))
         nc.sync.dma_start(tabw[:], words(tab_words))
         nc.sync.dma_start(idx2[:], offs2)
         nc.sync.dma_start(wsc_raw[0:32:2, :].bitcast(I32), wa_scales[0].bitcast(I32))
         nc.sync.dma_start(wsc_raw[1:32:2, :].bitcast(I32), wd_scales[0].bitcast(I32))
         xplanes = xT.rearrange("(p i) t -> i p t", i=4)
         wb_raw, xw = [], []
-
-        def load_wb(a):
+        for a in range(2):
             wb_raw.append(sb(f"wb_raw{a}", [P, 4, R], F32, tag=("x2", "x3")[a]))
             nc.sync.dma_start(wb_raw[a][:], wb[512 * a : 512 * (a + 1), :].rearrange("(p i) r -> p i r", i=4))
 
@@ -88,25 +82,22 @@ def tile_list_htabg_mul_noneP_kernel(
             xw.append(sb(f"xw{i}", [P, T], F32, tag=f"x{i}"))
             nc.sync.dma_start(xw[i][:], xplanes[i])
 
-        load_wb(0)
-        load_wb(1)
-
-        turned = psum.tile([P, 4, BLK], F32, name="bank_a", bufs=RING)
+        turned = psum.tile([P, 4, G], F32, name="bank_a", bufs=RING)
         nc.tensor.transpose(turned[:, 0, :], wrows[:], ident[:])
-        pieces = turned[:, 0, 0:64].rearrange("e (g c) -> e c g", c=8)
+        pieces = turned[:, 0, 64:P].rearrange("e (g c) -> e c g", c=8)
         spread = [sb(f"spread{half}", [P, 4, 8, 16], F32, tag=("spread", "wb_bf0")[half]) for half in range(2)]
         for half in range(2):
             nc.scalar.copy(spread[half][:], pieces[:, 4 * half : 4 * half + 4].unsqueeze(3).to_broadcast([P, 4, 8, 16]))
         wgt = sb("wgt", [P, J], F32)
         for half in range(2):
-            back = psum.tile([P, 4, BLK], F32, name="bank_a", bufs=RING)
+            back = psum.tile([P, 4, G], F32, name="bank_a", bufs=RING)
             for c in range(4):
                 nc.tensor.transpose(back[:, c, :], spread[half][:, c].rearrange("e g s -> e (g s)"), ident[:])
             nc.scalar.copy(wgt[:, HALF * half : HALF * (half + 1)], back[:].rearrange("p c e -> p (c e)"))
 
-        def move_rows(queue, dst, src):
+        def move_rows(dst, src):
             for q in QUADRANTS:
-                queue.dma_start(
+                nc.sync.dma_start(
                     dst[32 * q : 32 * q + 4, :].bitcast(I32).rearrange("r (a j) -> r a j", a=2),
                     src[8 * q : 8 * q + 8, :].bitcast(I32),
                 )
@@ -115,7 +106,7 @@ def tile_list_htabg_mul_noneP_kernel(
         gw = sb("gw", [P, J], U32, tag="x1")
         nc.vector.tensor_copy(gs[:], tabs[:].indirect(idx[:]))
         load_x(0)
-        move_rows(nc.sync, planes, gs)
+        move_rows(planes, gs)
         nc.vector.tensor_copy(gw[:], tabw[:].bitcast(U32).indirect(idx[:]))
         parted = sb("parted", [P, 4 * J], U8)
         nc.vector.tensor_copy(
@@ -134,10 +125,10 @@ def tile_list_htabg_mul_noneP_kernel(
                 wb_raw[a][:, :, 4 * m0 : 4 * m1].rearrange("p i (m t) -> p m i t", t=4),
             )
 
-        round_wb(nc.scalar.copy, 0, WB_SPLIT[0], BLK)
+        round_wb(nc.scalar.copy, 0, WB_SPLIT[0], G)
         round_wb(nc.vector.tensor_copy, 0, 0, WB_SPLIT[0])
         quant(wb_bf[0][:], wb_codes[0][:], wb_sc[0][:])
-        round_wb(nc.scalar.copy, 1, WB_SPLIT[1], BLK)
+        round_wb(nc.scalar.copy, 1, WB_SPLIT[1], G)
         round_wb(nc.vector.tensor_copy, 1, 0, WB_SPLIT[1])
         wsc = sb("wsc", [P, R], U8, tag="wb_bf0")
         nc.vector.tensor_copy(wsc[:].rearrange("p (t m) -> p t m", t=4), wsc_raw[:].rearrange("p (m t) -> p t m", t=4))
@@ -145,149 +136,156 @@ def tile_list_htabg_mul_noneP_kernel(
         load_x(2)
         load_x(3)
 
-        yb_first, yb = sb("yb_first", [P, 4, BLK], F32), sb("yb", [P, 4, J], F32)
+        xg, yb = sb("xg", [P, 4, J], F32), sb("yb", [P, 4, J], F32)
         for half in range(2):
             for t in range(4):
                 bank = psum.tile([P, HALF], F32, name=("bank_a", "bank_y")[half], bufs=RING)
                 for a in range(2):
                     nc.tensor.matmul_mx(
                         out=bank[:],
-                        lhsT=wb_codes[a][:, BLK * t : BLK * (t + 1)].bitcast(FP8X4),
-                        lhsT_scale=wb_sc[a][:, BLK * t : BLK * (t + 1)],
+                        lhsT=wb_codes[a][:, G * t : G * (t + 1)].bitcast(FP8X4),
+                        lhsT_scale=wb_sc[a][:, G * t : G * (t + 1)],
                         rhs=parted[:, 2 * (J * a + HALF * half) : 2 * (J * a + HALF * (half + 1))].bitcast(FP4X4),
                         rhs_scale=planes[:, J * a + HALF * half : J * a + HALF * (half + 1)],
                         start=(a == 0),
                         stop=(a == 1),
                     )
-                if half == 0:
-                    nc.scalar.copy(yb_first[:, t, :], bank[:, 0:BLK])
-                    nc.scalar.copy(yb[:, t, BLK:HALF], bank[:, BLK:HALF])
-                else:
-                    nc.scalar.copy(yb[:, t, HALF:J], bank[:])
+                nc.scalar.copy(yb[:, t, HALF * half : HALF * (half + 1)], bank[:])
 
-        xg = sb("xg", [P, 4, J], F32)
-
-        def gather(i, j0, w):
-            nc.vector.tensor_tensor(
-                xg[:, i, j0 : j0 + w], xw[i][:].indirect(idx2[:, j0 // 16 : (j0 + w) // 16]), wgt[:, j0 : j0 + w], MULT
-            )
+        def gather(i, g0, g1):
+            nc.vector.tensor_tensor(xg[:, i, tokens(g0, g1)], xw[i][:].indirect(idx2[:, 8 * g0 : 8 * g1]), wgt[:, tokens(g0, g1)], MULT)
 
         for i in range(3):
-            gather(i, 0, J)
-        for j0, w in ((0, BLK), (BLK, BLK), (WIDE, WIDE), (HALF, WIDE)):
-            gather(3, j0, w)
+            gather(i, 0, 8)
 
         w_raw = sb("w_raw", [P, R + N], I32, tag="x1")
         wa_raw, wd_raw = w_raw[:, 0:R], w_raw[:, R : R + N]
         nc.sync.dma_start(wa_raw, words(wa_words))
         nc.sync.dma_start(wd_raw, words(wd_words))
-        move_rows(nc.sync, planes[:, 0 : R + N], wsc)
+        move_rows(planes[:, 0 : R + N], wsc)
         wa_sc, wd_sc = planes[:, 0:R], planes[:, R : R + N]
 
         def deal(copy, dealt, raw):
             copy(dealt.rearrange("p (t c e) -> p c t e", t=4, e=4), raw.rearrange("p (c e t) -> p c t e", t=4, e=4))
 
-        wa = sb("wa", [P, R], I32)
-        deal(nc.vector.tensor_copy, wa[:], wa_raw)
-
-        def project(name, w_codes, w_sc, codes, sc, n0):
-            bank = psum.tile([P, 4, BLK], F32, name=name, bufs=RING)
+        def project(name, w_codes, w_sc, codes, sc, g):
+            bank = psum.tile([P, 4, G], F32, name=name, bufs=RING)
             for t in range(4):
                 nc.tensor.matmul_mx(
                     out=bank[:, t, :],
-                    lhsT=w_codes[:, BLK * t : BLK * (t + 1)].bitcast(FP8X4),
-                    lhsT_scale=w_sc[:, BLK * t : BLK * (t + 1)],
-                    rhs=codes[:, n0 : n0 + BLK].bitcast(FP8X4),
-                    rhs_scale=sc[:, n0 : n0 + BLK],
+                    lhsT=w_codes[:, G * t : G * (t + 1)].bitcast(FP8X4),
+                    lhsT_scale=w_sc[:, G * t : G * (t + 1)],
+                    rhs=codes.bitcast(FP8X4),
+                    rhs_scale=sc[:, tokens(g, g + 1)],
                     start=True,
                     stop=True,
                 )
             return bank
 
-        xq, hq, ys, y_banks = {}, {}, {}, []
-        y_bf = sb("y_bf", [P, J, 4], BF16)
-        y_sc = sb("y_sc", [P, J], U8)
-        y_codes = sb("y_codes", [P, J], U32)
+        def on_gpsimd(dst, src):
+            nc.gpsimd.tensor_scalar(dst, src, 1.0, -0.0, MULT, ADD)
+
+        wa = sb("wa", [P, R], I32)
+        x_bf, h_bf, y_bf = (sb(f"{v}_bf", [P, J, 4], BF16) for v in "xhy")
+        h_codes, y_codes = (sb(f"{v}_codes", [P, J], U32) for v in "hy")
+        x_codes = {}
+        x_sc, h_sc, y_sc = (sb(f"{v}_sc", [P, J], U8) for v in "xhy")
+        y = [sb(f"y{s}", [P, 4, 2 * G], F32) for s in range(4)]
         out_rows = out_0.rearrange("(p t) j -> p t j", t=4)
-        out_words = words(out_1)
+        x_place = {6: y_bf[:, tokens(0, 1), :], 7: y_bf[:, tokens(2, 3), :]}
+        x_place[0] = sb("x_bf0", [P, G, 4], BF16)[:]
+        x_place[1] = xg[:, 3, tokens(6, 8)].bitcast(BF16).rearrange("p (n t) -> p n t", t=4)
+        y_banks = {}
 
-        x_bf = {}
+        def round_x(copy, g0, g1):
+            copy(*by(2, x_place.get(g0, x_bf[:, tokens(g0, g1), :]), xg[:, :, tokens(g0, g1)]))
 
-        def round_x(c):
-            x_bf[c] = sb(f"x_bf{c}", [P, CHUNKS[c], 4], BF16)
-            weave_pairs(nc.scalar.copy, x_bf[c][:], xg[:, :, starts[c] : starts[c] + CHUNKS[c]])
+        def quant_x(g0, g1):
+            codes = sb(f"x_codes{g0}", [P, G * (g1 - g0)], U32, tag="x_codes0" if g0 == 4 else None)
+            for g in range(g0, g1):
+                x_codes[g] = codes[:, tokens(g - g0, g - g0 + 1)]
+            quant(x_place.get(g0, x_bf[:, tokens(g0, g1), :]), codes[:], x_sc[:, tokens(g0, g1)])
 
-        def quant_x(c):
-            j0, w = starts[c], CHUNKS[c]
-            xq[c] = (sb(f"x_codes{c}", [P, w], U32, tag="yb_first" if c == 2 else None), sb(f"x_sc{c}", [P, w], U8))
-            if c == 0:
-                borrowed = xg[:, 3, J - WIDE : J].bitcast(BF16).rearrange("p (n t) -> p n t", t=4)
-                parts = ((0, BLK, sb("x_bf0", [P, BLK, 4], BF16)[:]), (BLK, WIDE, borrowed))
-                for n0, n1, part in parts:
-                    weave_pairs(nc.scalar.copy, part, xg[:, :, j0 + n0 : j0 + n1])
-                    quant(part, xq[c][0][:, n0:n1], xq[c][1][:, n0:n1])
-            else:
-                quant(x_bf[c][:], xq[c][0][:], xq[c][1][:])
+        def make_h(g):
+            bank = project("bank_a", wa, wa_sc, x_codes[g], x_sc, g)
+            dst, ya = by(2, h_bf[:, tokens(g, g + 1), :], bank[:])
+            nc.vector.tensor_tensor(dst, ya, yb[:, :, tokens(g, g + 1)].rearrange("p t (c e) -> p c t e", e=2), MULT)
 
-        def make_h(c):
-            j0, w = starts[c], CHUNKS[c]
-            hq[c] = sb(f"h_bf{c}", [P, w, 4], BF16, tag=f"x_bf{c + 1}" if c else None)
-            for n0 in range(0, w, BLK):
-                bank = project("bank_a", wa, wa_sc, *xq[c], n0)
-                nc.vector.tensor_tensor(
-                    hq[c][:, n0 : n0 + BLK, :].rearrange("p (c e) t -> p c t e", e=2),
-                    bank[:].rearrange("p t (c e) -> p c t e", e=2),
-                    (yb[:, :, j0 + n0 : j0 + n0 + BLK] if j0 + n0 else yb_first[:]).rearrange("p t (c e) -> p c t e", e=2),
-                    MULT,
-                )
+        def y_of(g):
+            return y[g // 2][:, :, tokens(g % 2, g % 2 + 1)]
 
-        def make_y(c):
-            j0, w = starts[c], CHUNKS[c]
-            h_codes, h_sc = sb(f"h_codes{c}", [P, w], U32), sb(f"h_sc{c}", [P, w], U8)
-            quant(hq[c][:], h_codes[:], h_sc[:])
-            s, s0 = divmod(j0, WIDE)
-            if s0 == 0:
-                ys[s] = sb(f"y{s}", [P, 4, WIDE], F32)
-            banks = [project("bank_y", wd, wd_sc, h_codes, h_sc, n0) for n0 in range(0, w, BLK)]
-            for b, bank in enumerate(banks):
-                nc.scalar.copy(ys[s][:, :, s0 + BLK * b : s0 + BLK * (b + 1)], bank[:])
-            if s0 + w == WIDE:
-                nc.sync.dma_start(out_rows[:, :, WIDE * s : WIDE * (s + 1)], ys[s][:])
-            y_banks.extend(banks)
-            if c in SCALAR_ROUNDS:
-                b = SCALAR_ROUNDS[c]
-                weave_pairs(nc.scalar.copy, y_bf[:, BLK * b : BLK * (b + 1), :], y_banks[b][:])
+        def quant_h(g0, g1):
+            quant(h_bf[:, tokens(g0, g1), :], h_codes[:, tokens(g0, g1)], h_sc[:, tokens(g0, g1)])
+            for g in range(g0, g1):
+                y_banks[g] = project("bank_y", wd, wd_sc, h_codes[:, tokens(g, g + 1)], h_sc, g)
 
-        def planes_y(j0, j1):
-            quant(y_bf[:, j0:j1, :], y_codes[:, j0:j1], y_sc[:, j0:j1])
+        def copy_y(g):
+            nc.scalar.copy(y_of(g), y_banks[g][:])
+            if g % 2:
+                nc.sync.dma_start(out_rows[:, :, tokens(g - 1, g + 1)], y[g // 2][:])
 
-        def store_words(j0, j1):
-            nc.sync.dma_start(out_words[:, j0:j1], y_codes[:, j0:j1].bitcast(I32))
+        def round_y(copy, g, e, src):
+            copy(*by(e, y_bf[:, tokens(g, g + 1), :], src))
 
-        quant_x(0)
-        gather(3, J - WIDE, WIDE)
-        round_x(1)
+        def store_words(g0, g1):
+            nc.sync.dma_start(words(out_1)[:, tokens(g0, g1)], y_codes[:, tokens(g0, g1)].bitcast(I32))
+
+        def quant_y(g0, g1):
+            quant(y_bf[:, tokens(g0, g1), :], y_codes[:, tokens(g0, g1)], y_sc[:, tokens(g0, g1)])
+
+        gather(3, 0, 1)
+        gather(3, 1, 2)
+        gather(3, 2, 4)
+        gather(3, 4, 6)
+        deal(nc.vector.tensor_copy, wa[:], wa_raw)
+        for g in range(2):
+            round_x(nc.scalar.copy, g, g + 1)
+            quant_x(g, g + 1)
+        gather(3, 6, 8)
+        round_x(nc.scalar.copy, 2, 4)
         wd = sb("wd", [P, N], U32, tag="x_bf0")
         deal(nc.scalar.copy, wd[:], wd_raw.bitcast(U32))
-        for c in range(2, len(CHUNKS)):
-            round_x(c)
-        quant_x(1)
+        round_x(nc.scalar.copy, 4, 6)
+        round_x(nc.scalar.copy, 6, 7)
+        round_x(nc.scalar.copy, 7, 8)
+        quant_x(2, 4)
         make_h(0)
-        quant_x(2)
-        make_y(0)
-        for c in (1, 2):
-            make_h(c)
-            quant_x(c + 2)
-            make_y(c)
-        make_h(LAST - 1)
-        make_h(LAST)
-        make_y(LAST - 1)
-        planes_y(0, WIDE)
-        make_y(LAST)
-        for c in range(1, LAST):
-            weave_lines(nc.vector.tensor_copy, y_bf[:, starts[c] : starts[c + 1], :], ys[c][:, :, 0 : CHUNKS[c]])
-        planes_y(WIDE, starts[LAST - 1])
-        planes_y(starts[LAST - 1], J)
-        store_words(0, J)
+        make_h(1)
+        quant_x(4, 6)
+        quant_h(0, 2)
+        copy_y(0)
+        copy_y(1)
+        round_y(nc.scalar.copy, 1, 2, y_banks[1][:])
+        make_h(2)
+        make_h(3)
+        quant_x(6, 7)
+        quant_h(2, 4)
+        round_y(on_gpsimd, 0, 2, y_of(0))
+        copy_y(2)
+        copy_y(3)
+        make_h(4)
+        make_h(5)
+        quant_x(7, 8)
+        quant_h(4, 6)
+        round_y(on_gpsimd, 2, 2, y_of(2))
+        copy_y(4)
+        copy_y(5)
+        make_h(6)
+        make_h(7)
+        quant_h(6, 7)
+        quant_y(0, 2)
+        store_words(0, 2)
+        quant_h(7, 8)
+        copy_y(6)
+        copy_y(7)
+        round_y(nc.scalar.copy, 7, 2, y_banks[7][:])
+        round_y(nc.vector.tensor_copy, 3, 4, y_of(3))
+        nc.vector.tensor_copy(*by(4, y_bf[:, tokens(4, 6), :], y[2][:]))
+        quant_y(2, 4)
+        round_y(nc.vector.tensor_copy, 6, 4, y_of(6))
+        quant_y(4, 6)
+        store_words(2, 6)
+        quant_y(6, 8)
+        store_words(6, 8)
         for q in QUADRANTS:
             (nc.scalar, nc.sync)[q % 2].dma_start(out_2[0, 4 * q : 4 * q + 4, :].bitcast(I32), y_sc[32 * q : 32 * q + 4, :].bitcast(I32))

@@ -278,7 +278,7 @@ def tile_list_htabg_mul_noneP_kernel(
         quant_h(7, 8)
         copy_y(6)
         copy_y(7)
-        round_y(nc.scalar.copy, 7, 2, y_banks[7][:])
+        on_gpsimd(y_bf[:, tokens(7, 8), :], y_of(7).rearrange("p t j -> p j t"))
         round_y(nc.vector.tensor_copy, 3, 4, y_of(3))
         nc.vector.tensor_copy(*by(4, y_bf[:, tokens(4, 6), :], y[2][:]))
         quant_y(2, 4)

@@ -183,41 +183,44 @@ def tile_list_htabg_mul_noneP_kernel(
             return bank
 
         def on_gpsimd(dst, src):
-            nc.gpsimd.tensor_scalar(dst, src, 1.0, -0.0, MULT, ADD)
+            nc.gpsimd.tensor_scalar(dst, src.rearrange("p t j -> p j t"), 1.0, -0.0, MULT, ADD)
 
         wa = sb("wa", [P, R], I32)
-        x_bf, h_bf, y_bf = (sb(f"{v}_bf", [P, J, 4], BF16) for v in "xhy")
-        h_codes, y_codes = (sb(f"{v}_codes", [P, J], U32) for v in "hy")
-        x_codes = {}
+        y_bf = sb("y_bf", [P, J, 4], BF16)
+        x_codes, y_banks = {}, {}
         x_sc, h_sc, y_sc = (sb(f"{v}_sc", [P, J], U8) for v in "xhy")
         y = [sb(f"y{s}", [P, 4, 2 * G], F32) for s in range(4)]
         out_rows = out_0.rearrange("(p t) j -> p t j", t=4)
-        x_place = {6: y_bf[:, tokens(0, 1), :], 7: y_bf[:, tokens(2, 3), :]}
-        x_place[0] = sb("x_bf0", [P, G, 4], BF16)[:]
+        x_place = {g0: sb(f"x_bf{g0}", [P, G * n, 4], BF16)[:] for g0, n in ((0, 1), (2, 2), (4, 2))}
         x_place[1] = xg[:, 3, tokens(6, 8)].bitcast(BF16).rearrange("p (n t) -> p n t", t=4)
-        y_banks = {}
+        x_place[6] = y_bf[:, tokens(0, 2), :]
+        h_bf = sb("h_bf", [P, J, 4], BF16)
+        h_codes = sb("h_codes", [P, J], U32)
 
-        def round_x(copy, g0, g1):
-            copy(*by(2, x_place.get(g0, x_bf[:, tokens(g0, g1), :]), xg[:, :, tokens(g0, g1)]))
+        def h_place(g0, g1):
+            return y_bf[:, tokens(g0 - 2, g1 - 2), :] if g0 in (4, 5) else h_bf[:, tokens(g0, g1), :]
+
+        def round_x(g0, g1):
+            nc.scalar.copy(*by(2, x_place[g0], xg[:, :, tokens(g0, g1)]))
 
         def quant_x(g0, g1):
-            codes = sb(f"x_codes{g0}", [P, G * (g1 - g0)], U32, tag="x_codes0" if g0 == 4 else None)
+            codes = sb(f"x_codes{g0}", [P, G * (g1 - g0)], U32, tag={4: "x_codes0", 6: "x_codes2"}.get(g0))
             for g in range(g0, g1):
                 x_codes[g] = codes[:, tokens(g - g0, g - g0 + 1)]
-            quant(x_place.get(g0, x_bf[:, tokens(g0, g1), :]), codes[:], x_sc[:, tokens(g0, g1)])
+            quant(x_place[g0], codes[:], x_sc[:, tokens(g0, g1)])
 
-        def make_h(g):
-            bank = project("bank_a", wa, wa_sc, x_codes[g], x_sc, g)
-            dst, ya = by(2, h_bf[:, tokens(g, g + 1), :], bank[:])
-            nc.vector.tensor_tensor(dst, ya, yb[:, :, tokens(g, g + 1)].rearrange("p t (c e) -> p c t e", e=2), MULT)
+        def pair_of_h(g0):
+            for g in (g0, g0 + 1):
+                dst, ya = by(2, h_place(g, g + 1), project("bank_a", wa, wa_sc, x_codes[g], x_sc, g)[:])
+                nc.vector.tensor_tensor(dst, ya, yb[:, :, tokens(g, g + 1)].rearrange("p t (c e) -> p c t e", e=2), MULT)
+
+        def quant_h(g0, g1):
+            quant(h_place(g0, g1), h_codes[:, tokens(g0, g1)], h_sc[:, tokens(g0, g1)])
+            for g in range(g0, g1):
+                y_banks[g] = project("bank_y", wd, wd_sc, h_codes[:, tokens(g, g + 1)], h_sc, g)
 
         def y_of(g):
             return y[g // 2][:, :, tokens(g % 2, g % 2 + 1)]
-
-        def quant_h(g0, g1):
-            quant(h_bf[:, tokens(g0, g1), :], h_codes[:, tokens(g0, g1)], h_sc[:, tokens(g0, g1)])
-            for g in range(g0, g1):
-                y_banks[g] = project("bank_y", wd, wd_sc, h_codes[:, tokens(g, g + 1)], h_sc, g)
 
         def copy_y(g):
             nc.scalar.copy(y_of(g), y_banks[g][:])
@@ -227,65 +230,52 @@ def tile_list_htabg_mul_noneP_kernel(
         def round_y(copy, g, e, src):
             copy(*by(e, y_bf[:, tokens(g, g + 1), :], src))
 
-        def store_words(g0, g1):
-            nc.sync.dma_start(words(out_1)[:, tokens(g0, g1)], y_codes[:, tokens(g0, g1)].bitcast(I32))
+        def planes_y(g0, g1):
+            codes = sb(f"y_codes{g0}", [P, G * (g1 - g0)], U32)
+            quant(y_bf[:, tokens(g0, g1), :], codes[:], y_sc[:, tokens(g0, g1)])
+            nc.sync.dma_start(words(out_1)[:, tokens(g0, g1)], codes[:].bitcast(I32))
 
-        def quant_y(g0, g1):
-            quant(y_bf[:, tokens(g0, g1), :], y_codes[:, tokens(g0, g1)], y_sc[:, tokens(g0, g1)])
-
-        gather(3, 0, 1)
-        gather(3, 1, 2)
-        gather(3, 2, 4)
-        gather(3, 4, 6)
+        for g0, g1 in ((0, 1), (1, 2), (2, 4), (4, 6)):
+            gather(3, g0, g1)
         deal(nc.vector.tensor_copy, wa[:], wa_raw)
         for g in range(2):
-            round_x(nc.scalar.copy, g, g + 1)
+            round_x(g, g + 1)
             quant_x(g, g + 1)
         gather(3, 6, 8)
-        round_x(nc.scalar.copy, 2, 4)
+        round_x(2, 4)
         wd = sb("wd", [P, N], U32, tag="x_bf0")
         deal(nc.scalar.copy, wd[:], wd_raw.bitcast(U32))
-        round_x(nc.scalar.copy, 4, 6)
-        round_x(nc.scalar.copy, 6, 7)
-        round_x(nc.scalar.copy, 7, 8)
+        round_x(4, 6)
+        round_x(6, 8)
         quant_x(2, 4)
-        make_h(0)
-        make_h(1)
+        pair_of_h(0)
         quant_x(4, 6)
         quant_h(0, 2)
         copy_y(0)
         copy_y(1)
-        round_y(nc.scalar.copy, 1, 2, y_banks[1][:])
-        make_h(2)
-        make_h(3)
-        quant_x(6, 7)
+        pair_of_h(2)
+        quant_x(6, 8)
         quant_h(2, 4)
-        round_y(on_gpsimd, 0, 2, y_of(0))
+        on_gpsimd(y_bf[:, tokens(0, 1), :], y_of(0))
         copy_y(2)
         copy_y(3)
-        make_h(4)
-        make_h(5)
-        quant_x(7, 8)
+        pair_of_h(4)
+        round_y(nc.vector.tensor_copy, 1, 4, y_of(1))
         quant_h(4, 6)
-        round_y(on_gpsimd, 2, 2, y_of(2))
+        on_gpsimd(y_bf[:, tokens(2, 3), :], y_of(2))
+        round_y(nc.scalar.copy, 3, 2, y_banks[3][:])
         copy_y(4)
         copy_y(5)
-        make_h(6)
-        make_h(7)
+        pair_of_h(6)
         quant_h(6, 7)
-        quant_y(0, 2)
-        store_words(0, 2)
+        planes_y(0, 2)
         quant_h(7, 8)
         copy_y(6)
         copy_y(7)
-        on_gpsimd(y_bf[:, tokens(7, 8), :], y_of(7).rearrange("p t j -> p j t"))
-        round_y(nc.vector.tensor_copy, 3, 4, y_of(3))
+        round_y(nc.scalar.copy, 7, 2, y_banks[7][:])
         nc.vector.tensor_copy(*by(4, y_bf[:, tokens(4, 6), :], y[2][:]))
-        quant_y(2, 4)
         round_y(nc.vector.tensor_copy, 6, 4, y_of(6))
-        quant_y(4, 6)
-        store_words(2, 6)
-        quant_y(6, 8)
-        store_words(6, 8)
+        planes_y(2, 6)
+        planes_y(6, 8)
         for q in QUADRANTS:
             (nc.scalar, nc.sync)[q % 2].dma_start(out_2[0, 4 * q : 4 * q + 4, :].bitcast(I32), y_sc[32 * q : 32 * q + 4, :].bitcast(I32))

from contextlib import ExitStack

import concourse.mybir as mybir
from concourse.masks import make_identity

K, L, R, N, T, J = 512, 1024, 512, 512, 2048, 1024
FLOPS = 2 * J * (K * R + L * R + R * N)

F32 = mybir.dt.float32
BF16 = mybir.dt.bfloat16
I32 = mybir.dt.int32
U32 = mybir.dt.uint32
U16 = mybir.dt.uint16
U8 = mybir.dt.uint8
FP8X4 = mybir.dt.float8_e4m3fn_x4
FP4X4 = mybir.dt.float4_e2m1fn_x4
MULT = mybir.AluOpType.mult
ADD = mybir.AluOpType.add

P = 128
G = 128
HALF = J // 2
RING = 4
WB_SPLIT = (G // 4, G // 2)
QUADRANTS = (0, 2, 1, 3)


def tile_list_htabg_mul_noneP_kernel(
    tc, tab_words, tab_scales, xT, wgt2, wa_words, wa_scales, wb, wd_words, wd_scales, offs, offs2, out_0, out_1, out_2
):
    nc = tc.nc
    with ExitStack() as ctx:
        keep = ctx.enter_context(tc.tile_pool(name="keep", bufs=1))
        psum = ctx.enter_context(tc.psum_pool(name="psum", bufs=1))

        def sb(name, shape, dtype, tag=None):
            return keep.tile(shape, dtype, name=name, tag=tag or name, align_bytes=256)

        def words(dram):
            return dram[0].rearrange("p n i -> p (n i)").bitcast(I32)

        def by(e, dst, src):
            return dst.rearrange("p (c e) t -> p c t e", e=e), src.rearrange("p t (c e) -> p c t e", e=e)

        def tokens(g0, g1):
            return slice(G * g0, G * g1)

        def quant(bf, codes, sc):
            nc.vector.quantize_mx(out=codes.bitcast(FP8X4), scales=sc, in_=bf.rearrange("p n t -> p (n t)"))

        idx = keep.tile([P, J // 16], U16, name="idx")
        idx2 = keep.tile([P, J // 16], U16, name="idx2")
        tabw = sb("tabw", [P, T], I32)
        tabs = sb("tabs", [P, T], U8, tag="x0")
        wsc_raw = sb("wsc_raw", [P, R], U8)
        planes = sb("planes", [P, 2 * J], U8)
        for rows in (slice(32, 64), slice(64, P)):
            nc.vector.memset(tabs[rows, :].bitcast(I32), 0)
            nc.vector.memset(wsc_raw[rows, :].bitcast(I32), 0)
        nc.vector.memset(planes[:].bitcast(I32), 0)
        wrows = sb("wrows", [P, G], F32)
        zero = sb("zero", [P, 1], F32)
        nc.vector.memset(zero[:], 0.0)
        nc.scalar.copy(wrows[0:64, :], zero[0:64, :].to_broadcast([64, G]))
        ident = sb("ident", [P, P], F32)
        make_identity(nc, ident[:])

        nc.sync.dma_start(idx[:], offs)
        nc.sync.dma_start(tabs[0:32, :].bitcast(I32), tab_scales.rearrange("a s t -> s a t").bitcast(I32))
        nc.sync.dma_start(wrows[64:P, :], wgt2[0:P:16, :].rearrange("g (c e) -> g c e", e=G))
        nc.sync.dma_start(tabw[:], words(tab_words))
        nc.sync.dma_start(idx2[:], offs2)
        nc.sync.dma_start(wsc_raw[0:32:2, :].bitcast(I32), wa_scales[0].bitcast(I32))
        nc.sync.dma_start(wsc_raw[1:32:2, :].bitcast(I32), wd_scales[0].bitcast(I32))
        xplanes = xT.rearrange("(p i) t -> i p t", i=4)
        wb_raw, xw = [], []
        for a in range(2):
            wb_raw.append(sb(f"wb_raw{a}", [P, 4, R], F32, tag=("x2", "x3")[a]))
            nc.sync.dma_start(wb_raw[a][:], wb[512 * a : 512 * (a + 1), :].rearrange("(p i) r -> p i r", i=4))

        def load_x(i):
            xw.append(sb(f"xw{i}", [P, T], F32, tag=f"x{i}"))
            nc.sync.dma_start(xw[i][:], xplanes[i])

        turned = psum.tile([P, 4, G], F32, name="bank_a", bufs=RING)
        nc.tensor.transpose(turned[:, 0, :], wrows[:], ident[:])
        pieces = turned[:, 0, 64:P].rearrange("e (g c) -> e c g", c=8)
        spread = [sb(f"spread{half}", [P, 4, 8, 16], F32, tag=("spread", "wb_bf0")[half]) for half in range(2)]
        for half in range(2):
            nc.scalar.copy(spread[half][:], pieces[:, 4 * half : 4 * half + 4].unsqueeze(3).to_broadcast([P, 4, 8, 16]))
        wgt = sb("wgt", [P, J], F32)
        for half in range(2):
            back = psum.tile([P, 4, G], F32, name="bank_a", bufs=RING)
            for c in range(4):
                nc.tensor.transpose(back[:, c, :], spread[half][:, c].rearrange("e g s -> e (g s)"), ident[:])
            nc.scalar.copy(wgt[:, HALF * half : HALF * (half + 1)], back[:].rearrange("p c e -> p (c e)"))

        def move_rows(dst, src):
            for q in QUADRANTS:
                nc.sync.dma_start(
                    dst[32 * q : 32 * q + 4, :].bitcast(I32).rearrange("r (a j) -> r a j", a=2),
                    src[8 * q : 8 * q + 8, :].bitcast(I32),
                )

        gs = sb("gs", [P, J], U8)
        gw = sb("gw", [P, J], U32, tag="x1")
        nc.vector.tensor_copy(gs[:], tabs[:].indirect(idx[:]))
        load_x(0)
        move_rows(planes, gs)
        nc.vector.tensor_copy(gw[:], tabw[:].bitcast(U32).indirect(idx[:]))
        parted = sb("parted", [P, 4 * J], U8)
        nc.vector.tensor_copy(
            parted[:].bitcast(U16).rearrange("p (d j) -> p d j", d=2),
            gw[:].bitcast(U16).rearrange("p (j d) -> p d j", d=2),
        )
        load_x(1)

        wb_bf = [sb(f"wb_bf{a}", [P, R, 4], BF16) for a in range(2)]
        wb_codes = [sb(f"wb_codes{a}", [P, R], U32) for a in range(2)]
        wb_sc = [sb(f"wb_sc{a}", [P, R], U8) for a in range(2)]

        def round_wb(copy, a, m0, m1):
            copy(
                wb_bf[a][:].rearrange("p (t m) i -> p m i t", t=4)[:, m0:m1],
                wb_raw[a][:, :, 4 * m0 : 4 * m1].rearrange("p i (m t) -> p m i t", t=4),
            )

        round_wb(nc.scalar.copy, 0, WB_SPLIT[0], G)
        round_wb(nc.vector.tensor_copy, 0, 0, WB_SPLIT[0])
        quant(wb_bf[0][:], wb_codes[0][:], wb_sc[0][:])
        round_wb(nc.scalar.copy, 1, WB_SPLIT[1], G)
        round_wb(nc.vector.tensor_copy, 1, 0, WB_SPLIT[1])
        wsc = sb("wsc", [P, R], U8, tag="wb_bf0")
        nc.vector.tensor_copy(wsc[:].rearrange("p (t m) -> p t m", t=4), wsc_raw[:].rearrange("p (m t) -> p t m", t=4))
        quant(wb_bf[1][:], wb_codes[1][:], wb_sc[1][:])
        load_x(2)
        load_x(3)

        xg, yb = sb("xg", [P, 4, J], F32), sb("yb", [P, 4, J], F32)
        for half in range(2):
            for t in range(4):
                bank = psum.tile([P, HALF], F32, name=("bank_a", "bank_y")[half], bufs=RING)
                for a in range(2):
                    nc.tensor.matmul_mx(
                        out=bank[:],
                        lhsT=wb_codes[a][:, G * t : G * (t + 1)].bitcast(FP8X4),
                        lhsT_scale=wb_sc[a][:, G * t : G * (t + 1)],
                        rhs=parted[:, 2 * (J * a + HALF * half) : 2 * (J * a + HALF * (half + 1))].bitcast(FP4X4),
                        rhs_scale=planes[:, J * a + HALF * half : J * a + HALF * (half + 1)],
                        start=(a == 0),
                        stop=(a == 1),
                    )
                nc.scalar.copy(yb[:, t, HALF * half : HALF * (half + 1)], bank[:])

        def gather(i, g0, g1):
            nc.vector.tensor_tensor(xg[:, i, tokens(g0, g1)], xw[i][:].indirect(idx2[:, 8 * g0 : 8 * g1]), wgt[:, tokens(g0, g1)], MULT)

        for i in range(3):
            gather(i, 0, 8)

        w_raw = sb("w_raw", [P, R + N], I32, tag="x1")
        wa_raw, wd_raw = w_raw[:, 0:R], w_raw[:, R : R + N]
        nc.sync.dma_start(wa_raw, words(wa_words))
        nc.sync.dma_start(wd_raw, words(wd_words))
        move_rows(planes[:, 0 : R + N], wsc)
        wa_sc, wd_sc = planes[:, 0:R], planes[:, R : R + N]

        def deal(copy, dealt, raw):
            copy(dealt.rearrange("p (t c e) -> p c t e", t=4, e=4), raw.rearrange("p (c e t) -> p c t e", t=4, e=4))

        def project(name, w_codes, w_sc, codes, sc, g):
            bank = psum.tile([P, 4, G], F32, name=name, bufs=RING)
            for t in range(4):
                nc.tensor.matmul_mx(
                    out=bank[:, t, :],
                    lhsT=w_codes[:, G * t : G * (t + 1)].bitcast(FP8X4),
                    lhsT_scale=w_sc[:, G * t : G * (t + 1)],
                    rhs=codes.bitcast(FP8X4),
                    rhs_scale=sc[:, tokens(g, g + 1)],
                    start=True,
                    stop=True,
                )
            return bank

        def on_gpsimd(dst, src):
            nc.gpsimd.tensor_scalar(dst, src.rearrange("p t j -> p j t"), 1.0, -0.0, MULT, ADD)

        wa = sb("wa", [P, R], I32)
        y_bf = sb("y_bf", [P, J, 4], BF16)
        x_codes, y_banks = {}, {}
        x_sc, h_sc, y_sc = (sb(f"{v}_sc", [P, J], U8) for v in "xhy")
        y = [sb(f"y{s}", [P, 4, 2 * G], F32) for s in range(4)]
        out_rows = out_0.rearrange("(p t) j -> p t j", t=4)
        x_place = {g0: sb(f"x_bf{g0}", [P, G * n, 4], BF16)[:] for g0, n in ((0, 1), (2, 2), (4, 2))}
        x_place[1] = xg[:, 3, tokens(6, 8)].bitcast(BF16).rearrange("p (n t) -> p n t", t=4)
        x_place[6] = y_bf[:, tokens(0, 2), :]
        h_bf = sb("h_bf", [P, J, 4], BF16)
        h_codes = sb("h_codes", [P, J], U32)

        def h_place(g0, g1):
            return y_bf[:, tokens(g0 - 2, g1 - 2), :] if g0 in (4, 5) else h_bf[:, tokens(g0, g1), :]

        def round_x(g0, g1):
            nc.scalar.copy(*by(2, x_place[g0], xg[:, :, tokens(g0, g1)]))

        def quant_x(g0, g1):
            codes = sb(f"x_codes{g0}", [P, G * (g1 - g0)], U32, tag={4: "x_codes0", 6: "x_codes2"}.get(g0))
            for g in range(g0, g1):
                x_codes[g] = codes[:, tokens(g - g0, g - g0 + 1)]
            quant(x_place[g0], codes[:], x_sc[:, tokens(g0, g1)])

        def pair_of_h(g0):
            for g in (g0, g0 + 1):
                dst, ya = by(2, h_place(g, g + 1), project("bank_a", wa, wa_sc, x_codes[g], x_sc, g)[:])
                nc.vector.tensor_tensor(dst, ya, yb[:, :, tokens(g, g + 1)].rearrange("p t (c e) -> p c t e", e=2), MULT)

        def quant_h(g0, g1):
            quant(h_place(g0, g1), h_codes[:, tokens(g0, g1)], h_sc[:, tokens(g0, g1)])
            for g in range(g0, g1):
                y_banks[g] = project("bank_y", wd, wd_sc, h_codes[:, tokens(g, g + 1)], h_sc, g)

        def y_of(g):
            return y[g // 2][:, :, tokens(g % 2, g % 2 + 1)]

        def copy_y(g):
            nc.scalar.copy(y_of(g), y_banks[g][:])
            if g % 2:
                nc.sync.dma_start(out_rows[:, :, tokens(g - 1, g + 1)], y[g // 2][:])

        def round_y(copy, g, e, src):
            copy(*by(e, y_bf[:, tokens(g, g + 1), :], src))

        def planes_y(g0, g1):
            codes = sb(f"y_codes{g0}", [P, G * (g1 - g0)], U32)
            quant(y_bf[:, tokens(g0, g1), :], codes[:], y_sc[:, tokens(g0, g1)])
            nc.sync.dma_start(words(out_1)[:, tokens(g0, g1)], codes[:].bitcast(I32))

        for g0, g1 in ((0, 1), (1, 2), (2, 4), (4, 6)):
            gather(3, g0, g1)
        deal(nc.vector.tensor_copy, wa[:], wa_raw)
        for g in range(2):
            round_x(g, g + 1)
            quant_x(g, g + 1)
        gather(3, 6, 8)
        round_x(2, 4)
        wd = sb("wd", [P, N], U32, tag="x_bf0")
        deal(nc.scalar.copy, wd[:], wd_raw.bitcast(U32))
        round_x(4, 6)
        round_x(6, 8)
        quant_x(2, 4)
        pair_of_h(0)
        quant_x(4, 6)
        quant_h(0, 2)
        copy_y(0)
        copy_y(1)
        pair_of_h(2)
        quant_x(6, 8)
        quant_h(2, 4)
        on_gpsimd(y_bf[:, tokens(0, 1), :], y_of(0))
        copy_y(2)
        copy_y(3)
        pair_of_h(4)
        round_y(nc.vector.tensor_copy, 1, 4, y_of(1))
        quant_h(4, 6)
        on_gpsimd(y_bf[:, tokens(2, 3), :], y_of(2))
        round_y(nc.scalar.copy, 3, 2, y_banks[3][:])
        copy_y(4)
        copy_y(5)
        pair_of_h(6)
        quant_h(6, 7)
        planes_y(0, 2)
        quant_h(7, 8)
        copy_y(6)
        copy_y(7)
        round_y(nc.scalar.copy, 7, 2, y_banks[7][:])
        nc.vector.tensor_copy(*by(4, y_bf[:, tokens(4, 6), :], y[2][:]))
        round_y(nc.vector.tensor_copy, 6, 4, y_of(6))
        planes_y(2, 6)
        planes_y(6, 8)
        for q in QUADRANTS:
            (nc.scalar, nc.sync)[q % 2].dma_start(out_2[0, 4 * q : 4 * q + 4, :].bitcast(I32), y_sc[32 * q : 32 * q + 4, :].bitcast(I32))
